import numpy as np
import ml_dtypes


def mxq(x, axis, fmt="e4m3"):
    dtype, down = {"e4m3": (ml_dtypes.float8_e4m3fn, 7), "e5m2": (ml_dtypes.float8_e5m2, 14)}[fmt]
    v = np.moveaxis(np.asarray(x, np.float32).astype(ml_dtypes.bfloat16).astype(np.float64), axis, -1)
    blocks = v.reshape(v.shape[:-1] + (-1, 32))
    amax = np.abs(blocks).max(-1, keepdims=True)
    byte = np.maximum(np.where(amax > 0, np.frexp(amax)[1] - 1 + 127, 0) - down, 1)
    scale = np.exp2(byte - 127.0)
    codes = (blocks / scale).astype(np.float32).astype(dtype).astype(np.float64)
    return np.moveaxis((codes * scale).reshape(v.shape), -1, axis)


WIDE = False


def mx_kscale(k):
    if not WIDE:
        return np.ones(k)
    levels = np.array([24, -24, 12, -12, 0])
    if k % 512:
        return np.exp2(np.random.permutation(np.resize(levels, k // 32))).repeat(32)
    a = np.empty((k // 512, 16))
    for p in range(k // 512):
        a[p, :8] = np.random.permutation(np.resize(levels, 8))
        for g in range(8):
            far = levels[np.abs(levels - a[p, g]) >= 10]
            a[p, g + 8] = far[np.random.randint(len(far))]
    return np.exp2(a.ravel()).repeat(32)


def f64(x):
    return np.asarray(x).astype(np.float64)


def striped(idx):
    return np.tile(idx.reshape(-1, 16).T, (8, 1)).astype(np.uint16)


def unstriped(offs):
    return offs[:16].T.reshape(-1).astype(np.int64)


E2M1 = np.array([0.0, 0.5, 1.0, 1.5, 2.0, 3.0, 4.0, 6.0, -0.0, -0.5, -1.0, -1.5, -2.0, -3.0, -4.0, -6.0])


def pack_weight(w, fmt):
    k, n = w.shape
    w = f64(np.asarray(w, np.float32).astype(ml_dtypes.bfloat16)).reshape(k // 32, 32, n)
    amax = np.abs(w).max(1)
    if fmt == "e4m3":
        byte = np.frexp(amax)[1] - 1 + 127 - 7
    else:
        mant, ex = np.frexp(amax / 6.0)
        byte = np.where(mant > 0.5, ex, ex - 1) + 127
    byte = np.clip(np.where(amax > 0, byte, 1), 1, 254)
    scaled = (w * np.exp2(127.0 - byte)[:, None, :]).reshape(k, n).astype(np.float32)
    by_word = np.ascontiguousarray(scaled.reshape(k // 512, 128, 4, n).transpose(0, 1, 3, 2))
    if fmt == "e4m3":
        words = by_word.astype(ml_dtypes.float8_e4m3fn).view(np.uint8)
    else:
        c = by_word.astype(ml_dtypes.float4_e2m1fn).view(np.uint8) & 0xF
        words = (c[..., 0::2] | (c[..., 1::2] << 4)).reshape(k // 512, 128, 2 * n)
    return np.ascontiguousarray(words), np.ascontiguousarray(byte.astype(np.uint8).reshape(k // 512, 16, n))


def unpack_weight(words, scales, fmt):
    g, _, n = scales.shape
    words = np.ascontiguousarray(words).reshape(g, 128, n, -1)
    if fmt == "e4m3":
        vals = words.view(ml_dtypes.float8_e4m3fn).astype(np.float64)
    else:
        nib = np.empty((g, 128, n, 4), np.uint8)
        nib[..., 0::2] = words & 0xF
        nib[..., 1::2] = words >> 4
        vals = E2M1[nib]
    vals = vals * np.repeat(np.exp2(scales.astype(np.float64) - 127.0), 8, axis=1)[..., None]
    return vals.transpose(0, 1, 3, 2).reshape(g * 512, n)


def pack_table4(v):
    words, scales = pack_weight(v, "e2m1")
    g, t = words.shape[0] // 2, v.shape[1]
    return np.ascontiguousarray(words.reshape(g, 2, 128, t, 2).transpose(0, 2, 3, 1, 4).reshape(g, 128, t, 4)), scales


def unpack_table4(words, scales):
    g, _, t, _ = words.shape
    return unpack_weight(words.reshape(g, 128, t, 2, 2).transpose(0, 3, 1, 2, 4).reshape(2 * g, 128, 2 * t), scales, "e2m1")


def sigm(f):
    return 1.0 / (1.0 + np.exp(-np.maximum(f, -700.0)))


K, M, N, J, T = 1024, 1024, 256, 1024, 2048


def setup_inputs():
    n = np.random.standard_normal
    s = mx_kscale(K)[:, None]
    u = mx_kscale(J)[:, None]
    al = n((J, N)) / np.sqrt(J) / u
    al4 = pack_weight(al, "e2m1")
    alrest = al - unpack_weight(*al4, "e2m1")
    p_tab = pack_table4(0.5 * n((K, T)) / np.sqrt(K) / s)
    p_al8 = pack_weight(alrest, "e4m3")
    return {
        "x": (n((K, M)) * s).astype(np.float32),
        "tab_words": p_tab[0],
        "tab_scales": p_tab[1],
        "cw": (np.random.uniform(0.5, 2.0, J) * u[:, 0]).astype(np.float32),
        "cb": (0.3 * n(J)).astype(np.float32),
        "al4_words": al4[0],
        "al4_scales": al4[1],
        "al8_words": p_al8[0],
        "al8_scales": p_al8[1],
        "b": (0.3 * n(N)).astype(np.float32),
        "offs": striped(np.random.permutation(T)[:J]),
    }


def reference(x, tab_words, tab_scales, cw, cb, al4_words, al4_scales, al8_words, al8_scales, b, offs):
    idx = unstriped(offs)
    x_ = mxq(f64(x), 0, "e4m3")
    tab_ = unpack_table4(tab_words, tab_scales)[:, idx]
    d = tab_.T @ x_
    h = f64(cw)[:, None] * sigm(d + f64(cb)[:, None])
    h_ = mxq(h, 0, "e4m3")
    al4_ = unpack_weight(al4_words, al4_scales, "e2m1")
    al8_ = unpack_weight(al8_words, al8_scales, "e4m3")
    y = al4_.T @ h_ + al8_.T @ h_
    return y + f64(b)[:, None]

@@ -1,0 +1,228 @@
+from contextlib import ExitStack
+
+import concourse.mybir as mybir
+
+K, M, N, J, T = 1024, 1024, 256, 1024, 2048
+FLOPS = 2 * K * J * M + 2 * 2 * J * N * M
+
+F32 = mybir.dt.float32
+BF16 = mybir.dt.bfloat16
+I32 = mybir.dt.int32
+U32 = mybir.dt.uint32
+U16 = mybir.dt.uint16
+U8 = mybir.dt.uint8
+FP8X4 = mybir.dt.float8_e4m3fn_x4
+FP4X4 = mybir.dt.float4_e2m1fn_x4
+ACT = mybir.ActivationFunctionType
+ALU = mybir.AluOpType
+
+P = 128
+PACK = 4
+PASS = P * PACK
+LOADS = [(0, 256), (256, 512), (768, 256)]
+CHUNKS = [(0, 0, 256), (1, 0, 512), (2, 0, 128), (2, 128, 128)]
+X_ON_VECTOR = {(2, 0), (2, 1)}
+LIVE = 24
+
+
+def tile_list_kernl_sigm_res_bias_kernel(
+    tc, x, tab_words, tab_scales, cw, cb, al4_words, al4_scales, al8_words, al8_scales, b, offs, out
+):
+    nc = tc.nc
+    with ExitStack() as ctx:
+        keep = ctx.enter_context(tc.tile_pool(name="keep", bufs=1))
+        work = ctx.enter_context(tc.tile_pool(name="work", bufs=3))
+        d_psum = ctx.enter_context(tc.psum_pool(name="d_psum", bufs=4))
+        y_psum = ctx.enter_context(tc.psum_pool(name="y_psum", bufs=4))
+
+        offsets = keep.tile([P, J // 16], U16, name="offsets")
+        nc.sync.dma_start(offsets[:], offs)
+
+        tab_sc = keep.tile([P, T // 4], I32, name="tab_sc", align_bytes=64)
+        for q in range(4):
+            nc.sync.dma_start(tab_sc[32 * q + LIVE : 32 * (q + 1), :], tab_scales[:, 4 * q : 4 * q + 4, :].bitcast(I32))
+        for q in range(4):
+            nc.vector.memset(tab_sc[32 * q : 32 * q + LIVE, :], 0)
+        tab_w = keep.tile([P, T], I32, name="tab_w", align_bytes=64)
+        nc.sync.dma_start(tab_w[:], tab_words[0].rearrange("p t b -> p (t b)").bitcast(I32))
+
+        x_raw = {}
+
+        def load_x(c, a):
+            m0, w = LOADS[c]
+            raw = keep.tile([P, PACK, w], F32, name="x_raw%d%d" % (c, a), align_bytes=64)
+            nc.sync.dma_start(raw[:], x[PASS * a : PASS * (a + 1), m0 : m0 + w].rearrange("(p t) m -> p t m", t=PACK))
+            x_raw[c, a] = raw
+
+        for c in range(len(LOADS)):
+            load_x(c, 0)
+            load_x(c, 1)
+
+        cb_t = keep.tile([P, 2, PACK], F32, name="cb_t")
+        nc.gpsimd.dma_start(cb_t[:], cb.rearrange("(a p t) -> p a t", a=2, t=PACK))
+        cw_t = keep.tile([P, 2, PACK], F32, name="cw_t")
+        nc.gpsimd.dma_start(cw_t[:], cw.rearrange("(a p t) -> p a t", a=2, t=PACK))
+        al_sc = []
+        for name, src in (("al4_sc", al4_scales), ("al8_sc", al8_scales)):
+            plane = keep.tile([P, 2, N // 4], I32, name=name, align_bytes=64)
+            nc.vector.memset(plane[:], 0)
+            for q in range(4):
+                nc.gpsimd.dma_start(
+                    plane[32 * q : 32 * q + 4, :, :], src[:, 4 * q : 4 * q + 4, :].bitcast(I32).rearrange("a r n -> r a n")
+                )
+            al_sc.append(plane)
+        al4_w = keep.tile([P, 2, N // 2], I32, name="al4_w", align_bytes=64)
+        nc.gpsimd.dma_start(al4_w[:], al4_words.bitcast(I32).rearrange("a p n -> p a n"))
+        al8_w = keep.tile([P, 2, N], I32, name="al8_w", align_bytes=64)
+        nc.gpsimd.dma_start(al8_w[:], al8_words.rearrange("a p n i -> a p (n i)").bitcast(I32).rearrange("a p n -> p a n"))
+        b_t = keep.tile([P, 2], F32, name="b_t")
+        with nc.allow_non_contiguous_dma(reason="one bias value a partition"):
+            nc.gpsimd.dma_start(b_t[:], b.rearrange("(h p) -> p h", p=P))
+
+        warm_in = keep.tile([P, 1], F32, name="warm_in")
+        nc.vector.memset(warm_in[:], 0.0)
+        warm_out = keep.tile([P, 1], F32, name="warm_out")
+        nc.scalar.activation(warm_out[:], warm_in[:], ACT.Sigmoid)
+
+        planes = keep.tile([P, 2, J // 4], I32, name="planes", align_bytes=64)
+        nc.vector.memset(planes[96:128, :, :], 0)
+
+        picked_sc = keep.tile([P, J], U8, name="picked_sc", align_bytes=64)
+        nc.vector.tensor_copy(picked_sc[:], tab_sc[:].bitcast(U8).indirect(offsets[:]))
+        sorted_sc = keep.tile([P, J], U8, name="sorted_sc", align_bytes=64)
+        nc.vector.tensor_copy(
+            sorted_sc[:].rearrange("p (a t r) -> p a t r", a=2, t=PACK),
+            picked_sc[:].rearrange("p (a r t) -> p a t r", a=2, t=PACK),
+        )
+        for g in range(2):
+            nc.scalar.dma_start(planes[0:100, g, :], sorted_sc[LIVE + 4 * g : LIVE + 4 * g + 100, :].bitcast(I32))
+        v_sc = [planes[:, g, :].bitcast(U8) for g in range(2)]
+
+        v_w = {}
+
+        def pick_words(a):
+            picked = keep.tile([P, PASS], U32, name="picked_w%d" % a, align_bytes=64)
+            nc.vector.tensor_copy(picked[:], tab_w[:].bitcast(U32).indirect(offsets[:, 32 * a : 32 * (a + 1)]))
+            parted = keep.tile([P, 2, PASS], U16, name="v_w%d" % a, align_bytes=64)
+            nc.vector.tensor_copy(
+                parted[:].rearrange("p g (t r) -> p g r t", t=PACK),
+                picked[:].bitcast(U16).rearrange("p (r t g) -> p g r t", t=PACK, g=2),
+            )
+            v_w[a] = parted
+
+        x_q = {}
+
+        def prep_x(c, g):
+            w = LOADS[c][1]
+            grouped = work.tile([P, PACK * w], BF16, name="x_grouped", align_bytes=64)
+            dst = grouped[:].rearrange("p (c i t) -> p c t i", i=2, t=PACK)
+            src = x_raw[c, g][:].rearrange("p t (c i) -> p c t i", i=2)
+            if (c, g) in X_ON_VECTOR:
+                nc.vector.tensor_copy(dst, src)
+            else:
+                nc.scalar.copy(dst, src)
+            codes = keep.tile([P, w], U32, name="x_codes%d%d" % (c, g), align_bytes=64)
+            scales = keep.tile([P, w], U8, name="x_scales%d%d" % (c, g), align_bytes=64)
+            nc.vector.quantize_mx(out=codes[:].bitcast(FP8X4), scales=scales[:], in_=grouped[:])
+            x_q[c, g] = (codes, scales)
+
+        h_q = {}
+
+        def first_stage(c, a):
+            ld, x0, w = CHUNKS[c]
+            step = 512 if w == 512 else 128
+            sig = work.tile([P, PACK, w], F32, name="sig", align_bytes=64)
+            per_bank = min(512 // w, 2)
+            for t0 in range(0, PACK, per_bank):
+                bank = d_psum.tile([P, per_bank, w], F32, name="d_bank")
+                for u in range(per_bank):
+                    t = t0 + u
+                    cols = slice(PASS * a + P * t, PASS * a + P * (t + 1))
+                    for n0 in range(0, w, step):
+                        for g in range(2):
+                            codes, scales = x_q[ld, g]
+                            nc.tensor.matmul_mx(
+                                out=bank[:, u, n0 : n0 + step],
+                                lhsT=v_w[a][:, g, P * t : P * (t + 1)].bitcast(FP4X4),
+                                lhsT_scale=v_sc[g][:, cols],
+                                rhs=codes[:, x0 + n0 : x0 + n0 + step].bitcast(FP8X4),
+                                rhs_scale=scales[:, x0 + n0 : x0 + n0 + step],
+                                start=(g == 0),
+                                stop=(g == 1),
+                            )
+                for u in range(per_bank):
+                    t = t0 + u
+                    nc.scalar.activation(sig[:, t, :], bank[:, u, :], ACT.Sigmoid, bias=cb_t[:, a, t : t + 1])
+            grouped = work.tile([P, PACK * w], BF16, name="h_grouped", align_bytes=64)
+            nc.vector.tensor_tensor(
+                grouped[:].rearrange("p (c i t) -> p c t i", i=2, t=PACK),
+                sig[:].rearrange("p t (c i) -> p c t i", i=2),
+                cw_t[:, a, :].rearrange("p (c t i) -> p c t i", c=1, i=1).to_broadcast([P, w // 2, PACK, 2]),
+                ALU.mult,
+            )
+            codes = keep.tile([P, w], U32, name="h_codes%d%d" % (c, a), align_bytes=64)
+            scales = keep.tile([P, w], U8, name="h_scales%d%d" % (c, a), align_bytes=64)
+            nc.vector.quantize_mx(out=codes[:].bitcast(FP8X4), scales=scales[:], in_=grouped[:])
+            h_q[c, a] = (codes, scales)
+
+        def second_passes(c, a, half, n0, step, dst):
+            codes, scales = h_q[c, a]
+            rows = slice(P * half, P * (half + 1))
+            al4 = al4_w[:, a, P // 2 * half : P // 2 * (half + 1)].bitcast(FP4X4)
+            al8 = al8_w[:, a, rows].bitcast(FP8X4)
+            for tier, lhsT in enumerate((al4, al8)):
+                nc.tensor.matmul_mx(
+                    out=dst,
+                    lhsT=lhsT,
+                    lhsT_scale=al_sc[tier][:, a, :].bitcast(U8)[:, rows],
+                    rhs=codes[:, n0 : n0 + step].bitcast(FP8X4),
+                    rhs_scale=scales[:, n0 : n0 + step],
+                    start=(a == 0 and tier == 0),
+                    stop=(a == 1 and tier == 1),
+                )
+
+        out_v = out.rearrange("(h p) m -> p h m", p=P)
+        y_banks = {}
+
+        def second_stage(c, a):
+            ld, x0, w = CHUNKS[c]
+            m0 = LOADS[ld][0] + x0
+            step = 512 if w == 512 else 128
+            for half in range(2):
+                for n0 in range(0, w, step):
+                    if a == 0:
+                        y_banks[c, half, n0] = y_psum.tile([P, step], F32, name="y_bank")
+                    second_passes(c, a, half, n0, step, y_banks[c, half, n0][:])
+            if a == 1:
+                res = work.tile([P, 2, w], F32, name="res", align_bytes=64)
+                for half in range(2):
+                    for n0 in range(0, w, step):
+                        nc.scalar.activation(
+                            res[:, half, n0 : n0 + step], y_banks[c, half, n0][:], ACT.Identity, bias=b_t[:, half : half + 1]
+                        )
+                nc.sync.dma_start(out_v[:, :, m0 : m0 + w], res[:])
+
+        pick_words(0)
+        prep_x(0, 0)
+        prep_x(0, 1)
+        first_stage(0, 0)
+        pick_words(1)
+        prep_x(1, 0)
+        first_stage(0, 1)
+        prep_x(1, 1)
+        first_stage(1, 0)
+        prep_x(2, 0)
+        prep_x(2, 1)
+        first_stage(1, 1)
+        second_stage(0, 0)
+        second_stage(0, 1)
+        first_stage(2, 0)
+        second_stage(1, 0)
+        first_stage(2, 1)
+        second_stage(1, 1)
+        first_stage(3, 0)
+        second_stage(2, 0)
+        first_stage(3, 1)
+        second_stage(2, 1)
+        second_stage(3, 0)
+        second_stage(3, 1)

@@ -19,9 +19,8 @@ ALU = mybir.AluOpType
 P = 128
 PACK = 4
 PASS = P * PACK
-LOADS = [(0, 256), (256, 512), (768, 256)]
-CHUNKS = [(0, 0, 256), (1, 0, 512), (2, 0, 128), (2, 128, 128)]
-X_ON_VECTOR = {(2, 0), (2, 1)}
+LOADS = [[0,256],[256,256],[512,256],[768,256]]
+CHUNKS = [[0,256],[256,256],[512,256],[768,128],[896,128]]
 LIVE = 24
 
 
@@ -31,16 +30,16 @@ def tile_list_kernl_sigm_res_bias_kernel(
     nc = tc.nc
     with ExitStack() as ctx:
         keep = ctx.enter_context(tc.tile_pool(name="keep", bufs=1))
-        work = ctx.enter_context(tc.tile_pool(name="work", bufs=3))
-        d_psum = ctx.enter_context(tc.psum_pool(name="d_psum", bufs=4))
-        y_psum = ctx.enter_context(tc.psum_pool(name="y_psum", bufs=4))
+        work = ctx.enter_context(tc.tile_pool(name="work", bufs=4))
+        d_psum = ctx.enter_context(tc.psum_pool(name="d_psum", bufs=5))
+        y_psum = ctx.enter_context(tc.psum_pool(name="y_psum", bufs=3))
 
         offsets = keep.tile([P, J // 16], U16, name="offsets")
         nc.sync.dma_start(offsets[:], offs)
 
         tab_sc = keep.tile([P, T // 4], I32, name="tab_sc", align_bytes=64)
         for q in range(4):
-            nc.sync.dma_start(tab_sc[32 * q + LIVE : 32 * (q + 1), :], tab_scales[:, 4 * q : 4 * q + 4, :].bitcast(I32))
+            nc.sync.dma_start(tab_sc[32 * q + LIVE : 32 * (q + 1), :], tab_scales[:, 4 * q : 4 * q + 4, :].bitcast(I32).rearrange("a r n -> r a n"))
         for q in range(4):
             nc.vector.memset(tab_sc[32 * q : 32 * q + LIVE, :], 0)
         tab_w = keep.tile([P, T], I32, name="tab_w", align_bytes=64)
@@ -54,27 +53,37 @@ def tile_list_kernl_sigm_res_bias_kernel(
             nc.sync.dma_start(raw[:], x[PASS * a : PASS * (a + 1), m0 : m0 + w].rearrange("(p t) m -> p t m", t=PACK))
             x_raw[c, a] = raw
 
-        for c in range(len(LOADS)):
-            load_x(c, 0)
-            load_x(c, 1)
+        al4_w = keep.tile([P, 2, N // 2], I32, name="al4_w", align_bytes=64)
+        al8_w = keep.tile([P, 2, N], I32, name="al8_w", align_bytes=64)
+
+        def load_al4():
+            nc.sync.dma_start(al4_w[:], al4_words.bitcast(I32).rearrange("a p n -> p a n"))
+
+        def load_al8():
+            nc.sync.dma_start(al8_w[:], al8_words.rearrange("a p n i -> a p (n i)").bitcast(I32).rearrange("a p n -> p a n"))
+
+        load_x(0, 0)
+        load_x(0, 1)
+        load_x(1, 0)
 
         cb_t = keep.tile([P, 2, PACK], F32, name="cb_t")
         nc.gpsimd.dma_start(cb_t[:], cb.rearrange("(a p t) -> p a t", a=2, t=PACK))
         cw_t = keep.tile([P, 2, PACK], F32, name="cw_t")
         nc.gpsimd.dma_start(cw_t[:], cw.rearrange("(a p t) -> p a t", a=2, t=PACK))
-        al_sc = []
-        for name, src in (("al4_sc", al4_scales), ("al8_sc", al8_scales)):
-            plane = keep.tile([P, 2, N // 4], I32, name=name, align_bytes=64)
-            nc.vector.memset(plane[:], 0)
+        planes = keep.tile([P, 2, J // 4], I32, name="planes", align_bytes=64)
+        nc.gpsimd.memset(planes[:], 0)
+        al_sc = [keep.tile([P, 2, N // 4], I32, name="al_sc%d" % tier, align_bytes=64) for tier in range(2)]
+        for plane in al_sc:
+            nc.gpsimd.memset(plane[:], 0)
+
+        def load_al_sc(tier, queue):
+            src = (al4_scales, al8_scales)[tier]
             for q in range(4):
-                nc.gpsimd.dma_start(
-                    plane[32 * q : 32 * q + 4, :, :], src[:, 4 * q : 4 * q + 4, :].bitcast(I32).rearrange("a r n -> r a n")
+                queue.dma_start(
+                    al_sc[tier][32 * q : 32 * q + 4, :, :], src[:, 4 * q : 4 * q + 4, :].bitcast(I32).rearrange("a r n -> r a n")
                 )
-            al_sc.append(plane)
-        al4_w = keep.tile([P, 2, N // 2], I32, name="al4_w", align_bytes=64)
-        nc.gpsimd.dma_start(al4_w[:], al4_words.bitcast(I32).rearrange("a p n -> p a n"))
-        al8_w = keep.tile([P, 2, N], I32, name="al8_w", align_bytes=64)
-        nc.gpsimd.dma_start(al8_w[:], al8_words.rearrange("a p n i -> a p (n i)").bitcast(I32).rearrange("a p n -> p a n"))
+
+        load_al_sc(0, nc.gpsimd)
         b_t = keep.tile([P, 2], F32, name="b_t")
         with nc.allow_non_contiguous_dma(reason="one bias value a partition"):
             nc.gpsimd.dma_start(b_t[:], b.rearrange("(h p) -> p h", p=P))
@@ -84,24 +93,26 @@ def tile_list_kernl_sigm_res_bias_kernel(
         warm_out = keep.tile([P, 1], F32, name="warm_out")
         nc.scalar.activation(warm_out[:], warm_in[:], ACT.Sigmoid)
 
-        planes = keep.tile([P, 2, J // 4], I32, name="planes", align_bytes=64)
-        nc.vector.memset(planes[96:128, :, :], 0)
 
         picked_sc = keep.tile([P, J], U8, name="picked_sc", align_bytes=64)
-        nc.vector.tensor_copy(picked_sc[:], tab_sc[:].bitcast(U8).indirect(offsets[:]))
         sorted_sc = keep.tile([P, J], U8, name="sorted_sc", align_bytes=64)
-        nc.vector.tensor_copy(
-            sorted_sc[:].rearrange("p (a t r) -> p a t r", a=2, t=PACK),
-            picked_sc[:].rearrange("p (a r t) -> p a t r", a=2, t=PACK),
-        )
-        for g in range(2):
-            nc.scalar.dma_start(planes[0:100, g, :], sorted_sc[LIVE + 4 * g : LIVE + 4 * g + 100, :].bitcast(I32))
+        for a in range(2):
+            nc.vector.tensor_copy(
+                picked_sc[:, PASS * a : PASS * (a + 1)], tab_sc[:].bitcast(U8).indirect(offsets[:, 32 * a : 32 * (a + 1)])
+            )
+        for a in range(2):
+            nc.vector.tensor_copy(
+                sorted_sc[:, PASS * a : PASS * (a + 1)].rearrange("p (t r) -> p t r", t=PACK),
+                picked_sc[:, PASS * a : PASS * (a + 1)].rearrange("p (r t) -> p t r", t=PACK),
+            )
+        for q in range(4):
+            nc.sync.dma_start(planes[32 * q : 32 * q + 4, :, :], sorted_sc[32 * q + LIVE : 32 * (q + 1), :].bitcast(I32))
         v_sc = [planes[:, g, :].bitcast(U8) for g in range(2)]
 
         v_w = {}
 
         def pick_words(a):
-            picked = keep.tile([P, PASS], U32, name="picked_w%d" % a, align_bytes=64)
+            picked = keep.tile([P, PASS], U32, name="picked_w", align_bytes=64)
             nc.vector.tensor_copy(picked[:], tab_w[:].bitcast(U32).indirect(offsets[:, 32 * a : 32 * (a + 1)]))
             parted = keep.tile([P, 2, PASS], U16, name="v_w%d" % a, align_bytes=64)
             nc.vector.tensor_copy(
@@ -110,29 +121,30 @@ def tile_list_kernl_sigm_res_bias_kernel(
             )
             v_w[a] = parted
 
-        x_q = {}
+        x_codes = [keep.tile([P, M], U32, name="x_codes%d" % g, align_bytes=64) for g in range(2)]
+        x_scales = [keep.tile([P, M], U8, name="x_scales%d" % g, align_bytes=64) for g in range(2)]
 
-        def prep_x(c, g):
-            w = LOADS[c][1]
+        def prep_x(c, g, engine, c0=0, w=None):
+            w = w or LOADS[c][1]
+            m0 = LOADS[c][0] + c0
             grouped = work.tile([P, PACK * w], BF16, name="x_grouped", align_bytes=64)
             dst = grouped[:].rearrange("p (c i t) -> p c t i", i=2, t=PACK)
-            src = x_raw[c, g][:].rearrange("p t (c i) -> p c t i", i=2)
-            if (c, g) in X_ON_VECTOR:
+            src = x_raw[c, g][:, :, c0 : c0 + w].rearrange("p t (c i) -> p c t i", i=2)
+            if engine == "vector":
                 nc.vector.tensor_copy(dst, src)
             else:
                 nc.scalar.copy(dst, src)
-            codes = keep.tile([P, w], U32, name="x_codes%d%d" % (c, g), align_bytes=64)
-            scales = keep.tile([P, w], U8, name="x_scales%d%d" % (c, g), align_bytes=64)
-            nc.vector.quantize_mx(out=codes[:].bitcast(FP8X4), scales=scales[:], in_=grouped[:])
-            x_q[c, g] = (codes, scales)
+            nc.vector.quantize_mx(
+                out=x_codes[g][:, m0 : m0 + w].bitcast(FP8X4), scales=x_scales[g][:, m0 : m0 + w], in_=grouped[:]
+            )
 
         h_q = {}
 
         def first_stage(c, a):
-            ld, x0, w = CHUNKS[c]
+            x0, w = CHUNKS[c]
             step = 512 if w == 512 else 128
             sig = work.tile([P, PACK, w], F32, name="sig", align_bytes=64)
-            per_bank = min(512 // w, 2)
+            per_bank = 1
             for t0 in range(0, PACK, per_bank):
                 bank = d_psum.tile([P, per_bank, w], F32, name="d_bank")
                 for u in range(per_bank):
@@ -140,7 +152,7 @@ def tile_list_kernl_sigm_res_bias_kernel(
                     cols = slice(PASS * a + P * t, PASS * a + P * (t + 1))
                     for n0 in range(0, w, step):
                         for g in range(2):
-                            codes, scales = x_q[ld, g]
+                            codes, scales = x_codes[g], x_scales[g]
                             nc.tensor.matmul_mx(
                                 out=bank[:, u, n0 : n0 + step],
                                 lhsT=v_w[a][:, g, P * t : P * (t + 1)].bitcast(FP4X4),
@@ -184,45 +196,65 @@ def tile_list_kernl_sigm_res_bias_kernel(
         out_v = out.rearrange("(h p) m -> p h m", p=P)
         y_banks = {}
 
-        def second_stage(c, a):
-            ld, x0, w = CHUNKS[c]
-            m0 = LOADS[ld][0] + x0
-            step = 512 if w == 512 else 128
+        def store(c, sums, engines):
+            m0, w = CHUNKS[c]
+            res = work.tile([P, 2, w], F32, name="res", align_bytes=64)
             for half in range(2):
-                for n0 in range(0, w, step):
-                    if a == 0:
-                        y_banks[c, half, n0] = y_psum.tile([P, step], F32, name="y_bank")
-                    second_passes(c, a, half, n0, step, y_banks[c, half, n0][:])
-            if a == 1:
-                res = work.tile([P, 2, w], F32, name="res", align_bytes=64)
-                for half in range(2):
-                    for n0 in range(0, w, step):
-                        nc.scalar.activation(
-                            res[:, half, n0 : n0 + step], y_banks[c, half, n0][:], ACT.Identity, bias=b_t[:, half : half + 1]
-                        )
-                nc.sync.dma_start(out_v[:, :, m0 : m0 + w], res[:])
+                if engines[half] == "scalar":
+                    nc.scalar.activation(res[:, half, :], sums[half], ACT.Identity, bias=b_t[:, half : half + 1])
+                else:
+                    nc.vector.tensor_scalar(res[:, half, :], sums[half], b_t[:, half : half + 1], None, ALU.add)
+            nc.sync.dma_start(out_v[:, :, m0 : m0 + w], res[:])
 
+        def second_closed(c, engines):
+            w = CHUNKS[c][1]
+            bank = y_psum.tile([P, 2, w], F32, name="y_bank")
+            for half in range(2):
+                for n0 in range(0, w, P):
+                    for a in range(2):
+                        second_passes(c, a, half, n0, P, bank[:, half, n0 : n0 + P])
+            store(c, [bank[:, half, :] for half in range(2)], engines)
+
+        def second_open(c, a, engines):
+            w = CHUNKS[c][1]
+            for half in range(2):
+                if a == 0:
+                    y_banks[c, half] = y_psum.tile([P, w], F32, name="y_bank")
+                second_passes(c, a, half, 0, w, y_banks[c, half][:])
+            if a == 1:
+                store(c, [y_banks[c, half][:] for half in range(2)], engines)
+
+        prep_x(0, 1, "scalar")
+        load_x(1, 1)
+        load_x(2, 0)
+        prep_x(0, 0, "vector")
         pick_words(0)
-        prep_x(0, 0)
-        prep_x(0, 1)
+        load_x(2, 1)
+        load_x(3, 0)
+        load_al8()
         first_stage(0, 0)
         pick_words(1)
-        prep_x(1, 0)
+        load_x(3, 1)
         first_stage(0, 1)
-        prep_x(1, 1)
-        first_stage(1, 0)
-        prep_x(2, 0)
-        prep_x(2, 1)
+        prep_x(1, 0, "scalar")
+        prep_x(3, 0, "scalar")
+        prep_x(1, 1, "vector")
+        load_al4()
+        prep_x(2, 0, "vector")
+        prep_x(2, 1, "scalar")
+        load_al_sc(1, nc.sync)
         first_stage(1, 1)
-        second_stage(0, 0)
-        second_stage(0, 1)
+        prep_x(3, 1, "vector")
+        first_stage(1, 0)
         first_stage(2, 0)
-        second_stage(1, 0)
         first_stage(2, 1)
-        second_stage(1, 1)
+        second_closed(0, ("scalar", "scalar"))
+        first_stage(4, 1)
+        second_closed(1, ("vector", "scalar"))
         first_stage(3, 0)
-        second_stage(2, 0)
         first_stage(3, 1)
-        second_stage(2, 1)
-        second_stage(3, 0)
-        second_stage(3, 1)
+        first_stage(4, 0)
+        second_open(4, 0, None)
+        second_open(4, 1, ("scalar", "vector"))
+        second_closed(2, ("vector", "scalar"))
+        second_closed(3, ("scalar", "scalar"))

@@ -19,9 +19,10 @@ ALU = mybir.AluOpType
 P = 128
 PACK = 4
 PASS = P * PACK
-LOADS = [[0,256],[256,256],[512,256],[768,256]]
-CHUNKS = [[0,256],[256,256],[512,256],[768,128],[896,128]]
-LIVE = 24
+RUN = 4
+LOADS = [[0,0,256],[1,0,256],[0,256,512],[1,256,512],[0,768,256],[1,768,256]]
+PIECES = [[0,256],[256,256],[512,256],[768,256]]
+CHUNKS = [[0,256],[256,512],[768,128],[896,128]]
 
 
 def tile_list_kernl_sigm_res_bias_kernel(
@@ -31,47 +32,20 @@ def tile_list_kernl_sigm_res_bias_kernel(
     with ExitStack() as ctx:
         keep = ctx.enter_context(tc.tile_pool(name="keep", bufs=1))
         work = ctx.enter_context(tc.tile_pool(name="work", bufs=4))
-        d_psum = ctx.enter_context(tc.psum_pool(name="d_psum", bufs=5))
-        y_psum = ctx.enter_context(tc.psum_pool(name="y_psum", bufs=3))
+        psum = ctx.enter_context(tc.psum_pool(name="psum", bufs=1))
 
         offsets = keep.tile([P, J // 16], U16, name="offsets")
         nc.sync.dma_start(offsets[:], offs)
 
         tab_sc = keep.tile([P, T // 4], I32, name="tab_sc", align_bytes=64)
-        for q in range(4):
-            nc.sync.dma_start(tab_sc[32 * q + LIVE : 32 * (q + 1), :], tab_scales[:, 4 * q : 4 * q + 4, :].bitcast(I32).rearrange("a r n -> r a n"))
-        for q in range(4):
-            nc.vector.memset(tab_sc[32 * q : 32 * q + LIVE, :], 0)
-        tab_w = keep.tile([P, T], I32, name="tab_w", align_bytes=64)
-        nc.sync.dma_start(tab_w[:], tab_words[0].rearrange("p t b -> p (t b)").bitcast(I32))
+        nc.sync.dma_start(tab_sc[0:32, :], tab_scales.bitcast(I32).rearrange("g r n -> r g n"))
+        nc.vector.memset(tab_sc[32:64, :], 0)
+        nc.vector.memset(tab_sc[64:128, :], 0)
 
-        x_raw = {}
-
-        def load_x(c, a):
-            m0, w = LOADS[c]
-            raw = keep.tile([P, PACK, w], F32, name="x_raw%d%d" % (c, a), align_bytes=64)
-            nc.sync.dma_start(raw[:], x[PASS * a : PASS * (a + 1), m0 : m0 + w].rearrange("(p t) m -> p t m", t=PACK))
-            x_raw[c, a] = raw
-
-        al4_w = keep.tile([P, 2, N // 2], I32, name="al4_w", align_bytes=64)
-        al8_w = keep.tile([P, 2, N], I32, name="al8_w", align_bytes=64)
-
-        def load_al4():
-            nc.sync.dma_start(al4_w[:], al4_words.bitcast(I32).rearrange("a p n -> p a n"))
-
-        def load_al8():
-            nc.sync.dma_start(al8_w[:], al8_words.rearrange("a p n i -> a p (n i)").bitcast(I32).rearrange("a p n -> p a n"))
-
-        load_x(0, 0)
-        load_x(0, 1)
-        load_x(1, 0)
-
-        cb_t = keep.tile([P, 2, PACK], F32, name="cb_t")
-        nc.gpsimd.dma_start(cb_t[:], cb.rearrange("(a p t) -> p a t", a=2, t=PACK))
-        cw_t = keep.tile([P, 2, PACK], F32, name="cw_t")
-        nc.gpsimd.dma_start(cw_t[:], cw.rearrange("(a p t) -> p a t", a=2, t=PACK))
         planes = keep.tile([P, 2, J // 4], I32, name="planes", align_bytes=64)
         nc.gpsimd.memset(planes[:], 0)
+        cb_t = keep.tile([P, 2, PACK], F32, name="cb_t")
+        cw_t = keep.tile([P, 2, PACK], F32, name="cw_t")
         al_sc = [keep.tile([P, 2, N // 4], I32, name="al_sc%d" % tier, align_bytes=64) for tier in range(2)]
         for plane in al_sc:
             nc.gpsimd.memset(plane[:], 0)
@@ -83,98 +57,167 @@ def tile_list_kernl_sigm_res_bias_kernel(
                     al_sc[tier][32 * q : 32 * q + 4, :, :], src[:, 4 * q : 4 * q + 4, :].bitcast(I32).rearrange("a r n -> r a n")
                 )
 
-        load_al_sc(0, nc.gpsimd)
         b_t = keep.tile([P, 2], F32, name="b_t")
-        with nc.allow_non_contiguous_dma(reason="one bias value a partition"):
-            nc.gpsimd.dma_start(b_t[:], b.rearrange("(h p) -> p h", p=P))
+
+        def load_cb(queue):
+            queue.dma_start(cb_t[:], cb.rearrange("(a p t) -> p a t", a=2, t=PACK))
+
+        def load_cw(queue):
+            queue.dma_start(cw_t[:], cw.rearrange("(a p t) -> p a t", a=2, t=PACK))
+
+        cw_runs = keep.tile([P, 2, PACK, RUN], F32, name="cw_runs", align_bytes=64)
+
+        def spread_cw():
+            nc.scalar.copy(cw_runs[:], cw_t[:].rearrange("p a (t i) -> p a t i", i=1).to_broadcast([P, 2, PACK, RUN]))
+
+        def load_b(queue):
+            with nc.allow_non_contiguous_dma(reason="one bias value a partition"):
+                queue.dma_start(b_t[:], b.rearrange("(h p) -> p h", p=P))
 
         warm_in = keep.tile([P, 1], F32, name="warm_in")
         nc.vector.memset(warm_in[:], 0.0)
         warm_out = keep.tile([P, 1], F32, name="warm_out")
         nc.scalar.activation(warm_out[:], warm_in[:], ACT.Sigmoid)
 
+        grouped_ring = [keep.tile([P, PACK * 512], BF16, name="grouped%d" % i, align_bytes=64) for i in range(6)]
+        sig_ring = [keep.tile([P, PACK * 512], F32, name="sig%d" % i, align_bytes=64) for i in range(4)]
+        d_ring = [psum.tile([P, 512], F32, name="d_bank%d" % i) for i in range(5)]
+        y_ring = [psum.tile([P, 512], F32, name="y_bank%d" % i) for i in range(3)]
+
+        rings = {"grouped": grouped_ring, "sig": sig_ring, "d": d_ring, "y": y_ring}
+        turns = {"grouped": 0, "sig": 0, "d": 0, "y": 0}
+
+        def take(name):
+            turns[name] += 1
+            return rings[name][(turns[name] - 1) % len(rings[name])]
+
+        tab_w = keep.tile([P, T], I32, name="tab_w", align_bytes=64)
+
+        def load_words():
+            nc.sync.dma_start(tab_w[:], tab_words[0].rearrange("p t b -> p (t b)").bitcast(I32))
+
+        x_raw = {}
+
+        def load_x(i):
+            g, m0, w = LOADS[i]
+            x_raw[i] = keep.tile([P, PACK, w], F32, name="x_raw%d" % i, align_bytes=64)
+            nc.sync.dma_start(x_raw[i][:], x[PASS * g : PASS * (g + 1), m0 : m0 + w].rearrange("(p t) m -> p t m", t=PACK))
+
+        al4_w = keep.tile([P, 2, N // 2], I32, name="al4_w", align_bytes=64)
+        al8_w = keep.tile([P, 2, N], I32, name="al8_w", align_bytes=64)
+
+        def load_al4():
+            nc.sync.dma_start(al4_w[:], al4_words.bitcast(I32).rearrange("a p n -> p a n"))
+
+        def load_al8():
+            nc.sync.dma_start(al8_w[:], al8_words.rearrange("a p n i -> a p (n i)").bitcast(I32).rearrange("a p n -> p a n"))
 
         picked_sc = keep.tile([P, J], U8, name="picked_sc", align_bytes=64)
         sorted_sc = keep.tile([P, J], U8, name="sorted_sc", align_bytes=64)
-        for a in range(2):
+
+        def pick_scales(a):
             nc.vector.tensor_copy(
                 picked_sc[:, PASS * a : PASS * (a + 1)], tab_sc[:].bitcast(U8).indirect(offsets[:, 32 * a : 32 * (a + 1)])
             )
-        for a in range(2):
+
+        def sort_scales(a):
             nc.vector.tensor_copy(
                 sorted_sc[:, PASS * a : PASS * (a + 1)].rearrange("p (t r) -> p t r", t=PACK),
                 picked_sc[:, PASS * a : PASS * (a + 1)].rearrange("p (r t) -> p t r", t=PACK),
             )
-        for q in range(4):
-            nc.sync.dma_start(planes[32 * q : 32 * q + 4, :, :], sorted_sc[32 * q + LIVE : 32 * (q + 1), :].bitcast(I32))
-        v_sc = [planes[:, g, :].bitcast(U8) for g in range(2)]
 
+        def move_planes(queue):
+            for q in range(4):
+                queue.dma_start(planes[32 * q : 32 * q + 4, :, :], sorted_sc[8 * q : 8 * (q + 1), :].bitcast(I32))
+
+        v_sc = [planes[:, g, :].bitcast(U8) for g in range(2)]
+        picked_w = {}
         v_w = {}
 
         def pick_words(a):
-            picked = keep.tile([P, PASS], U32, name="picked_w", align_bytes=64)
-            nc.vector.tensor_copy(picked[:], tab_w[:].bitcast(U32).indirect(offsets[:, 32 * a : 32 * (a + 1)]))
-            parted = keep.tile([P, 2, PASS], U16, name="v_w%d" % a, align_bytes=64)
+            picked_w[a] = keep.tile([P, PASS], U32, name="picked_w%d" % a, align_bytes=64)
+            nc.vector.tensor_copy(picked_w[a][:], tab_w[:].bitcast(U32).indirect(offsets[:, 32 * a : 32 * (a + 1)]))
+
+        def part_words(a):
+            v_w[a] = keep.tile([P, 2, PASS], U16, name="v_w%d" % a, align_bytes=64)
             nc.vector.tensor_copy(
-                parted[:].rearrange("p g (t r) -> p g r t", t=PACK),
-                picked[:].bitcast(U16).rearrange("p (r t g) -> p g r t", t=PACK, g=2),
+                v_w[a][:].rearrange("p g (t r) -> p g r t", t=PACK),
+                picked_w[a][:].bitcast(U16).rearrange("p (r t g) -> p g r t", t=PACK, g=2),
             )
-            v_w[a] = parted
 
         x_codes = [keep.tile([P, M], U32, name="x_codes%d" % g, align_bytes=64) for g in range(2)]
         x_scales = [keep.tile([P, M], U8, name="x_scales%d" % g, align_bytes=64) for g in range(2)]
+        x_grouped = {}
 
-        def prep_x(c, g, engine, c0=0, w=None):
-            w = w or LOADS[c][1]
-            m0 = LOADS[c][0] + c0
-            grouped = work.tile([P, PACK * w], BF16, name="x_grouped", align_bytes=64)
-            dst = grouped[:].rearrange("p (c i t) -> p c t i", i=2, t=PACK)
-            src = x_raw[c, g][:, :, c0 : c0 + w].rearrange("p t (c i) -> p c t i", i=2)
+        def copy_x(s, g, engine):
+            m0, w = PIECES[s]
+            i = [n for n, (h, l0, lw) in enumerate(LOADS) if h == g and l0 <= m0 < l0 + lw][0]
+            c0 = m0 - LOADS[i][1]
+            x_grouped[s, g] = take("grouped")[:, 0 : PACK * w]
+            dst = x_grouped[s, g].rearrange("p (c i t) -> p c t i", i=RUN, t=PACK)
+            src = x_raw[i][:, :, c0 : c0 + w].rearrange("p t (c i) -> p c t i", i=RUN)
             if engine == "vector":
                 nc.vector.tensor_copy(dst, src)
             else:
                 nc.scalar.copy(dst, src)
+
+        def quant_x(s, g):
+            m0, w = PIECES[s]
             nc.vector.quantize_mx(
-                out=x_codes[g][:, m0 : m0 + w].bitcast(FP8X4), scales=x_scales[g][:, m0 : m0 + w], in_=grouped[:]
+                out=x_codes[g][:, m0 : m0 + w].bitcast(FP8X4), scales=x_scales[g][:, m0 : m0 + w], in_=x_grouped[s, g]
             )
 
+        def warm_pe(count):
+            for i in range(count):
+                nc.tensor.matmul_mx(
+                    out=y_ring[-1][:, 0:256],
+                    lhsT=x_codes[0][:, 0:P].bitcast(FP8X4),
+                    lhsT_scale=x_scales[0][:, 0:P],
+                    rhs=x_codes[0][:, 0:256].bitcast(FP8X4),
+                    rhs_scale=x_scales[0][:, 0:256],
+                    start=True,
+                    stop=True,
+                )
+
+        sigs = {}
+        h_grouped = {}
         h_q = {}
 
         def first_stage(c, a):
-            x0, w = CHUNKS[c]
-            step = 512 if w == 512 else 128
-            sig = work.tile([P, PACK, w], F32, name="sig", align_bytes=64)
-            per_bank = 1
-            for t0 in range(0, PACK, per_bank):
-                bank = d_psum.tile([P, per_bank, w], F32, name="d_bank")
-                for u in range(per_bank):
-                    t = t0 + u
-                    cols = slice(PASS * a + P * t, PASS * a + P * (t + 1))
-                    for n0 in range(0, w, step):
-                        for g in range(2):
-                            codes, scales = x_codes[g], x_scales[g]
-                            nc.tensor.matmul_mx(
-                                out=bank[:, u, n0 : n0 + step],
-                                lhsT=v_w[a][:, g, P * t : P * (t + 1)].bitcast(FP4X4),
-                                lhsT_scale=v_sc[g][:, cols],
-                                rhs=codes[:, x0 + n0 : x0 + n0 + step].bitcast(FP8X4),
-                                rhs_scale=scales[:, x0 + n0 : x0 + n0 + step],
-                                start=(g == 0),
-                                stop=(g == 1),
-                            )
-                for u in range(per_bank):
-                    t = t0 + u
-                    nc.scalar.activation(sig[:, t, :], bank[:, u, :], ACT.Sigmoid, bias=cb_t[:, a, t : t + 1])
-            grouped = work.tile([P, PACK * w], BF16, name="h_grouped", align_bytes=64)
+            m0, w = CHUNKS[c]
+            step = 512 if w == 512 else P
+            sigs[c, a] = take("sig")[:, 0 : PACK * w].rearrange("p (t m) -> p t m", t=PACK)
+            for t in range(PACK):
+                bank = take("d")[:, 0:w]
+                cols = slice(PASS * a + P * t, PASS * a + P * (t + 1))
+                for n0 in range(0, w, step):
+                    for g in range(2):
+                        nc.tensor.matmul_mx(
+                            out=bank[:, n0 : n0 + step],
+                            lhsT=v_w[a][:, g, P * t : P * (t + 1)].bitcast(FP4X4),
+                            lhsT_scale=v_sc[g][:, cols],
+                            rhs=x_codes[g][:, m0 + n0 : m0 + n0 + step].bitcast(FP8X4),
+                            rhs_scale=x_scales[g][:, m0 + n0 : m0 + n0 + step],
+                            start=(g == 0),
+                            stop=(g == 1),
+                        )
+                nc.scalar.activation(sigs[c, a][:, t, :], bank, ACT.Sigmoid, bias=cb_t[:, a, t : t + 1])
+
+        def weigh(c, a):
+            w = CHUNKS[c][1]
+            h_grouped[c, a] = take("grouped")[:, 0 : PACK * w]
             nc.vector.tensor_tensor(
-                grouped[:].rearrange("p (c i t) -> p c t i", i=2, t=PACK),
-                sig[:].rearrange("p t (c i) -> p c t i", i=2),
-                cw_t[:, a, :].rearrange("p (c t i) -> p c t i", c=1, i=1).to_broadcast([P, w // 2, PACK, 2]),
+                h_grouped[c, a].rearrange("p (c i t) -> p c t i", i=RUN, t=PACK),
+                sigs[c, a].rearrange("p t (c i) -> p c t i", i=RUN),
+                cw_runs[:, a : a + 1, :, :].to_broadcast([P, w // RUN, PACK, RUN]),
                 ALU.mult,
             )
+
+        def quant_h(c, a):
+            w = CHUNKS[c][1]
             codes = keep.tile([P, w], U32, name="h_codes%d%d" % (c, a), align_bytes=64)
             scales = keep.tile([P, w], U8, name="h_scales%d%d" % (c, a), align_bytes=64)
-            nc.vector.quantize_mx(out=codes[:].bitcast(FP8X4), scales=scales[:], in_=grouped[:])
+            nc.vector.quantize_mx(out=codes[:].bitcast(FP8X4), scales=scales[:], in_=h_grouped[c, a])
             h_q[c, a] = (codes, scales)
 
         def second_passes(c, a, half, n0, step, dst):
@@ -194,67 +237,105 @@ def tile_list_kernl_sigm_res_bias_kernel(
                 )
 
         out_v = out.rearrange("(h p) m -> p h m", p=P)
-        y_banks = {}
+        sums = {}
 
-        def store(c, sums, engines):
+        def second_closed(c):
+            w = CHUNKS[c][1]
+            bank = take("y")[:, 0 : 2 * w].rearrange("p (h m) -> p h m", h=2)
+            for half in range(2):
+                sums[c, half] = bank[:, half, :]
+                for n0 in range(0, w, P):
+                    for a in range(2):
+                        second_passes(c, a, half, n0, P, bank[:, half, n0 : n0 + P])
+
+        def second_open(c, a):
+            w = CHUNKS[c][1]
+            for half in range(2):
+                if a == 0:
+                    sums[c, half] = take("y")[:, 0:w]
+                second_passes(c, a, half, 0, w, sums[c, half])
+
+        def store(c, engines):
             m0, w = CHUNKS[c]
             res = work.tile([P, 2, w], F32, name="res", align_bytes=64)
             for half in range(2):
                 if engines[half] == "scalar":
-                    nc.scalar.activation(res[:, half, :], sums[half], ACT.Identity, bias=b_t[:, half : half + 1])
+                    nc.scalar.activation(res[:, half, :], sums[c, half], ACT.Identity, bias=b_t[:, half : half + 1])
                 else:
-                    nc.vector.tensor_scalar(res[:, half, :], sums[half], b_t[:, half : half + 1], None, ALU.add)
+                    nc.vector.tensor_scalar(res[:, half, :], sums[c, half], b_t[:, half : half + 1], None, ALU.add)
             nc.sync.dma_start(out_v[:, :, m0 : m0 + w], res[:])
 
-        def second_closed(c, engines):
-            w = CHUNKS[c][1]
-            bank = y_psum.tile([P, 2, w], F32, name="y_bank")
-            for half in range(2):
-                for n0 in range(0, w, P):
-                    for a in range(2):
-                        second_passes(c, a, half, n0, P, bank[:, half, n0 : n0 + P])
-            store(c, [bank[:, half, :] for half in range(2)], engines)
-
-        def second_open(c, a, engines):
-            w = CHUNKS[c][1]
-            for half in range(2):
-                if a == 0:
-                    y_banks[c, half] = y_psum.tile([P, w], F32, name="y_bank")
-                second_passes(c, a, half, 0, w, y_banks[c, half][:])
-            if a == 1:
-                store(c, [y_banks[c, half][:] for half in range(2)], engines)
-
-        prep_x(0, 1, "scalar")
-        load_x(1, 1)
-        load_x(2, 0)
-        prep_x(0, 0, "vector")
+        load_words()
+        pick_scales(0)
+        load_x(2)
+        copy_x(2, 0, "scalar")
         pick_words(0)
-        load_x(2, 1)
-        load_x(3, 0)
-        load_al8()
-        first_stage(0, 0)
+        load_x(1)
+        copy_x(0, 1, "scalar")
+        load_x(0)
+        load_x(3)
+        sort_scales(0)
+        pick_scales(1)
+        quant_x(0, 1)
+        copy_x(0, 0, "scalar")
+        load_x(5)
+        copy_x(2, 1, "scalar")
+        sort_scales(1)
+        load_x(4)
+        quant_x(0, 0)
         pick_words(1)
-        load_x(3, 1)
-        first_stage(0, 1)
-        prep_x(1, 0, "scalar")
-        prep_x(3, 0, "scalar")
-        prep_x(1, 1, "vector")
+        load_cb(nc.scalar)
+        copy_x(1, 1, "vector")
         load_al4()
-        prep_x(2, 0, "vector")
-        prep_x(2, 1, "scalar")
-        load_al_sc(1, nc.sync)
-        first_stage(1, 1)
-        prep_x(3, 1, "vector")
+        quant_x(1, 1)
+        move_planes(nc.scalar)
+        load_cw(nc.scalar)
+        part_words(0)
+        part_words(1)
+        first_stage(0, 1)
+        load_b(nc.sync)
+        load_al_sc(0, nc.sync)
+        copy_x(1, 0, "scalar")
+        quant_x(2, 1)
+        quant_x(2, 0)
+        first_stage(0, 0)
+        copy_x(3, 1, "vector")
+        spread_cw()
+        weigh(0, 1)
+        quant_x(1, 0)
+        quant_x(3, 1)
+        quant_h(0, 1)
         first_stage(1, 0)
+        weigh(0, 0)
+        quant_h(0, 0)
+        copy_x(3, 0, "vector")
+        quant_x(3, 0)
+        first_stage(1, 1)
         first_stage(2, 0)
+        load_al_sc(1, nc.sync)
+        weigh(1, 0)
+        weigh(1, 1)
+        load_al8()
+        quant_h(1, 0)
         first_stage(2, 1)
-        second_closed(0, ("scalar", "scalar"))
-        first_stage(4, 1)
-        second_closed(1, ("vector", "scalar"))
         first_stage(3, 0)
+        quant_h(1, 1)
+        weigh(2, 0)
+        second_closed(0)
+        quant_h(2, 0)
         first_stage(3, 1)
-        first_stage(4, 0)
-        second_open(4, 0, None)
-        second_open(4, 1, ("scalar", "vector"))
-        second_closed(2, ("vector", "scalar"))
-        second_closed(3, ("scalar", "scalar"))
+        weigh(2, 1)
+        quant_h(2, 1)
+        second_open(1, 0)
+        weigh(3, 0)
+        quant_h(3, 0)
+        second_open(1, 1)
+        weigh(3, 1)
+        store(0, ("scalar", "scalar"))
+        quant_h(3, 1)
+        store(1, ("scalar", "scalar"))
+        second_closed(2)
+        second_open(3, 0)
+        second_open(3, 1)
+        store(3, ("vector", "scalar"))
+        store(2, ("scalar", "scalar"))

@@ -20,9 +20,9 @@ P = 128
 PACK = 4
 PASS = P * PACK
 RUN = 4
-LOADS = [[0,0,256],[1,0,256],[0,256,512],[1,256,512],[0,768,256],[1,768,256]]
-PIECES = [[0,256],[256,256],[512,256],[768,256]]
-CHUNKS = [[0,256],[256,512],[768,128],[896,128]]
+WIDE = 512
+PIECE = 256
+D_BANKS = 4
 
 
 def tile_list_kernl_sigm_res_bias_kernel(
@@ -31,311 +31,274 @@ def tile_list_kernl_sigm_res_bias_kernel(
     nc = tc.nc
     with ExitStack() as ctx:
         keep = ctx.enter_context(tc.tile_pool(name="keep", bufs=1))
-        work = ctx.enter_context(tc.tile_pool(name="work", bufs=4))
         psum = ctx.enter_context(tc.psum_pool(name="psum", bufs=1))
 
         offsets = keep.tile([P, J // 16], U16, name="offsets")
         nc.sync.dma_start(offsets[:], offs)
 
         tab_sc = keep.tile([P, T // 4], I32, name="tab_sc", align_bytes=64)
-        nc.sync.dma_start(tab_sc[0:32, :], tab_scales.bitcast(I32).rearrange("g r n -> r g n"))
+        nc.scalar.dma_start(tab_sc[0:32, :], tab_scales.bitcast(I32).rearrange("g r n -> r g n"))
         nc.vector.memset(tab_sc[32:64, :], 0)
         nc.vector.memset(tab_sc[64:128, :], 0)
 
-        planes = keep.tile([P, 2, J // 4], I32, name="planes", align_bytes=64)
-        nc.gpsimd.memset(planes[:], 0)
-        cb_t = keep.tile([P, 2, PACK], F32, name="cb_t")
-        cw_t = keep.tile([P, 2, PACK], F32, name="cw_t")
-        al_sc = [keep.tile([P, 2, N // 4], I32, name="al_sc%d" % tier, align_bytes=64) for tier in range(2)]
-        for plane in al_sc:
-            nc.gpsimd.memset(plane[:], 0)
-
-        def load_al_sc(tier, queue):
-            src = (al4_scales, al8_scales)[tier]
-            for q in range(4):
-                queue.dma_start(
-                    al_sc[tier][32 * q : 32 * q + 4, :, :], src[:, 4 * q : 4 * q + 4, :].bitcast(I32).rearrange("a r n -> r a n")
-                )
-
-        b_t = keep.tile([P, 2], F32, name="b_t")
-
-        def load_cb(queue):
-            queue.dma_start(cb_t[:], cb.rearrange("(a p t) -> p a t", a=2, t=PACK))
-
-        def load_cw(queue):
-            queue.dma_start(cw_t[:], cw.rearrange("(a p t) -> p a t", a=2, t=PACK))
-
-        cw_runs = keep.tile([P, 2, PACK, RUN], F32, name="cw_runs", align_bytes=64)
-
-        def spread_cw():
-            nc.scalar.copy(cw_runs[:], cw_t[:].rearrange("p a (t i) -> p a t i", i=1).to_broadcast([P, 2, PACK, RUN]))
-
-        def load_b(queue):
-            with nc.allow_non_contiguous_dma(reason="one bias value a partition"):
-                queue.dma_start(b_t[:], b.rearrange("(h p) -> p h", p=P))
+        planes = keep.tile([P, 2, (J + 2 * N) // 4], I32, name="planes", align_bytes=64)
+        nc.vector.memset(planes[:], 0)
 
         warm_in = keep.tile([P, 1], F32, name="warm_in")
         nc.vector.memset(warm_in[:], 0.0)
         warm_out = keep.tile([P, 1], F32, name="warm_out")
         nc.scalar.activation(warm_out[:], warm_in[:], ACT.Sigmoid)
 
-        grouped_ring = [keep.tile([P, PACK * 512], BF16, name="grouped%d" % i, align_bytes=64) for i in range(6)]
-        sig_ring = [keep.tile([P, PACK * 512], F32, name="sig%d" % i, align_bytes=64) for i in range(4)]
-        d_ring = [psum.tile([P, 512], F32, name="d_bank%d" % i) for i in range(5)]
-        y_ring = [psum.tile([P, 512], F32, name="y_bank%d" % i) for i in range(3)]
+        cb_t = keep.tile([P, 2, PACK], F32, name="cb_t")
+        cw_t = keep.tile([P, 2, PACK], F32, name="cw_t")
+        nc.gpsimd.dma_start(cb_t[:], cb.rearrange("(a p t) -> p a t", a=2, t=PACK))
+        nc.gpsimd.dma_start(cw_t[:], cw.rearrange("(a p t) -> p a t", a=2, t=PACK))
+        b_t = keep.tile([P, 2], F32, name="b_t")
+        with nc.allow_non_contiguous_dma(reason="one bias value a partition"):
+            nc.gpsimd.dma_start(b_t[:], b.rearrange("(h p) -> p h", p=P))
+        sorted_sc = keep.tile([P, J + 2 * N], U8, name="sorted_sc", align_bytes=64)
+        for tier, src in enumerate((al4_scales, al8_scales)):
+            cols = slice(J + N * tier, J + N * (tier + 1))
+            nc.scalar.dma_start(sorted_sc[0:32, cols].bitcast(I32), src.bitcast(I32).rearrange("g r n -> r g n"))
+        cw_runs = keep.tile([P, 2, PACK, RUN], F32, name="cw_runs", align_bytes=64)
+        nc.gpsimd.tensor_copy(cw_runs[:], cw_t[:].rearrange("p a (t i) -> p a t i", i=1).to_broadcast([P, 2, PACK, RUN]))
 
-        rings = {"grouped": grouped_ring, "sig": sig_ring, "d": d_ring, "y": y_ring}
-        turns = {"grouped": 0, "sig": 0, "d": 0, "y": 0}
+        banks = [psum.tile([P, 512], F32, name="bank%d" % i) for i in range(8)]
+        turns = {"d": 0}
 
-        def take(name):
-            turns[name] += 1
-            return rings[name][(turns[name] - 1) % len(rings[name])]
+        def next_bank():
+            turns["d"] = turns["d"] + 1
+            return banks[(turns["d"] - 1) % D_BANKS]
 
         tab_w = keep.tile([P, T], I32, name="tab_w", align_bytes=64)
-
-        def load_words():
-            nc.sync.dma_start(tab_w[:], tab_words[0].rearrange("p t b -> p (t b)").bitcast(I32))
-
         x_raw = {}
 
-        def load_x(i):
-            g, m0, w = LOADS[i]
-            x_raw[i] = keep.tile([P, PACK, w], F32, name="x_raw%d" % i, align_bytes=64)
-            nc.sync.dma_start(x_raw[i][:], x[PASS * g : PASS * (g + 1), m0 : m0 + w].rearrange("(p t) m -> p t m", t=PACK))
+        sig_tiles = {
+            (c, a): keep.tile([P, PACK * WIDE], F32, name="sig%d%d" % (c, a), align_bytes=64) for c in range(2) for a in range(2)
+        }
+        sigs = {key: tile[:].rearrange("p (t m) -> p t m", t=PACK) for key, tile in sig_tiles.items()}
 
-        al4_w = keep.tile([P, 2, N // 2], I32, name="al4_w", align_bytes=64)
-        al8_w = keep.tile([P, 2, N], I32, name="al8_w", align_bytes=64)
-
-        def load_al4():
-            nc.sync.dma_start(al4_w[:], al4_words.bitcast(I32).rearrange("a p n -> p a n"))
-
-        def load_al8():
-            nc.sync.dma_start(al8_w[:], al8_words.rearrange("a p n i -> a p (n i)").bitcast(I32).rearrange("a p n -> p a n"))
+        def load_x(s, g):
+            if g == 0 and s >= 2:
+                raw = sig_tiles[0, 1][:, PACK * PIECE * (s - 2) : PACK * PIECE * (s - 1)]
+            else:
+                raw = keep.tile([P, PACK * PIECE], F32, name="x_raw%d%d" % (s, g), tag="raw%d%d" % (s, g), align_bytes=64)[:]
+            x_raw[s, g] = raw.rearrange("p (t m) -> p t m", t=PACK)
+            rows = x[PASS * g : PASS * (g + 1), PIECE * s : PIECE * (s + 1)]
+            nc.sync.dma_start(x_raw[s, g], rows.rearrange("(p t) m -> p t m", t=PACK))
 
         picked_sc = keep.tile([P, J], U8, name="picked_sc", align_bytes=64)
-        sorted_sc = keep.tile([P, J], U8, name="sorted_sc", align_bytes=64)
-
-        def pick_scales(a):
-            nc.vector.tensor_copy(
-                picked_sc[:, PASS * a : PASS * (a + 1)], tab_sc[:].bitcast(U8).indirect(offsets[:, 32 * a : 32 * (a + 1)])
-            )
-
-        def sort_scales(a):
-            nc.vector.tensor_copy(
-                sorted_sc[:, PASS * a : PASS * (a + 1)].rearrange("p (t r) -> p t r", t=PACK),
-                picked_sc[:, PASS * a : PASS * (a + 1)].rearrange("p (r t) -> p t r", t=PACK),
-            )
-
-        def move_planes(queue):
-            for q in range(4):
-                queue.dma_start(planes[32 * q : 32 * q + 4, :, :], sorted_sc[8 * q : 8 * (q + 1), :].bitcast(I32))
-
-        v_sc = [planes[:, g, :].bitcast(U8) for g in range(2)]
-        picked_w = {}
+        picked_w = keep.tile([P, PASS], U32, name="picked_w", align_bytes=64)
         v_w = {}
 
         def pick_words(a):
-            picked_w[a] = keep.tile([P, PASS], U32, name="picked_w%d" % a, align_bytes=64)
-            nc.vector.tensor_copy(picked_w[a][:], tab_w[:].bitcast(U32).indirect(offsets[:, 32 * a : 32 * (a + 1)]))
+            nc.vector.tensor_copy(picked_w[:], tab_w[:].bitcast(U32).indirect(offsets[:, 32 * a : 32 * (a + 1)]))
 
-        def part_words(a):
-            v_w[a] = keep.tile([P, 2, PASS], U16, name="v_w%d" % a, align_bytes=64)
+        def part_words(a, tag):
+            v_w[a] = keep.tile([P, 2, PASS], U16, name="v_w%d" % a, tag=tag, align_bytes=64)
             nc.vector.tensor_copy(
                 v_w[a][:].rearrange("p g (t r) -> p g r t", t=PACK),
-                picked_w[a][:].bitcast(U16).rearrange("p (r t g) -> p g r t", t=PACK, g=2),
+                picked_w[:].bitcast(U16).rearrange("p (r t g) -> p g r t", t=PACK, g=2),
             )
 
-        x_codes = [keep.tile([P, M], U32, name="x_codes%d" % g, align_bytes=64) for g in range(2)]
-        x_scales = [keep.tile([P, M], U8, name="x_scales%d" % g, align_bytes=64) for g in range(2)]
-        x_grouped = {}
+        x_codes = [keep.tile([P, 2 * WIDE], U32, name="x_codes%d" % c, align_bytes=64) for c in range(2)]
+        x_scales = [keep.tile([P, 2 * WIDE], U8, name="x_scales%d" % c, align_bytes=64) for c in range(2)]
+        x_grouped = [keep.tile([P, 2 * PACK * WIDE], BF16, name="x_grouped%d" % c, align_bytes=64) for c in range(2)]
 
-        def copy_x(s, g, engine):
-            m0, w = PIECES[s]
-            i = [n for n, (h, l0, lw) in enumerate(LOADS) if h == g and l0 <= m0 < l0 + lw][0]
-            c0 = m0 - LOADS[i][1]
-            x_grouped[s, g] = take("grouped")[:, 0 : PACK * w]
-            dst = x_grouped[s, g].rearrange("p (c i t) -> p c t i", i=RUN, t=PACK)
-            src = x_raw[i][:, :, c0 : c0 + w].rearrange("p t (c i) -> p c t i", i=RUN)
-            if engine == "vector":
-                nc.vector.tensor_copy(dst, src)
-            else:
-                nc.scalar.copy(dst, src)
+        def x_staged(c, g, n0, w):
+            at = WIDE * g + n0
+            if c == 0:
+                at = PIECE * g if n0 == 0 else PIECE * (3 - g)
+            return x_grouped[c][:, PACK * at : PACK * (at + w)]
 
-        def quant_x(s, g):
-            m0, w = PIECES[s]
+        def copy_x(s, g, copy):
+            copy(
+                x_staged(s // 2, g, PIECE * (s % 2), PIECE).rearrange("p (c i t) -> p c t i", i=RUN, t=PACK),
+                x_raw[s, g].rearrange("p t (c i) -> p c t i", i=RUN),
+            )
+
+        def quantise(name, grouped, width):
+            codes = keep.tile([P, width], U32, name=name + "_codes", align_bytes=64)
+            scales = keep.tile([P, width], U8, name=name + "_scales", align_bytes=64)
+            nc.vector.quantize_mx(out=codes[:].bitcast(FP8X4), scales=scales[:], in_=grouped)
+            return codes, scales
+
+        def quant_x(c, g, n0, w):
+            at = WIDE * g + n0
             nc.vector.quantize_mx(
-                out=x_codes[g][:, m0 : m0 + w].bitcast(FP8X4), scales=x_scales[g][:, m0 : m0 + w], in_=x_grouped[s, g]
+                out=x_codes[c][:, at : at + w].bitcast(FP8X4),
+                scales=x_scales[c][:, at : at + w],
+                in_=x_staged(c, g, n0, w),
             )
 
-        def warm_pe(count):
-            for i in range(count):
-                nc.tensor.matmul_mx(
-                    out=y_ring[-1][:, 0:256],
-                    lhsT=x_codes[0][:, 0:P].bitcast(FP8X4),
-                    lhsT_scale=x_scales[0][:, 0:P],
-                    rhs=x_codes[0][:, 0:256].bitcast(FP8X4),
-                    rhs_scale=x_scales[0][:, 0:256],
-                    start=True,
-                    stop=True,
-                )
-
-        sigs = {}
-        h_grouped = {}
-        h_q = {}
-
-        def first_stage(c, a):
-            m0, w = CHUNKS[c]
-            step = 512 if w == 512 else P
-            sigs[c, a] = take("sig")[:, 0 : PACK * w].rearrange("p (t m) -> p t m", t=PACK)
+        def first_stage(c, a, n0, w):
+            step = w if w == WIDE else P
             for t in range(PACK):
-                bank = take("d")[:, 0:w]
-                cols = slice(PASS * a + P * t, PASS * a + P * (t + 1))
-                for n0 in range(0, w, step):
+                bank = next_bank()
+                for k in range(0, w, step):
                     for g in range(2):
+                        at = WIDE * g + n0 + k
                         nc.tensor.matmul_mx(
-                            out=bank[:, n0 : n0 + step],
+                            out=bank[:, k : k + step],
                             lhsT=v_w[a][:, g, P * t : P * (t + 1)].bitcast(FP4X4),
-                            lhsT_scale=v_sc[g][:, cols],
-                            rhs=x_codes[g][:, m0 + n0 : m0 + n0 + step].bitcast(FP8X4),
-                            rhs_scale=x_scales[g][:, m0 + n0 : m0 + n0 + step],
+                            lhsT_scale=planes[:, g, :].bitcast(U8)[:, PASS * a + P * t : PASS * a + P * (t + 1)],
+                            rhs=x_codes[c][:, at : at + step].bitcast(FP8X4),
+                            rhs_scale=x_scales[c][:, at : at + step],
                             start=(g == 0),
                             stop=(g == 1),
                         )
-                nc.scalar.activation(sigs[c, a][:, t, :], bank, ACT.Sigmoid, bias=cb_t[:, a, t : t + 1])
+                nc.scalar.activation(sigs[c, a][:, t, n0 : n0 + w], bank[:, 0:w], ACT.Sigmoid, bias=cb_t[:, a, t : t + 1])
 
-        def weigh(c, a):
-            w = CHUNKS[c][1]
-            h_grouped[c, a] = take("grouped")[:, 0 : PACK * w]
+        h_q = {}
+
+        def weigh(dst, c, a, n0, w):
             nc.vector.tensor_tensor(
-                h_grouped[c, a].rearrange("p (c i t) -> p c t i", i=RUN, t=PACK),
-                sigs[c, a].rearrange("p t (c i) -> p c t i", i=RUN),
+                dst.rearrange("p (c i t) -> p c t i", i=RUN, t=PACK),
+                sigs[c, a][:, :, n0 : n0 + w].rearrange("p t (c i) -> p c t i", i=RUN),
                 cw_runs[:, a : a + 1, :, :].to_broadcast([P, w // RUN, PACK, RUN]),
                 ALU.mult,
             )
 
-        def quant_h(c, a):
-            w = CHUNKS[c][1]
-            codes = keep.tile([P, w], U32, name="h_codes%d%d" % (c, a), align_bytes=64)
-            scales = keep.tile([P, w], U8, name="h_scales%d%d" % (c, a), align_bytes=64)
-            nc.vector.quantize_mx(out=codes[:].bitcast(FP8X4), scales=scales[:], in_=h_grouped[c, a])
-            h_q[c, a] = (codes, scales)
+        def staging(name, columns):
+            return keep.tile([P, PACK * columns], BF16, name=name, align_bytes=64)
 
-        def second_passes(c, a, half, n0, step, dst):
-            codes, scales = h_q[c, a]
+        def quant_h(grouped, parts):
+            c, a, n0, w = parts[0]
+            codes, scales = quantise("h%d%d%d" % (c, a, n0), grouped[:], sum(part[3] for part in parts))
+            at = 0
+            for c, a, n0, w in parts:
+                for k in range(0, w, P):
+                    h_q[c, a, n0 + k] = (codes[:, at + k : at + w], scales[:, at + k : at + w])
+                at = at + w
+
+        al4_w = keep.tile([P, 2, N // 2], I32, name="al4_w", align_bytes=64)
+        al8_w = keep.tile([P, 2, N], I32, name="al8_w", align_bytes=64)
+
+        def second_passes(c, a, n0, w, half, dst, closes=True):
+            codes, scales = h_q[c, a, n0]
             rows = slice(P * half, P * (half + 1))
             al4 = al4_w[:, a, P // 2 * half : P // 2 * (half + 1)].bitcast(FP4X4)
             al8 = al8_w[:, a, rows].bitcast(FP8X4)
-            for tier, lhsT in enumerate((al4, al8)):
+            step = w if w == 512 else P
+            passes = [(0, al4, k, step) for k in range(0, w, step)]
+            passes = [(1, al8, 0, w)] + passes if a == 0 else passes + [(1, al8, 0, w)]
+            for tier, lhsT, k, n in passes:
                 nc.tensor.matmul_mx(
-                    out=dst,
+                    out=dst[:, k : k + n],
                     lhsT=lhsT,
-                    lhsT_scale=al_sc[tier][:, a, :].bitcast(U8)[:, rows],
-                    rhs=codes[:, n0 : n0 + step].bitcast(FP8X4),
-                    rhs_scale=scales[:, n0 : n0 + step],
-                    start=(a == 0 and tier == 0),
-                    stop=(a == 1 and tier == 1),
+                    lhsT_scale=planes[:, a, :].bitcast(U8)[:, J + N * tier + P * half : J + N * tier + P * (half + 1)],
+                    rhs=codes[:, k : k + n].bitcast(FP8X4),
+                    rhs_scale=scales[:, k : k + n],
+                    start=(a == 0 and tier == 1),
+                    stop=(a == 1 and tier == 1 and closes),
                 )
 
         out_v = out.rearrange("(h p) m -> p h m", p=P)
-        sums = {}
 
-        def second_closed(c):
-            w = CHUNKS[c][1]
-            bank = take("y")[:, 0 : 2 * w].rearrange("p (h m) -> p h m", h=2)
+        def add_bias(dst, sums, half, engine):
+            if engine == "scalar":
+                nc.scalar.activation(dst, sums, ACT.Identity, bias=b_t[:, half : half + 1])
+            else:
+                nc.vector.tensor_scalar(dst, sums, b_t[:, half : half + 1], None, ALU.add)
+
+        def store(c, n0, w, sums, engines, res):
+            res = res.rearrange("p (h m) -> p h m", h=2)
             for half in range(2):
-                sums[c, half] = bank[:, half, :]
-                for n0 in range(0, w, P):
-                    for a in range(2):
-                        second_passes(c, a, half, n0, P, bank[:, half, n0 : n0 + P])
+                add_bias(res[:, half, :], sums[half], half, engines[half])
+            m0 = WIDE * c + n0
+            nc.sync.dma_start(out_v[:, :, m0 : m0 + w], res)
 
-        def second_open(c, a):
-            w = CHUNKS[c][1]
+        def second_stage(c, n0, w, sums):
             for half in range(2):
-                if a == 0:
-                    sums[c, half] = take("y")[:, 0:w]
-                second_passes(c, a, half, 0, w, sums[c, half])
+                for a in range(2):
+                    second_passes(c, a, n0, w, half, sums[half])
 
-        def store(c, engines):
-            m0, w = CHUNKS[c]
-            res = work.tile([P, 2, w], F32, name="res", align_bytes=64)
-            for half in range(2):
-                if engines[half] == "scalar":
-                    nc.scalar.activation(res[:, half, :], sums[c, half], ACT.Identity, bias=b_t[:, half : half + 1])
-                else:
-                    nc.vector.tensor_scalar(res[:, half, :], sums[c, half], b_t[:, half : half + 1], None, ALU.add)
-            nc.sync.dma_start(out_v[:, :, m0 : m0 + w], res[:])
+        def one_bank(i, w):
+            return [banks[i][:, 0:w], banks[i][:, w : 2 * w]]
 
-        load_words()
-        pick_scales(0)
-        load_x(2)
-        copy_x(2, 0, "scalar")
+        load_x(0, 0)
+        load_x(0, 1)
+        nc.sync.dma_start(tab_w[:], tab_words[0].rearrange("p t b -> p (t b)").bitcast(I32))
+        load_x(1, 0)
+        for a in range(2):
+            cols = slice(PASS * a, PASS * (a + 1))
+            nc.vector.tensor_copy(picked_sc[:, cols], tab_sc[:].bitcast(U8).indirect(offsets[:, 32 * a : 32 * (a + 1)]))
+            nc.vector.tensor_copy(
+                sorted_sc[:, cols].rearrange("p (t r) -> p r t", t=PACK), picked_sc[:, cols].rearrange("p (r t) -> p r t", t=PACK)
+            )
+        for q in range(4):
+            nc.sync.dma_start(planes[32 * q : 32 * q + 4, :, :], sorted_sc[8 * q : 8 * (q + 1), :].bitcast(I32))
+        load_x(1, 1)
+        load_x(2, 0)
+        load_x(2, 1)
+        load_x(3, 0)
+        load_x(3, 1)
+        nc.sync.dma_start(al4_w[:], al4_words.bitcast(I32).rearrange("a p n -> p a n"))
+        nc.sync.dma_start(al8_w[:], al8_words.rearrange("a p n i -> a p (n i)").bitcast(I32).rearrange("a p n -> p a n"))
+
+        scalar, vector = nc.scalar.copy, nc.vector.tensor_copy
+        for g in range(2):
+            copy_x(0, g, scalar)
+            quant_x(0, g, 0, PIECE)
+        for i in range(8):
+            nc.tensor.matmul_mx(
+                out=banks[D_BANKS + 2][:, 0:PIECE],
+                lhsT=x_codes[0][:, 0:P].bitcast(FP8X4),
+                lhsT_scale=x_scales[0][:, 0:P],
+                rhs=x_codes[0][:, 0:PIECE].bitcast(FP8X4),
+                rhs_scale=x_scales[0][:, 0:PIECE],
+                start=True,
+                stop=True,
+            )
         pick_words(0)
-        load_x(1)
-        copy_x(0, 1, "scalar")
-        load_x(0)
-        load_x(3)
-        sort_scales(0)
-        pick_scales(1)
-        quant_x(0, 1)
-        copy_x(0, 0, "scalar")
-        load_x(5)
-        copy_x(2, 1, "scalar")
-        sort_scales(1)
-        load_x(4)
-        quant_x(0, 0)
+        part_words(0, "v_w0")
+        copy_x(1, 0, scalar)
+        first_stage(0, 0, 0, PIECE)
         pick_words(1)
-        load_cb(nc.scalar)
-        copy_x(1, 1, "vector")
-        load_al4()
-        quant_x(1, 1)
-        move_planes(nc.scalar)
-        load_cw(nc.scalar)
-        part_words(0)
-        part_words(1)
-        first_stage(0, 1)
-        load_b(nc.sync)
-        load_al_sc(0, nc.sync)
-        copy_x(1, 0, "scalar")
-        quant_x(2, 1)
-        quant_x(2, 0)
-        first_stage(0, 0)
-        copy_x(3, 1, "vector")
-        spread_cw()
-        weigh(0, 1)
-        quant_x(1, 0)
-        quant_x(3, 1)
-        quant_h(0, 1)
-        first_stage(1, 0)
-        weigh(0, 0)
-        quant_h(0, 0)
-        copy_x(3, 0, "vector")
-        quant_x(3, 0)
-        first_stage(1, 1)
-        first_stage(2, 0)
-        load_al_sc(1, nc.sync)
-        weigh(1, 0)
-        weigh(1, 1)
-        load_al8()
-        quant_h(1, 0)
-        first_stage(2, 1)
-        first_stage(3, 0)
-        quant_h(1, 1)
-        weigh(2, 0)
-        second_closed(0)
-        quant_h(2, 0)
-        first_stage(3, 1)
-        weigh(2, 1)
-        quant_h(2, 1)
-        second_open(1, 0)
-        weigh(3, 0)
-        quant_h(3, 0)
-        second_open(1, 1)
-        weigh(3, 1)
-        store(0, ("scalar", "scalar"))
-        quant_h(3, 1)
-        store(1, ("scalar", "scalar"))
-        second_closed(2)
-        second_open(3, 0)
-        second_open(3, 1)
-        store(3, ("vector", "scalar"))
-        store(2, ("scalar", "scalar"))
+        quant_x(0, 0, PIECE, PIECE)
+        copy_x(1, 1, vector)
+        quant_x(0, 1, PIECE, PIECE)
+        part_words(1, "raw11")
+        copy_x(2, 0, scalar)
+        early = x_grouped[0][:, PACK * WIDE : 2 * PACK * WIDE]
+        weigh(early[:, 0 : PACK * PIECE], 0, 0, 0, PIECE)
+        first_stage(0, 0, PIECE, PIECE)
+        copy_x(2, 1, vector)
+        copy_x(3, 0, scalar)
+        weigh(early[:, PACK * PIECE : PACK * WIDE], 0, 0, PIECE, PIECE)
+        first_stage(0, 1, 0, WIDE)
+        copy_x(3, 1, vector)
+        quant_x(1, 0, 0, WIDE)
+        quant_x(1, 1, 0, WIDE)
+        quant_h(early, [(0, 0, 0, WIDE)])
+        first_stage(1, 0, 0, WIDE)
+        grouped = x_grouped[1][:, PACK * WIDE : 2 * PACK * WIDE]
+        weigh(grouped, 0, 1, 0, WIDE)
+        first_stage(1, 1, 0, WIDE)
+        late = staging("h_late", WIDE)[:]
+        quant_h(grouped, [(0, 1, 0, WIDE)])
+        weigh(late, 1, 0, 0, WIDE)
+        sums = [banks[D_BANKS][:], banks[D_BANKS + 1][:]]
+        second_stage(0, 0, WIDE, sums)
+        store(0, 0, WIDE, sums, ("scalar", "scalar"), sig_tiles[0, 1][:, 0 : 2 * WIDE])
+        ranges = ((0, PIECE), (PIECE, P), (PIECE + P, P))
+        ends = [late[:, 0 : PACK * PIECE], late[:, 0 : PACK * P], late[:, PACK * PIECE : PACK * (PIECE + P)]]
+        quant_h(late, [(1, 0, 0, WIDE)])
+        weigh(ends[0], 1, 1, *ranges[0])
+        end_sums = [[banks[D_BANKS + 2][:, 0:PIECE], banks[D_BANKS + 3][:, 0:PIECE]], [banks[D_BANKS][:, 0:PIECE], banks[D_BANKS + 1][:, 0:PIECE]]]
+        for i in range(2):
+            for half in range(2):
+                second_passes(1, 0, PIECE * i, PIECE, half, end_sums[i][half])
+        quant_h(ends[0], [(1, 1) + ranges[0]])
+        weigh(ends[1], 1, 1, *ranges[1])
+        weigh(ends[2], 1, 1, *ranges[2])
+        quant_h(ends[1], [(1, 1) + ranges[1]])
+        quant_h(ends[2], [(1, 1) + ranges[2]])
+        res = [keep.tile([P, 2 * PIECE], F32, name="res%d" % i, align_bytes=64) for i in range(2)]
+        for half in range(2):
+            second_passes(1, 1, 0, PIECE, half, end_sums[0][half])
+        store(1, 0, PIECE, end_sums[0], ("scalar", "scalar"), res[0][:])
+        for k in range(0, PIECE, P):
+            for half in range(2):
+                second_passes(1, 1, PIECE + k, P, half, end_sums[1][half][:, k : k + P], k > 0)
+        store(1, PIECE, PIECE, end_sums[1], ("vector", "scalar"), res[1][:])

@@ -22,7 +22,7 @@ PASS = P * PACK
 RUN = 4
 WIDE = 512
 PIECE = 256
-D_BANKS = 4
+D_BANKS = 5
 
 
 def tile_list_kernl_sigm_res_bias_kernel(
@@ -79,8 +79,8 @@ def tile_list_kernl_sigm_res_bias_kernel(
         sigs = {key: tile[:].rearrange("p (t m) -> p t m", t=PACK) for key, tile in sig_tiles.items()}
 
         def load_x(s, g):
-            if g == 0 and s >= 2:
-                raw = sig_tiles[0, 1][:, PACK * PIECE * (s - 2) : PACK * PIECE * (s - 1)]
+            if (s, g) == (2, 0):
+                raw = sig_tiles[0, 1][:, 0 : PACK * PIECE]
             else:
                 raw = keep.tile([P, PACK * PIECE], F32, name="x_raw%d%d" % (s, g), tag="raw%d%d" % (s, g), align_bytes=64)[:]
             x_raw[s, g] = raw.rearrange("p (t m) -> p t m", t=PACK)
@@ -97,8 +97,8 @@ def tile_list_kernl_sigm_res_bias_kernel(
         def part_words(a, tag):
             v_w[a] = keep.tile([P, 2, PASS], U16, name="v_w%d" % a, tag=tag, align_bytes=64)
             nc.vector.tensor_copy(
-                v_w[a][:].rearrange("p g (t r) -> p g r t", t=PACK),
-                picked_w[:].bitcast(U16).rearrange("p (r t g) -> p g r t", t=PACK, g=2),
+                v_w[a][:].rearrange("p g (t b i) -> p g b t i", t=PACK, i=4),
+                picked_w[:].bitcast(U16).rearrange("p (b i t g) -> p g b t i", t=PACK, g=2, i=4),
             )
 
         x_codes = [keep.tile([P, 2 * WIDE], U32, name="x_codes%d" % c, align_bytes=64) for c in range(2)]
@@ -224,7 +224,8 @@ def tile_list_kernl_sigm_res_bias_kernel(
             cols = slice(PASS * a, PASS * (a + 1))
             nc.vector.tensor_copy(picked_sc[:, cols], tab_sc[:].bitcast(U8).indirect(offsets[:, 32 * a : 32 * (a + 1)]))
             nc.vector.tensor_copy(
-                sorted_sc[:, cols].rearrange("p (t r) -> p r t", t=PACK), picked_sc[:, cols].rearrange("p (r t) -> p r t", t=PACK)
+                sorted_sc[:, cols].rearrange("p (t b i) -> p b t i", t=PACK, i=16),
+                picked_sc[:, cols].rearrange("p (b i t) -> p b t i", t=PACK, i=16),
             )
         for q in range(4):
             nc.sync.dma_start(planes[32 * q : 32 * q + 4, :, :], sorted_sc[8 * q : 8 * (q + 1), :].bitcast(I32))
@@ -264,41 +265,47 @@ def tile_list_kernl_sigm_res_bias_kernel(
         weigh(early[:, 0 : PACK * PIECE], 0, 0, 0, PIECE)
         first_stage(0, 0, PIECE, PIECE)
         copy_x(2, 1, vector)
-        copy_x(3, 0, scalar)
         weigh(early[:, PACK * PIECE : PACK * WIDE], 0, 0, PIECE, PIECE)
         first_stage(0, 1, 0, WIDE)
-        copy_x(3, 1, vector)
-        quant_x(1, 0, 0, WIDE)
-        quant_x(1, 1, 0, WIDE)
+        for g in range(2):
+            quant_x(1, g, 0, PIECE)
         quant_h(early, [(0, 0, 0, WIDE)])
-        first_stage(1, 0, 0, WIDE)
-        grouped = x_grouped[1][:, PACK * WIDE : 2 * PACK * WIDE]
+        first_stage(1, 0, 0, PIECE)
+        grouped = staging("h_wide", WIDE)[:]
         weigh(grouped, 0, 1, 0, WIDE)
-        first_stage(1, 1, 0, WIDE)
-        late = staging("h_late", WIDE)[:]
+        copy_x(3, 0, scalar)
+        copy_x(3, 1, scalar)
+        first_stage(1, 1, 0, PIECE)
+        for g in range(2):
+            quant_x(1, g, PIECE, PIECE)
         quant_h(grouped, [(0, 1, 0, WIDE)])
-        weigh(late, 1, 0, 0, WIDE)
-        sums = [banks[D_BANKS][:], banks[D_BANKS + 1][:]]
-        second_stage(0, 0, WIDE, sums)
-        store(0, 0, WIDE, sums, ("scalar", "scalar"), sig_tiles[0, 1][:, 0 : 2 * WIDE])
-        ranges = ((0, PIECE), (PIECE, P), (PIECE + P, P))
-        ends = [late[:, 0 : PACK * PIECE], late[:, 0 : PACK * P], late[:, PACK * PIECE : PACK * (PIECE + P)]]
-        quant_h(late, [(1, 0, 0, WIDE)])
-        weigh(ends[0], 1, 1, *ranges[0])
-        end_sums = [[banks[D_BANKS + 2][:, 0:PIECE], banks[D_BANKS + 3][:, 0:PIECE]], [banks[D_BANKS][:, 0:PIECE], banks[D_BANKS + 1][:, 0:PIECE]]]
-        for i in range(2):
-            for half in range(2):
-                second_passes(1, 0, PIECE * i, PIECE, half, end_sums[i][half])
-        quant_h(ends[0], [(1, 1) + ranges[0]])
-        weigh(ends[1], 1, 1, *ranges[1])
-        weigh(ends[2], 1, 1, *ranges[2])
-        quant_h(ends[1], [(1, 1) + ranges[1]])
-        quant_h(ends[2], [(1, 1) + ranges[2]])
-        res = [keep.tile([P, 2 * PIECE], F32, name="res%d" % i, align_bytes=64) for i in range(2)]
+        third = staging("h_third", 2 * PIECE)[:]
+        for a in range(2):
+            weigh(third[:, PACK * PIECE * a : PACK * PIECE * (a + 1)], 1, a, 0, PIECE)
+        first_stage(1, 0, PIECE, PIECE)
+        wide_sums = [banks[D_BANKS][:], banks[D_BANKS + 1][:]]
+        second_stage(0, 0, WIDE, wide_sums)
+        quant_h(third, [(1, a, 0, PIECE) for a in range(2)])
+        fourth = staging("h_fourth", PIECE)[:]
+        weigh(fourth, 1, 0, PIECE, PIECE)
+        first_stage(1, 1, PIECE, PIECE)
+        ends = [staging("h_end%d" % i, P)[:] for i in range(2)]
+        weigh(ends[0], 1, 1, PIECE, P)
+        quant_h(fourth, [(1, 0, PIECE, PIECE)])
+        second_stage(1, 0, PIECE, one_bank(D_BANKS + 2, PIECE))
+        res = [keep.tile([P, 2 * w], F32, name="res%d" % i, align_bytes=64) for i, w in enumerate((WIDE, PIECE, P, P))]
+        store(0, 0, WIDE, wide_sums, ("scalar", "scalar"), res[0][:])
+        store(1, 0, PIECE, one_bank(D_BANKS + 2, PIECE), ("scalar", "scalar"), res[1][:])
+        end_sums = [next_bank()[:, 0:P], next_bank()[:, 0:P]]
         for half in range(2):
-            second_passes(1, 1, 0, PIECE, half, end_sums[0][half])
-        store(1, 0, PIECE, end_sums[0], ("scalar", "scalar"), res[0][:])
-        for k in range(0, PIECE, P):
-            for half in range(2):
-                second_passes(1, 1, PIECE + k, P, half, end_sums[1][half][:, k : k + P], k > 0)
-        store(1, PIECE, PIECE, end_sums[1], ("vector", "scalar"), res[1][:])
+            second_passes(1, 0, PIECE + P, P, half, end_sums[half])
+        weigh(ends[1], 1, 1, PIECE + P, P)
+        quant_h(ends[0], [(1, 1, PIECE, P)])
+        quant_h(ends[1], [(1, 1, PIECE + P, P)])
+        bank = next_bank()
+        sums = [bank[:, 0:P], bank[:, P : 2 * P]]
+        second_stage(1, PIECE, P, sums)
+        store(1, PIECE, P, sums, ("scalar", "scalar"), res[2][:])
+        for half in range(2):
+            second_passes(1, 1, PIECE + P, P, half, end_sums[half])
+        store(1, PIECE + P, P, end_sums, ("vector", "scalar"), res[3][:])

@@ -42,7 +42,7 @@ def tile_list_kernl_sigm_res_bias_kernel(
         nc.vector.memset(tab_sc[64:128, :], 0)
 
         planes = keep.tile([P, 2, (J + 2 * N) // 4], I32, name="planes", align_bytes=64)
-        nc.vector.memset(planes[:], 0)
+        nc.gpsimd.memset(planes[:], 0)
 
         warm_in = keep.tile([P, 1], F32, name="warm_in")
         nc.vector.memset(warm_in[:], 0.0)
@@ -51,17 +51,14 @@ def tile_list_kernl_sigm_res_bias_kernel(
 
         cb_t = keep.tile([P, 2, PACK], F32, name="cb_t")
         cw_t = keep.tile([P, 2, PACK], F32, name="cw_t")
-        nc.gpsimd.dma_start(cb_t[:], cb.rearrange("(a p t) -> p a t", a=2, t=PACK))
-        nc.gpsimd.dma_start(cw_t[:], cw.rearrange("(a p t) -> p a t", a=2, t=PACK))
-        b_t = keep.tile([P, 2], F32, name="b_t")
-        with nc.allow_non_contiguous_dma(reason="one bias value a partition"):
-            nc.gpsimd.dma_start(b_t[:], b.rearrange("(h p) -> p h", p=P))
         sorted_sc = keep.tile([P, J + 2 * N], U8, name="sorted_sc", align_bytes=64)
         for tier, src in enumerate((al4_scales, al8_scales)):
             cols = slice(J + N * tier, J + N * (tier + 1))
             nc.scalar.dma_start(sorted_sc[0:32, cols].bitcast(I32), src.bitcast(I32).rearrange("g r n -> r g n"))
+        nc.scalar.dma_start(cb_t[:], cb.rearrange("(a p t) -> p a t", a=2, t=PACK))
+        nc.scalar.dma_start(cw_t[:], cw.rearrange("(a p t) -> p a t", a=2, t=PACK))
         cw_runs = keep.tile([P, 2, PACK, RUN], F32, name="cw_runs", align_bytes=64)
-        nc.gpsimd.tensor_copy(cw_runs[:], cw_t[:].rearrange("p a (t i) -> p a t i", i=1).to_broadcast([P, 2, PACK, RUN]))
+        nc.scalar.copy(cw_runs[:], cw_t[:].rearrange("p a (t i) -> p a t i", i=1).to_broadcast([P, 2, PACK, RUN]))
 
         banks = [psum.tile([P, 512], F32, name="bank%d" % i) for i in range(8)]
         turns = {"d": 0}
@@ -171,6 +168,7 @@ def tile_list_kernl_sigm_res_bias_kernel(
                     h_q[c, a, n0 + k] = (codes[:, at + k : at + w], scales[:, at + k : at + w])
                 at = at + w
 
+        b_t = keep.tile([P, 2], F32, name="b_t")
         al4_w = keep.tile([P, 2, N // 2], I32, name="al4_w", align_bytes=64)
         al8_w = keep.tile([P, 2, N], I32, name="al8_w", align_bytes=64)
 
@@ -217,8 +215,8 @@ def tile_list_kernl_sigm_res_bias_kernel(
             return [banks[i][:, 0:w], banks[i][:, w : 2 * w]]
 
         load_x(0, 0)
-        load_x(0, 1)
         nc.sync.dma_start(tab_w[:], tab_words[0].rearrange("p t b -> p (t b)").bitcast(I32))
+        load_x(0, 1)
         load_x(1, 0)
         for a in range(2):
             cols = slice(PASS * a, PASS * (a + 1))
@@ -236,6 +234,8 @@ def tile_list_kernl_sigm_res_bias_kernel(
         load_x(3, 1)
         nc.sync.dma_start(al4_w[:], al4_words.bitcast(I32).rearrange("a p n -> p a n"))
         nc.sync.dma_start(al8_w[:], al8_words.rearrange("a p n i -> a p (n i)").bitcast(I32).rearrange("a p n -> p a n"))
+        with nc.allow_non_contiguous_dma(reason="one bias value a partition"):
+            nc.sync.dma_start(b_t[:], b.rearrange("(h p) -> p h", p=P))
 
         scalar, vector = nc.scalar.copy, nc.vector.tensor_copy
         for g in range(2):

@@ -1,6 +1,7 @@
 from contextlib import ExitStack
 
 import concourse.mybir as mybir
+from concourse.masks import make_identity
 
 K, M, N, J, T = 1024, 1024, 256, 1024, 2048
 FLOPS = 2 * K * J * M + 2 * 2 * J * N * M
@@ -22,7 +23,10 @@ PASS = P * PACK
 RUN = 4
 WIDE = 512
 PIECE = 256
-D_BANKS = 5
+D_BANKS = 7
+ON_GPSIMD = 4
+SHARES = 16
+WARM_EARLY, WARM_LATE = 5, 4
 
 
 def tile_list_kernl_sigm_res_bias_kernel(
@@ -33,162 +37,181 @@ def tile_list_kernl_sigm_res_bias_kernel(
         keep = ctx.enter_context(tc.tile_pool(name="keep", bufs=1))
         psum = ctx.enter_context(tc.psum_pool(name="psum", bufs=1))
 
+        def tile(name, shape, dtype, tag=None):
+            return keep.tile([P] + shape, dtype, name=name, tag=tag or name, align_bytes=64)
+
         offsets = keep.tile([P, J // 16], U16, name="offsets")
         nc.sync.dma_start(offsets[:], offs)
 
-        tab_sc = keep.tile([P, T // 4], I32, name="tab_sc", align_bytes=64)
-        nc.scalar.dma_start(tab_sc[0:32, :], tab_scales.bitcast(I32).rearrange("g r n -> r g n"))
+        tab_sc = tile("tab_sc", [T // 4], I32)
+        nc.sync.dma_start(tab_sc[0:32, :], tab_scales.bitcast(I32).rearrange("g r n -> r g n"))
         nc.vector.memset(tab_sc[32:64, :], 0)
         nc.vector.memset(tab_sc[64:128, :], 0)
 
-        planes = keep.tile([P, 2, (J + 2 * N) // 4], I32, name="planes", align_bytes=64)
-        nc.gpsimd.memset(planes[:], 0)
+        planes = [tile("planes%d" % a, [2, columns // 4], I32) for a, columns in enumerate((PASS, PASS + 2 * N))]
+        for plane in planes:
+            nc.gpsimd.memset(plane[:], 0)
 
         warm_in = keep.tile([P, 1], F32, name="warm_in")
         nc.vector.memset(warm_in[:], 0.0)
         warm_out = keep.tile([P, 1], F32, name="warm_out")
         nc.scalar.activation(warm_out[:], warm_in[:], ACT.Sigmoid)
 
-        cb_t = keep.tile([P, 2, PACK], F32, name="cb_t")
-        cw_t = keep.tile([P, 2, PACK], F32, name="cw_t")
-        sorted_sc = keep.tile([P, J + 2 * N], U8, name="sorted_sc", align_bytes=64)
+        sorted_sc = tile("sorted_sc", [J + 2 * N], U8)
         for tier, src in enumerate((al4_scales, al8_scales)):
             cols = slice(J + N * tier, J + N * (tier + 1))
             nc.scalar.dma_start(sorted_sc[0:32, cols].bitcast(I32), src.bitcast(I32).rearrange("g r n -> r g n"))
-        nc.scalar.dma_start(cb_t[:], cb.rearrange("(a p t) -> p a t", a=2, t=PACK))
+
+        cb_t = keep.tile([P, 2, PACK], F32, name="cb_t")
+        cw_t = keep.tile([P, 2, PACK], F32, name="cw_t")
         nc.scalar.dma_start(cw_t[:], cw.rearrange("(a p t) -> p a t", a=2, t=PACK))
-        cw_runs = keep.tile([P, 2, PACK, RUN], F32, name="cw_runs", align_bytes=64)
-        nc.scalar.copy(cw_runs[:], cw_t[:].rearrange("p a (t i) -> p a t i", i=1).to_broadcast([P, 2, PACK, RUN]))
 
         banks = [psum.tile([P, 512], F32, name="bank%d" % i) for i in range(8)]
+        identity = tile("identity", [P], F32)
+        make_identity(nc, identity[:])
+        cw_runs = tile("cw_runs", [P], F32)
+        nc.gpsimd.memset(cw_runs[:], 0.0)
         turns = {"d": 0}
 
         def next_bank():
             turns["d"] = turns["d"] + 1
             return banks[(turns["d"] - 1) % D_BANKS]
 
-        tab_w = keep.tile([P, T], I32, name="tab_w", align_bytes=64)
+        tab_w = tile("tab_w", [T], I32)
         x_raw = {}
-
-        sig_tiles = {
-            (c, a): keep.tile([P, PACK * WIDE], F32, name="sig%d%d" % (c, a), align_bytes=64) for c in range(2) for a in range(2)
-        }
-        sigs = {key: tile[:].rearrange("p (t m) -> p t m", t=PACK) for key, tile in sig_tiles.items()}
+        sigs = {}
 
         def load_x(s, g):
-            if (s, g) == (2, 0):
-                raw = sig_tiles[0, 1][:, 0 : PACK * PIECE]
-            else:
-                raw = keep.tile([P, PACK * PIECE], F32, name="x_raw%d%d" % (s, g), tag="raw%d%d" % (s, g), align_bytes=64)[:]
-            x_raw[s, g] = raw.rearrange("p (t m) -> p t m", t=PACK)
+            x_raw[s, g] = tile("x_raw%d%d" % (s, g), [PACK, PIECE], F32)
             rows = x[PASS * g : PASS * (g + 1), PIECE * s : PIECE * (s + 1)]
-            nc.sync.dma_start(x_raw[s, g], rows.rearrange("(p t) m -> p t m", t=PACK))
+            nc.sync.dma_start(x_raw[s, g][:], rows.rearrange("(p t) m -> p t m", t=PACK))
 
-        picked_sc = keep.tile([P, J], U8, name="picked_sc", align_bytes=64)
-        picked_w = keep.tile([P, PASS], U32, name="picked_w", align_bytes=64)
-        v_w = {}
+        picked_sc = tile("picked_sc", [J], U8)
+        picked_w = {}
+        v_w = [tile("v_w%d" % a, [2, PASS], U16) for a in range(2)]
 
-        def pick_words(a):
-            nc.vector.tensor_copy(picked_w[:], tab_w[:].bitcast(U32).indirect(offsets[:, 32 * a : 32 * (a + 1)]))
+        def pick_words(first, count, tag=None):
+            picked_w[first] = tile("picked_w%d" % first, [count], U32, tag)
+            entries = offsets[:, first // 16 : (first + count) // 16]
+            nc.vector.tensor_copy(picked_w[first][:], tab_w[:].bitcast(U32).indirect(entries))
 
-        def part_words(a, tag):
-            v_w[a] = keep.tile([P, 2, PASS], U16, name="v_w%d" % a, tag=tag, align_bytes=64)
+        def part_words(first, count):
+            a, at = divmod(first, PASS)
+            by_slot = v_w[a][:].rearrange("p g (t r) -> p g t r", t=PACK)[:, :, :, at // PACK : (at + count) // PACK]
             nc.vector.tensor_copy(
-                v_w[a][:].rearrange("p g (t b i) -> p g b t i", t=PACK, i=4),
-                picked_w[:].bitcast(U16).rearrange("p (b i t g) -> p g b t i", t=PACK, g=2, i=4),
+                by_slot.rearrange("p g t (b i) -> p g b t i", i=4),
+                picked_w[first][:].bitcast(U16).rearrange("p (b i t g) -> p g b t i", t=PACK, g=2, i=4),
             )
 
-        x_codes = [keep.tile([P, 2 * WIDE], U32, name="x_codes%d" % c, align_bytes=64) for c in range(2)]
-        x_scales = [keep.tile([P, 2 * WIDE], U8, name="x_scales%d" % c, align_bytes=64) for c in range(2)]
-        x_grouped = [keep.tile([P, 2 * PACK * WIDE], BF16, name="x_grouped%d" % c, align_bytes=64) for c in range(2)]
+        x_staged = {}
+        x_q = {}
 
-        def x_staged(c, g, n0, w):
-            at = WIDE * g + n0
-            if c == 0:
-                at = PIECE * g if n0 == 0 else PIECE * (3 - g)
-            return x_grouped[c][:, PACK * at : PACK * (at + w)]
-
-        def copy_x(s, g, copy):
+        def copy_x(s, g, copy, tag=None):
+            x_staged[s, g] = tile("x_staged%d%d" % (s, g), [PACK * PIECE], BF16, tag)
             copy(
-                x_staged(s // 2, g, PIECE * (s % 2), PIECE).rearrange("p (c i t) -> p c t i", i=RUN, t=PACK),
-                x_raw[s, g].rearrange("p t (c i) -> p c t i", i=RUN),
+                x_staged[s, g][:].rearrange("p (c i t) -> p c t i", i=RUN, t=PACK),
+                x_raw[s, g][:].rearrange("p t (c i) -> p c t i", i=RUN),
             )
 
-        def quantise(name, grouped, width):
-            codes = keep.tile([P, width], U32, name=name + "_codes", align_bytes=64)
-            scales = keep.tile([P, width], U8, name=name + "_scales", align_bytes=64)
-            nc.vector.quantize_mx(out=codes[:].bitcast(FP8X4), scales=scales[:], in_=grouped)
-            return codes, scales
+        x_codes = {(c, g): tile("x_codes%d%d" % (c, g), [WIDE], U32) for c in range(2) for g in range(2)}
+        x_scales = {(c, g): tile("x_scales%d%d" % (c, g), [WIDE], U8) for c in range(2) for g in range(2)}
 
-        def quant_x(c, g, n0, w):
-            at = WIDE * g + n0
-            nc.vector.quantize_mx(
-                out=x_codes[c][:, at : at + w].bitcast(FP8X4),
-                scales=x_scales[c][:, at : at + w],
-                in_=x_staged(c, g, n0, w),
-            )
+        def quant_x(s, g):
+            cols = slice(PIECE * (s % 2), PIECE * (s % 2 + 1))
+            x_q[s, g] = (x_codes[s // 2, g][:, cols], x_scales[s // 2, g][:, cols])
+            nc.vector.quantize_mx(out=x_q[s, g][0].bitcast(FP8X4), scales=x_q[s, g][1], in_=x_staged[s, g][:])
 
-        def first_stage(c, a, n0, w):
+        def sigmoid(m0, a, t, sums):
+            nc.scalar.activation(sigs[m0, a][:, t, :], sums, ACT.Sigmoid, bias=cb_t[:, a, t : t + 1])
+
+        def first_stage(m0, w, a, tag=None, cuts=()):
+            parts = list(zip((0,) + cuts, cuts + (w,)))
+            for first, last in parts:
+                sigs[m0 + first, a] = tile("sig%d_%d" % (m0 + first, a), [PACK, last - first], F32, tag)
+            c, n0 = divmod(m0, WIDE)
             step = w if w == WIDE else P
-            for t in range(PACK):
-                bank = next_bank()
+            sums = [next_bank() for t in range(PACK)]
+            for t, bank in enumerate(sums):
                 for k in range(0, w, step):
                     for g in range(2):
-                        at = WIDE * g + n0 + k
                         nc.tensor.matmul_mx(
                             out=bank[:, k : k + step],
                             lhsT=v_w[a][:, g, P * t : P * (t + 1)].bitcast(FP4X4),
-                            lhsT_scale=planes[:, g, :].bitcast(U8)[:, PASS * a + P * t : PASS * a + P * (t + 1)],
-                            rhs=x_codes[c][:, at : at + step].bitcast(FP8X4),
-                            rhs_scale=x_scales[c][:, at : at + step],
+                            lhsT_scale=planes[a][:, g, :].bitcast(U8)[:, P * t : P * (t + 1)],
+                            rhs=x_codes[c, g][:, n0 + k : n0 + k + step].bitcast(FP8X4),
+                            rhs_scale=x_scales[c, g][:, n0 + k : n0 + k + step],
                             start=(g == 0),
                             stop=(g == 1),
                         )
-                nc.scalar.activation(sigs[c, a][:, t, n0 : n0 + w], bank[:, 0:w], ACT.Sigmoid, bias=cb_t[:, a, t : t + 1])
+                sigmoid(m0, a, t, bank[:, 0 : parts[0][1]])
+            for first, last in parts[1:]:
+                for t, bank in enumerate(sums):
+                    sigmoid(m0 + first, a, t, bank[:, first:last])
 
-        h_q = {}
+        h_staged = {}
+        h_codes = {(c, a): tile("h_codes%d%d" % (c, a), [WIDE], U32) for c in range(2) for a in range(2)}
+        h_scales = {(c, a): tile("h_scales%d%d" % (c, a), [WIDE], U8) for c in range(2) for a in range(2)}
 
-        def weigh(dst, c, a, n0, w):
-            nc.vector.tensor_tensor(
-                dst.rearrange("p (c i t) -> p c t i", i=RUN, t=PACK),
-                sigs[c, a][:, :, n0 : n0 + w].rearrange("p t (c i) -> p c t i", i=RUN),
-                cw_runs[:, a : a + 1, :, :].to_broadcast([P, w // RUN, PACK, RUN]),
-                ALU.mult,
+        def spread_cw():
+            runs = cw_runs[:, 0 : 2 * PACK * RUN].rearrange("p (a t i) -> p a t i", a=2, t=PACK)
+            nc.gpsimd.tensor_copy(runs, cw_t[:].rearrange("p a (t i) -> p a t i", i=1).to_broadcast([P, 2, PACK, RUN]))
+            turned = tile("cw_turned", [P], F32)
+            nc.tensor.transpose(banks[D_BANKS][:, P : 2 * P], cw_runs[:], identity[:])
+            nc.scalar.copy(turned[:], banks[D_BANKS][:, P : 2 * P])
+            nc.tensor.transpose(banks[D_BANKS][:, 0:P], turned[:], identity[:])
+
+        def weigh_woven(m0, a, n0, w, tag=None):
+            h_staged[m0 + n0, a] = tile("h_staged%d_%d" % (m0 + n0, a), [PACK * w], BF16, tag)
+            cut = w - w * ON_GPSIMD // SHARES
+            for engine, factors, first, last in ((nc.vector, banks[D_BANKS], 0, cut), (nc.gpsimd, cw_runs, cut, w)):
+                runs = factors[:, PACK * RUN * a : PACK * RUN * (a + 1)].rearrange("p (c t i) -> p c t i", c=1, t=PACK)
+                engine.tensor_tensor(
+                    h_staged[m0 + n0, a][:, PACK * first : PACK * last].rearrange("p (c i t) -> p c t i", i=RUN, t=PACK),
+                    sigs[m0, a][:, :, n0 + first : n0 + last].rearrange("p t (c i) -> p c t i", i=RUN),
+                    runs.to_broadcast([P, (last - first) // RUN, PACK, RUN]),
+                    ALU.mult,
+                )
+
+        def quant_h(m0, w, a):
+            c, n0 = divmod(m0, WIDE)
+            nc.vector.quantize_mx(
+                out=h_codes[c, a][:, n0 : n0 + w].bitcast(FP8X4),
+                scales=h_scales[c, a][:, n0 : n0 + w],
+                in_=h_staged[m0, a][:],
             )
 
-        def staging(name, columns):
-            return keep.tile([P, PACK * columns], BF16, name=name, align_bytes=64)
-
-        def quant_h(grouped, parts):
-            c, a, n0, w = parts[0]
-            codes, scales = quantise("h%d%d%d" % (c, a, n0), grouped[:], sum(part[3] for part in parts))
-            at = 0
-            for c, a, n0, w in parts:
-                for k in range(0, w, P):
-                    h_q[c, a, n0 + k] = (codes[:, at + k : at + w], scales[:, at + k : at + w])
-                at = at + w
+        def warm_up(lhsT, passes):
+            codes, scales = x_q[0, 0]
+            for i in range(passes):
+                nc.tensor.matmul_mx(
+                    out=banks[D_BANKS - 1][:, 0:PIECE],
+                    lhsT=lhsT,
+                    lhsT_scale=scales[:, 0:P],
+                    rhs=codes.bitcast(FP8X4),
+                    rhs_scale=scales,
+                    start=True,
+                    stop=True,
+                )
 
         b_t = keep.tile([P, 2], F32, name="b_t")
-        al4_w = keep.tile([P, 2, N // 2], I32, name="al4_w", align_bytes=64)
-        al8_w = keep.tile([P, 2, N], I32, name="al8_w", align_bytes=64)
+        al4_w = tile("al4_w", [2, N // 2], I32)
+        al8_w = tile("al8_w", [2, N], I32)
 
-        def second_passes(c, a, n0, w, half, dst, closes=True):
-            codes, scales = h_q[c, a, n0]
-            rows = slice(P * half, P * (half + 1))
+        def second_passes(c, at, w, a, half, dst, opens, closes):
+            codes, scales = h_codes[c, a], h_scales[c, a]
             al4 = al4_w[:, a, P // 2 * half : P // 2 * (half + 1)].bitcast(FP4X4)
-            al8 = al8_w[:, a, rows].bitcast(FP8X4)
-            step = w if w == 512 else P
-            passes = [(0, al4, k, step) for k in range(0, w, step)]
-            passes = [(1, al8, 0, w)] + passes if a == 0 else passes + [(1, al8, 0, w)]
-            for tier, lhsT, k, n in passes:
+            al8 = al8_w[:, a, P * half : P * (half + 1)].bitcast(FP8X4)
+            step = w if w == WIDE else P
+            passes = [(1, al8, 0, w)] + [(0, al4, k, step) for k in range(0, w, step)]
+            for i, (tier, lhsT, k, n) in enumerate(passes):
                 nc.tensor.matmul_mx(
                     out=dst[:, k : k + n],
                     lhsT=lhsT,
-                    lhsT_scale=planes[:, a, :].bitcast(U8)[:, J + N * tier + P * half : J + N * tier + P * (half + 1)],
-                    rhs=codes[:, k : k + n].bitcast(FP8X4),
-                    rhs_scale=scales[:, k : k + n],
-                    start=(a == 0 and tier == 1),
-                    stop=(a == 1 and tier == 1 and closes),
+                    lhsT_scale=planes[1][:, a, :].bitcast(U8)[:, PASS + N * tier + P * half : PASS + N * tier + P * (half + 1)],
+                    rhs=codes[:, at + k : at + k + n].bitcast(FP8X4),
+                    rhs_scale=scales[:, at + k : at + k + n],
+                    start=(opens and i == 0),
+                    stop=(closes and i == len(passes) - 1),
                 )
 
         out_v = out.rearrange("(h p) m -> p h m", p=P)
@@ -199,25 +222,19 @@ def tile_list_kernl_sigm_res_bias_kernel(
             else:
                 nc.vector.tensor_scalar(dst, sums, b_t[:, half : half + 1], None, ALU.add)
 
-        def store(c, n0, w, sums, engines, res):
-            res = res.rearrange("p (h m) -> p h m", h=2)
+        def store(m0, w, sums, engines, tag=None):
+            res = tile("res%d" % m0, [2, w], F32, tag)
             for half in range(2):
                 add_bias(res[:, half, :], sums[half], half, engines[half])
-            m0 = WIDE * c + n0
-            nc.sync.dma_start(out_v[:, :, m0 : m0 + w], res)
-
-        def second_stage(c, n0, w, sums):
-            for half in range(2):
-                for a in range(2):
-                    second_passes(c, a, n0, w, half, sums[half])
-
-        def one_bank(i, w):
-            return [banks[i][:, 0:w], banks[i][:, w : 2 * w]]
+            nc.sync.dma_start(out_v[:, :, m0 : m0 + w], res[:])
 
         load_x(0, 0)
         nc.sync.dma_start(tab_w[:], tab_words[0].rearrange("p t b -> p (t b)").bitcast(I32))
         load_x(0, 1)
-        load_x(1, 0)
+
+        scalar, vector = nc.scalar.copy, nc.vector.tensor_copy
+        copy_x(0, 0, scalar)
+        spread_cw()
         for a in range(2):
             cols = slice(PASS * a, PASS * (a + 1))
             nc.vector.tensor_copy(picked_sc[:, cols], tab_sc[:].bitcast(U8).indirect(offsets[:, 32 * a : 32 * (a + 1)]))
@@ -225,87 +242,89 @@ def tile_list_kernl_sigm_res_bias_kernel(
                 sorted_sc[:, cols].rearrange("p (t b i) -> p b t i", t=PACK, i=16),
                 picked_sc[:, cols].rearrange("p (b i t) -> p b t i", t=PACK, i=16),
             )
-        for q in range(4):
-            nc.sync.dma_start(planes[32 * q : 32 * q + 4, :, :], sorted_sc[8 * q : 8 * (q + 1), :].bitcast(I32))
+        quant_x(0, 0)
+        warm_up(x_q[0, 0][0][:, 0:P].bitcast(FP8X4), WARM_EARLY)
+
+        def move_scales(plane, first, last):
+            for q in (0, 2, 1, 3):
+                rows = sorted_sc[8 * q : 8 * (q + 1), first:last].bitcast(I32)
+                nc.sync.dma_start(plane[32 * q : 32 * q + 4, :, :], rows)
+
+        load_x(1, 0)
+        move_scales(planes[0], 0, PASS)
+        nc.sync.dma_start(cb_t[:], cb.rearrange("(a p t) -> p a t", a=2, t=PACK))
         load_x(1, 1)
         load_x(2, 0)
-        load_x(2, 1)
+        move_scales(planes[1], PASS, J + 2 * N)
         load_x(3, 0)
+        load_x(2, 1)
         load_x(3, 1)
-        nc.sync.dma_start(al4_w[:], al4_words.bitcast(I32).rearrange("a p n -> p a n"))
         nc.sync.dma_start(al8_w[:], al8_words.rearrange("a p n i -> a p (n i)").bitcast(I32).rearrange("a p n -> p a n"))
+        nc.sync.dma_start(al4_w[:], al4_words.bitcast(I32).rearrange("a p n -> p a n"))
         with nc.allow_non_contiguous_dma(reason="one bias value a partition"):
             nc.sync.dma_start(b_t[:], b.rearrange("(h p) -> p h", p=P))
 
-        scalar, vector = nc.scalar.copy, nc.vector.tensor_copy
-        for g in range(2):
-            copy_x(0, g, scalar)
-            quant_x(0, g, 0, PIECE)
-        for i in range(8):
-            nc.tensor.matmul_mx(
-                out=banks[D_BANKS + 2][:, 0:PIECE],
-                lhsT=x_codes[0][:, 0:P].bitcast(FP8X4),
-                lhsT_scale=x_scales[0][:, 0:P],
-                rhs=x_codes[0][:, 0:PIECE].bitcast(FP8X4),
-                rhs_scale=x_scales[0][:, 0:PIECE],
-                start=True,
-                stop=True,
-            )
-        pick_words(0)
-        part_words(0, "v_w0")
+        pick_words(0, PASS)
+        part_words(0, PASS)
+        pick_words(PASS, PASS // 2)
+        warm_up(picked_w[0][:].bitcast(U16)[:, 0:P].bitcast(FP4X4), WARM_LATE)
+        copy_x(0, 1, scalar)
+        quant_x(0, 1)
+        pick_words(PASS + PASS // 2, PASS // 2, "x_staged01")
         copy_x(1, 0, scalar)
-        first_stage(0, 0, 0, PIECE)
-        pick_words(1)
-        quant_x(0, 0, PIECE, PIECE)
+        part_words(PASS, PASS // 2)
+        quant_x(1, 0)
+        part_words(PASS + PASS // 2, PASS // 2)
+        first_stage(0, PIECE, 0, "x_raw10")
         copy_x(1, 1, vector)
-        quant_x(0, 1, PIECE, PIECE)
-        part_words(1, "raw11")
+        quant_x(1, 1)
+        weigh_woven(0, 0, 0, PIECE, "x_staged11")
         copy_x(2, 0, scalar)
-        early = x_grouped[0][:, PACK * WIDE : 2 * PACK * WIDE]
-        weigh(early[:, 0 : PACK * PIECE], 0, 0, 0, PIECE)
-        first_stage(0, 0, PIECE, PIECE)
-        copy_x(2, 1, vector)
-        weigh(early[:, PACK * PIECE : PACK * WIDE], 0, 0, PIECE, PIECE)
-        first_stage(0, 1, 0, WIDE)
-        for g in range(2):
-            quant_x(1, g, 0, PIECE)
-        quant_h(early, [(0, 0, 0, WIDE)])
-        first_stage(1, 0, 0, PIECE)
-        grouped = staging("h_wide", WIDE)[:]
-        weigh(grouped, 0, 1, 0, WIDE)
-        copy_x(3, 0, scalar)
-        copy_x(3, 1, scalar)
-        first_stage(1, 1, 0, PIECE)
-        for g in range(2):
-            quant_x(1, g, PIECE, PIECE)
-        quant_h(grouped, [(0, 1, 0, WIDE)])
-        third = staging("h_third", 2 * PIECE)[:]
+        quant_x(2, 0)
+        first_stage(PIECE, PIECE, 0, "x_raw20")
+        quant_h(0, PIECE, 0)
+        copy_x(3, 0, vector)
+        quant_x(3, 0)
+        weigh_woven(PIECE, 0, 0, PIECE, "x_raw30")
+        copy_x(2, 1, scalar)
+        copy_x(3, 1, vector)
+        quant_x(2, 1)
+        first_stage(0, WIDE, 1, "x_raw21")
+        quant_h(PIECE, PIECE, 0)
+        quant_x(3, 1)
+        first_stage(WIDE, WIDE, 0)
+        weigh_woven(0, 1, 0, WIDE, "x_staged31")
+        quant_h(0, WIDE, 1)
+        first_stage(WIDE, WIDE, 1, cuts=(PIECE, PIECE + P))
+        weigh_woven(WIDE, 0, 0, WIDE)
+        quant_h(WIDE, WIDE, 0)
+        weigh_woven(WIDE, 1, 0, PIECE)
+        quant_h(WIDE, PIECE, 1)
+        for i in range(2):
+            weigh_woven(WIDE + PIECE + P * i, 1, 0, P)
+            quant_h(WIDE + PIECE + P * i, P, 1)
+
+        first_sums = [next_bank()[:] for half in range(2)]
         for a in range(2):
-            weigh(third[:, PACK * PIECE * a : PACK * PIECE * (a + 1)], 1, a, 0, PIECE)
-        first_stage(1, 0, PIECE, PIECE)
-        wide_sums = [banks[D_BANKS][:], banks[D_BANKS + 1][:]]
-        second_stage(0, 0, WIDE, wide_sums)
-        quant_h(third, [(1, a, 0, PIECE) for a in range(2)])
-        fourth = staging("h_fourth", PIECE)[:]
-        weigh(fourth, 1, 0, PIECE, PIECE)
-        first_stage(1, 1, PIECE, PIECE)
-        ends = [staging("h_end%d" % i, P)[:] for i in range(2)]
-        weigh(ends[0], 1, 1, PIECE, P)
-        quant_h(fourth, [(1, 0, PIECE, PIECE)])
-        second_stage(1, 0, PIECE, one_bank(D_BANKS + 2, PIECE))
-        res = [keep.tile([P, 2 * w], F32, name="res%d" % i, align_bytes=64) for i, w in enumerate((WIDE, PIECE, P, P))]
-        store(0, 0, WIDE, wide_sums, ("scalar", "scalar"), res[0][:])
-        store(1, 0, PIECE, one_bank(D_BANKS + 2, PIECE), ("scalar", "scalar"), res[1][:])
-        end_sums = [next_bank()[:, 0:P], next_bank()[:, 0:P]]
-        for half in range(2):
-            second_passes(1, 0, PIECE + P, P, half, end_sums[half])
-        weigh(ends[1], 1, 1, PIECE + P, P)
-        quant_h(ends[0], [(1, 1, PIECE, P)])
-        quant_h(ends[1], [(1, 1, PIECE + P, P)])
+            for half in range(2):
+                second_passes(0, 0, WIDE, a, half, first_sums[half], a == 0, a == 1)
         bank = next_bank()
-        sums = [bank[:, 0:P], bank[:, P : 2 * P]]
-        second_stage(1, PIECE, P, sums)
-        store(1, PIECE, P, sums, ("scalar", "scalar"), res[2][:])
+        third_sums = [bank[:, 0:PIECE], bank[:, PIECE : 2 * PIECE]]
+        bank = next_bank()
+        end_sums = [[bank[:, 0:P], bank[:, P : 2 * P]], [next_bank()[:, 0:P] for half in range(2)]]
         for half in range(2):
-            second_passes(1, 1, PIECE + P, P, half, end_sums[half])
-        store(1, PIECE + P, P, end_sums, ("vector", "scalar"), res[3][:])
+            second_passes(1, 0, PIECE, 0, half, third_sums[half], half == 0, False)
+        store(0, WIDE, first_sums, ("scalar", "scalar"), "sig512_1")
+        for half in range(2):
+            second_passes(1, 0, PIECE, 1, half, third_sums[half], False, half == 1)
+        for half in range(2):
+            second_passes(1, PIECE, P, 0, half, end_sums[0][half], half == 0, False)
+        for half in range(2):
+            second_passes(1, PIECE + P, P, 0, half, end_sums[1][half], True, False)
+        store(WIDE, PIECE, third_sums, ("scalar", "scalar"))
+        for half in range(2):
+            second_passes(1, PIECE, P, 1, half, end_sums[0][half], False, half == 1)
+        store(WIDE + PIECE, P, end_sums[0], ("vector", "vector"))
+        for half in range(2):
+            second_passes(1, PIECE + P, P, 1, half, end_sums[1][half], False, True)
+        store(WIDE + PIECE + P, P, end_sums[1], ("vector", "scalar"))

@@ -1,7 +1,6 @@
 from contextlib import ExitStack
 
 import concourse.mybir as mybir
-from concourse.masks import make_identity
 
 K, M, N, J, T = 1024, 1024, 256, 1024, 2048
 FLOPS = 2 * K * J * M + 2 * 2 * J * N * M
@@ -43,13 +42,29 @@ def tile_list_kernl_sigm_res_bias_kernel(
         offsets = keep.tile([P, J // 16], U16, name="offsets")
         nc.sync.dma_start(offsets[:], offs)
 
+        cw_t = keep.tile([P, 2, PACK], F32, name="cw_t")
+        nc.scalar.dma_start(cw_t[:], cw.rearrange("(a p t) -> p a t", a=2, t=PACK))
+
+        identity = tile("identity", [P], F32)
+        ones = tile("ones", [P], F32)
+        nc.vector.memset(ones[:], 1.0)
+        count = tile("count", [P], F32)
+        nc.vector.tensor_tensor_scan(count[:], ones[:], ones[:], 0.0, ALU.mult, ALU.add)
+        count_turned = tile("count_turned", [P], F32)
+        nc.vector.transpose(count_turned[:], count[:])
+        for q in range(4):
+            rows = slice(32 * q, 32 * (q + 1))
+            nc.vector.tensor_scalar(identity[rows, :], count[rows, :], count_turned[rows, 32 * q : 32 * q + 1], None, ALU.is_equal)
+
         tab_sc = tile("tab_sc", [T // 4], I32)
         nc.sync.dma_start(tab_sc[0:32, :], tab_scales.bitcast(I32).rearrange("g r n -> r g n"))
         nc.vector.memset(tab_sc[32:64, :], 0)
         nc.vector.memset(tab_sc[64:128, :], 0)
 
-        planes = [tile("planes%d" % a, [2, columns // 4], I32) for a, columns in enumerate((PASS, PASS + 2 * N))]
-        for plane in planes:
+        cw_runs = tile("cw_runs", [P], F32)
+        planes = [tile("planes%d" % a, [2, PASS // 4], I32) for a in range(2)]
+        al_planes = [tile("al_planes%d" % tier, [2, N // 4], I32) for tier in range(2)]
+        for plane in planes + al_planes:
             nc.gpsimd.memset(plane[:], 0)
 
         warm_in = keep.tile([P, 1], F32, name="warm_in")
@@ -57,20 +72,11 @@ def tile_list_kernl_sigm_res_bias_kernel(
         warm_out = keep.tile([P, 1], F32, name="warm_out")
         nc.scalar.activation(warm_out[:], warm_in[:], ACT.Sigmoid)
 
-        sorted_sc = tile("sorted_sc", [J + 2 * N], U8)
-        for tier, src in enumerate((al4_scales, al8_scales)):
-            cols = slice(J + N * tier, J + N * (tier + 1))
-            nc.scalar.dma_start(sorted_sc[0:32, cols].bitcast(I32), src.bitcast(I32).rearrange("g r n -> r g n"))
+        sorted_sc = tile("sorted_sc", [J], U8)
 
         cb_t = keep.tile([P, 2, PACK], F32, name="cb_t")
-        cw_t = keep.tile([P, 2, PACK], F32, name="cw_t")
-        nc.scalar.dma_start(cw_t[:], cw.rearrange("(a p t) -> p a t", a=2, t=PACK))
 
         banks = [psum.tile([P, 512], F32, name="bank%d" % i) for i in range(8)]
-        identity = tile("identity", [P], F32)
-        make_identity(nc, identity[:])
-        cw_runs = tile("cw_runs", [P], F32)
-        nc.gpsimd.memset(cw_runs[:], 0.0)
         turns = {"d": 0}
 
         def next_bank():
@@ -103,13 +109,17 @@ def tile_list_kernl_sigm_res_bias_kernel(
                 picked_w[first][:].bitcast(U16).rearrange("p (b i t g) -> p g b t i", t=PACK, g=2, i=4),
             )
 
-        x_staged = {}
-        x_q = {}
+        x_staged = {(c, g): tile("x_staged%d%d" % (c, g), [2, PACK * PIECE], BF16) for c, g in ((1, 0), (1, 1))}
+        x_first = {}
 
-        def copy_x(s, g, copy, tag=None):
-            x_staged[s, g] = tile("x_staged%d%d" % (s, g), [PACK * PIECE], BF16, tag)
+        def staging(s, g):
+            return x_first[s, g][:] if s < 2 else x_staged[1, g][:, s - 2, :]
+
+        def copy_x(s, g, copy):
+            if s < 2:
+                x_first[s, g] = tile("x_first%d%d" % (s, g), [PACK * PIECE], BF16)
             copy(
-                x_staged[s, g][:].rearrange("p (c i t) -> p c t i", i=RUN, t=PACK),
+                staging(s, g).rearrange("p (c i t) -> p c t i", i=RUN, t=PACK),
                 x_raw[s, g][:].rearrange("p t (c i) -> p c t i", i=RUN),
             )
 
@@ -117,9 +127,14 @@ def tile_list_kernl_sigm_res_bias_kernel(
         x_scales = {(c, g): tile("x_scales%d%d" % (c, g), [WIDE], U8) for c in range(2) for g in range(2)}
 
         def quant_x(s, g):
-            cols = slice(PIECE * (s % 2), PIECE * (s % 2 + 1))
-            x_q[s, g] = (x_codes[s // 2, g][:, cols], x_scales[s // 2, g][:, cols])
-            nc.vector.quantize_mx(out=x_q[s, g][0].bitcast(FP8X4), scales=x_q[s, g][1], in_=x_staged[s, g][:])
+            cols = slice(PIECE * s, PIECE * (s + 1))
+            nc.vector.quantize_mx(
+                out=x_codes[0, g][:, cols].bitcast(FP8X4), scales=x_scales[0, g][:, cols], in_=x_first[s, g][:]
+            )
+
+        def quant_late_x(g):
+            staged = x_staged[1, g][:].rearrange("p s c -> p (s c)")
+            nc.vector.quantize_mx(out=x_codes[1, g][:].bitcast(FP8X4), scales=x_scales[1, g][:], in_=staged)
 
         def sigmoid(m0, a, t, sums):
             nc.scalar.activation(sigs[m0, a][:, t, :], sums, ACT.Sigmoid, bias=cb_t[:, a, t : t + 1])
@@ -127,7 +142,7 @@ def tile_list_kernl_sigm_res_bias_kernel(
         def first_stage(m0, w, a, tag=None, cuts=()):
             parts = list(zip((0,) + cuts, cuts + (w,)))
             for first, last in parts:
-                sigs[m0 + first, a] = tile("sig%d_%d" % (m0 + first, a), [PACK, last - first], F32, tag)
+                sigs[m0 + first, a] = tile("sig%d_%d" % (m0 + first, a), [PACK, last - first], F32, tag if first == 0 else None)
             c, n0 = divmod(m0, WIDE)
             step = w if w == WIDE else P
             sums = [next_bank() for t in range(PACK)]
@@ -148,43 +163,39 @@ def tile_list_kernl_sigm_res_bias_kernel(
                 for t, bank in enumerate(sums):
                     sigmoid(m0 + first, a, t, bank[:, first:last])
 
-        h_staged = {}
-        h_codes = {(c, a): tile("h_codes%d%d" % (c, a), [WIDE], U32) for c in range(2) for a in range(2)}
-        h_scales = {(c, a): tile("h_scales%d%d" % (c, a), [WIDE], U8) for c in range(2) for a in range(2)}
+        h_codes = [tile("h_codes%d" % c, [2 * WIDE], U32) for c in range(2)]
+        h_scales = [tile("h_scales%d" % c, [2 * WIDE], U8) for c in range(2)]
 
         def spread_cw():
-            runs = cw_runs[:, 0 : 2 * PACK * RUN].rearrange("p (a t i) -> p a t i", a=2, t=PACK)
-            nc.gpsimd.tensor_copy(runs, cw_t[:].rearrange("p a (t i) -> p a t i", i=1).to_broadcast([P, 2, PACK, RUN]))
+            runs = cw_runs[:].rearrange("p (r k i) -> p r k i", k=2 * PACK, i=RUN)
+            values = cw_t[:].rearrange("p a (t r i) -> p r (a t) i", r=1, i=1)
+            nc.scalar.copy(runs, values.to_broadcast([P, P // (2 * PACK * RUN), 2 * PACK, RUN]))
             turned = tile("cw_turned", [P], F32)
             nc.tensor.transpose(banks[D_BANKS][:, P : 2 * P], cw_runs[:], identity[:])
             nc.scalar.copy(turned[:], banks[D_BANKS][:, P : 2 * P])
             nc.tensor.transpose(banks[D_BANKS][:, 0:P], turned[:], identity[:])
 
-        def weigh_woven(m0, a, n0, w, tag=None):
-            h_staged[m0 + n0, a] = tile("h_staged%d_%d" % (m0 + n0, a), [PACK * w], BF16, tag)
+        def weigh(m0, w, a, staged):
             cut = w - w * ON_GPSIMD // SHARES
             for engine, factors, first, last in ((nc.vector, banks[D_BANKS], 0, cut), (nc.gpsimd, cw_runs, cut, w)):
                 runs = factors[:, PACK * RUN * a : PACK * RUN * (a + 1)].rearrange("p (c t i) -> p c t i", c=1, t=PACK)
                 engine.tensor_tensor(
-                    h_staged[m0 + n0, a][:, PACK * first : PACK * last].rearrange("p (c i t) -> p c t i", i=RUN, t=PACK),
-                    sigs[m0, a][:, :, n0 + first : n0 + last].rearrange("p t (c i) -> p c t i", i=RUN),
+                    staged[:, PACK * first : PACK * last].rearrange("p (c i t) -> p c t i", i=RUN, t=PACK),
+                    sigs[m0, a][:, :, first:last].rearrange("p t (c i) -> p c t i", i=RUN),
                     runs.to_broadcast([P, (last - first) // RUN, PACK, RUN]),
                     ALU.mult,
                 )
 
-        def quant_h(m0, w, a):
+        def quant_h(m0, w, a, staged):
             c, n0 = divmod(m0, WIDE)
-            nc.vector.quantize_mx(
-                out=h_codes[c, a][:, n0 : n0 + w].bitcast(FP8X4),
-                scales=h_scales[c, a][:, n0 : n0 + w],
-                in_=h_staged[m0, a][:],
-            )
+            cols = slice(WIDE * a + n0, WIDE * a + n0 + w)
+            nc.vector.quantize_mx(out=h_codes[c][:, cols].bitcast(FP8X4), scales=h_scales[c][:, cols], in_=staged)
 
         def warm_up(lhsT, passes):
-            codes, scales = x_q[0, 0]
+            codes, scales = x_codes[0, 0][:, 0:PIECE], x_scales[0, 0][:, 0:PIECE]
             for i in range(passes):
                 nc.tensor.matmul_mx(
-                    out=banks[D_BANKS - 1][:, 0:PIECE],
+                    out=banks[D_BANKS][:, PIECE : 2 * PIECE],
                     lhsT=lhsT,
                     lhsT_scale=scales[:, 0:P],
                     rhs=codes.bitcast(FP8X4),
@@ -198,7 +209,7 @@ def tile_list_kernl_sigm_res_bias_kernel(
         al8_w = tile("al8_w", [2, N], I32)
 
         def second_passes(c, at, w, a, half, dst, opens, closes):
-            codes, scales = h_codes[c, a], h_scales[c, a]
+            codes, scales = h_codes[c][:, WIDE * a : WIDE * (a + 1)], h_scales[c][:, WIDE * a : WIDE * (a + 1)]
             al4 = al4_w[:, a, P // 2 * half : P // 2 * (half + 1)].bitcast(FP4X4)
             al8 = al8_w[:, a, P * half : P * (half + 1)].bitcast(FP8X4)
             step = w if w == WIDE else P
@@ -207,7 +218,7 @@ def tile_list_kernl_sigm_res_bias_kernel(
                 nc.tensor.matmul_mx(
                     out=dst[:, k : k + n],
                     lhsT=lhsT,
-                    lhsT_scale=planes[1][:, a, :].bitcast(U8)[:, PASS + N * tier + P * half : PASS + N * tier + P * (half + 1)],
+                    lhsT_scale=al_planes[tier][:, a, :].bitcast(U8)[:, P * half : P * (half + 1)],
                     rhs=codes[:, at + k : at + k + n].bitcast(FP8X4),
                     rhs_scale=scales[:, at + k : at + k + n],
                     start=(opens and i == 0),
@@ -233,8 +244,8 @@ def tile_list_kernl_sigm_res_bias_kernel(
         load_x(0, 1)
 
         scalar, vector = nc.scalar.copy, nc.vector.tensor_copy
-        copy_x(0, 0, scalar)
         spread_cw()
+        copy_x(0, 0, scalar)
         for a in range(2):
             cols = slice(PASS * a, PASS * (a + 1))
             nc.vector.tensor_copy(picked_sc[:, cols], tab_sc[:].bitcast(U8).indirect(offsets[:, 32 * a : 32 * (a + 1)]))
@@ -243,7 +254,7 @@ def tile_list_kernl_sigm_res_bias_kernel(
                 picked_sc[:, cols].rearrange("p (b i t) -> p b t i", t=PACK, i=16),
             )
         quant_x(0, 0)
-        warm_up(x_q[0, 0][0][:, 0:P].bitcast(FP8X4), WARM_EARLY)
+        warm_up(x_codes[0, 0][:, 0:P].bitcast(FP8X4), WARM_EARLY)
 
         def move_scales(plane, first, last):
             for q in (0, 2, 1, 3):
@@ -255,12 +266,16 @@ def tile_list_kernl_sigm_res_bias_kernel(
         nc.sync.dma_start(cb_t[:], cb.rearrange("(a p t) -> p a t", a=2, t=PACK))
         load_x(1, 1)
         load_x(2, 0)
-        move_scales(planes[1], PASS, J + 2 * N)
+        move_scales(planes[1], PASS, J)
         load_x(3, 0)
         load_x(2, 1)
         load_x(3, 1)
         nc.sync.dma_start(al8_w[:], al8_words.rearrange("a p n i -> a p (n i)").bitcast(I32).rearrange("a p n -> p a n"))
         nc.sync.dma_start(al4_w[:], al4_words.bitcast(I32).rearrange("a p n -> p a n"))
+        for tier, src in enumerate((al4_scales, al8_scales)):
+            for q in (0, 2, 1, 3):
+                rows = src.bitcast(I32)[:, 4 * q : 4 * (q + 1), :].rearrange("a r n -> r a n")
+                nc.sync.dma_start(al_planes[tier][32 * q : 32 * q + 4, :, :], rows)
         with nc.allow_non_contiguous_dma(reason="one bias value a partition"):
             nc.sync.dma_start(b_t[:], b.rearrange("(h p) -> p h", p=P))
 
@@ -270,7 +285,7 @@ def tile_list_kernl_sigm_res_bias_kernel(
         warm_up(picked_w[0][:].bitcast(U16)[:, 0:P].bitcast(FP4X4), WARM_LATE)
         copy_x(0, 1, scalar)
         quant_x(0, 1)
-        pick_words(PASS + PASS // 2, PASS // 2, "x_staged01")
+        pick_words(PASS + PASS // 2, PASS // 2, "x_first01")
         copy_x(1, 0, scalar)
         part_words(PASS, PASS // 2)
         quant_x(1, 0)
@@ -278,31 +293,30 @@ def tile_list_kernl_sigm_res_bias_kernel(
         first_stage(0, PIECE, 0, "x_raw10")
         copy_x(1, 1, vector)
         quant_x(1, 1)
-        weigh_woven(0, 0, 0, PIECE, "x_staged11")
+        h_first = tile("h_first", [PACK * PIECE], BF16, "x_first11")[:]
+        weigh(0, PIECE, 0, h_first)
         copy_x(2, 0, scalar)
-        quant_x(2, 0)
         first_stage(PIECE, PIECE, 0, "x_raw20")
-        quant_h(0, PIECE, 0)
+        quant_h(0, PIECE, 0, h_first)
         copy_x(3, 0, vector)
-        quant_x(3, 0)
-        weigh_woven(PIECE, 0, 0, PIECE, "x_raw30")
+        h_pair = tile("h_pair", [PACK * WIDE], BF16, "x_raw30")[:]
+        weigh(PIECE, PIECE, 0, h_pair[:, 0 : PACK * PIECE])
+        quant_late_x(0)
         copy_x(2, 1, scalar)
-        copy_x(3, 1, vector)
-        quant_x(2, 1)
-        first_stage(0, WIDE, 1, "x_raw21")
-        quant_h(PIECE, PIECE, 0)
-        quant_x(3, 1)
-        first_stage(WIDE, WIDE, 0)
-        weigh_woven(0, 1, 0, WIDE, "x_staged31")
-        quant_h(0, WIDE, 1)
+        copy_x(3, 1, scalar)
+        first_stage(0, WIDE, 1, "x_raw21", cuts=(PIECE,))
+        quant_late_x(1)
+        first_stage(WIDE, WIDE, 0, cuts=(PIECE,))
         first_stage(WIDE, WIDE, 1, cuts=(PIECE, PIECE + P))
-        weigh_woven(WIDE, 0, 0, WIDE)
-        quant_h(WIDE, WIDE, 0)
-        weigh_woven(WIDE, 1, 0, PIECE)
-        quant_h(WIDE, PIECE, 1)
-        for i in range(2):
-            weigh_woven(WIDE + PIECE + P * i, 1, 0, P)
-            quant_h(WIDE + PIECE + P * i, P, 1)
+        weigh(0, PIECE, 1, h_pair[:, PACK * PIECE : PACK * WIDE])
+        waiting = (PIECE, WIDE, 0, h_pair)
+        ranges = [(PIECE, PIECE, 1), (WIDE, PIECE, 0), (WIDE + PIECE, PIECE, 0), (WIDE, PIECE, 1)]
+        for m0, w, a in ranges + [(WIDE + PIECE, P, 1), (WIDE + PIECE + P, P, 1)]:
+            staged = tile("h_staged%d_%d" % (m0, a), [PACK * w], BF16)[:]
+            weigh(m0, w, a, staged)
+            quant_h(*waiting)
+            waiting = (m0, w, a, staged)
+        quant_h(*waiting)
 
         first_sums = [next_bank()[:] for half in range(2)]
         for a in range(2):
@@ -314,13 +328,13 @@ def tile_list_kernl_sigm_res_bias_kernel(
         end_sums = [[bank[:, 0:P], bank[:, P : 2 * P]], [next_bank()[:, 0:P] for half in range(2)]]
         for half in range(2):
             second_passes(1, 0, PIECE, 0, half, third_sums[half], half == 0, False)
-        store(0, WIDE, first_sums, ("scalar", "scalar"), "sig512_1")
-        for half in range(2):
-            second_passes(1, 0, PIECE, 1, half, third_sums[half], False, half == 1)
         for half in range(2):
             second_passes(1, PIECE, P, 0, half, end_sums[0][half], half == 0, False)
         for half in range(2):
             second_passes(1, PIECE + P, P, 0, half, end_sums[1][half], True, False)
+        store(0, WIDE, first_sums, ("scalar", "scalar"), "sig768_0")
+        for half in range(2):
+            second_passes(1, 0, PIECE, 1, half, third_sums[half], False, half == 1)
         store(WIDE, PIECE, third_sums, ("scalar", "scalar"))
         for half in range(2):
             second_passes(1, PIECE, P, 1, half, end_sums[0][half], False, half == 1)

@@ -23,8 +23,19 @@ RUN = 4
 WIDE = 512
 PIECE = 256
 D_BANKS = 7
-ON_GPSIMD = 4
-SHARES = 16
+SIDE = 64
+PLACED = {
+    "x_first11": 0,
+    "h_main0_0": 0,
+    "h_side0_0": 1536,
+    "x_raw30": 2048,
+    "h_main256_0": 2048,
+    "h_side256_0": 3584,
+    "x_staged11": 6144,
+    "h_side0_1": 6144,
+    "h_side512_0": 6144,
+    "h_side512_1": 6144,
+}
 WARM_EARLY, WARM_LATE = 5, 4
 
 
@@ -34,9 +45,12 @@ def tile_list_kernl_sigm_res_bias_kernel(
     nc = tc.nc
     with ExitStack() as ctx:
         keep = ctx.enter_context(tc.tile_pool(name="keep", bufs=1))
+        shared = ctx.enter_context(tc.tile_pool(name="shared", bufs=1))
         psum = ctx.enter_context(tc.psum_pool(name="psum", bufs=1))
 
         def tile(name, shape, dtype, tag=None):
+            if name in PLACED:
+                return shared.tile([P] + shape, dtype, name=name, align_bytes=64, offset=PLACED[name])
             return keep.tile([P] + shape, dtype, name=name, tag=tag or name, align_bytes=64)
 
         offsets = keep.tile([P, J // 16], U16, name="offsets")
@@ -175,21 +189,35 @@ def tile_list_kernl_sigm_res_bias_kernel(
             nc.scalar.copy(turned[:], banks[D_BANKS][:, P : 2 * P])
             nc.tensor.transpose(banks[D_BANKS][:, 0:P], turned[:], identity[:])
 
-        def weigh(m0, w, a, staged):
-            cut = w - w * ON_GPSIMD // SHARES
-            for engine, factors, first, last in ((nc.vector, banks[D_BANKS], 0, cut), (nc.gpsimd, cw_runs, cut, w)):
+        h_parts = {}
+
+        def weigh(m0, w, a, side=SIDE, tag=None):
+            cut = w - side
+            main = tile("h_main%d_%d" % (m0, a), [PACK * cut], BF16)
+            shares = [(nc.vector, banks[D_BANKS], main, 0, cut)]
+            if side:
+                shares.append((nc.gpsimd, cw_runs, tile("h_side%d_%d" % (m0, a), [PACK * side], BF16, tag), cut, w))
+            h_parts[m0, a] = [(staged, first, last) for engine, factors, staged, first, last in shares]
+            for engine, factors, staged, first, last in shares:
                 runs = factors[:, PACK * RUN * a : PACK * RUN * (a + 1)].rearrange("p (c t i) -> p c t i", c=1, t=PACK)
                 engine.tensor_tensor(
-                    staged[:, PACK * first : PACK * last].rearrange("p (c i t) -> p c t i", i=RUN, t=PACK),
+                    staged[:].rearrange("p (c i t) -> p c t i", i=RUN, t=PACK),
                     sigs[m0, a][:, :, first:last].rearrange("p t (c i) -> p c t i", i=RUN),
                     runs.to_broadcast([P, (last - first) // RUN, PACK, RUN]),
                     ALU.mult,
                 )
 
-        def quant_h(m0, w, a, staged):
+        def quant_h(m0, a):
             c, n0 = divmod(m0, WIDE)
-            cols = slice(WIDE * a + n0, WIDE * a + n0 + w)
-            nc.vector.quantize_mx(out=h_codes[c][:, cols].bitcast(FP8X4), scales=h_scales[c][:, cols], in_=staged)
+            for staged, first, last in reversed(h_parts[m0, a]):
+                for k in range(first, last, P):
+                    end = min(k + P, last)
+                    cols = slice(WIDE * a + n0 + k, WIDE * a + n0 + end)
+                    nc.vector.quantize_mx(
+                        out=h_codes[c][:, cols].bitcast(FP8X4),
+                        scales=h_scales[c][:, cols],
+                        in_=staged[:, PACK * (k - first) : PACK * (end - first)],
+                    )
 
         def warm_up(lhsT, passes):
             codes, scales = x_codes[0, 0][:, 0:PIECE], x_scales[0, 0][:, 0:PIECE]
@@ -293,30 +321,30 @@ def tile_list_kernl_sigm_res_bias_kernel(
         first_stage(0, PIECE, 0, "x_raw10")
         copy_x(1, 1, vector)
         quant_x(1, 1)
-        h_first = tile("h_first", [PACK * PIECE], BF16, "x_first11")[:]
-        weigh(0, PIECE, 0, h_first)
+        weigh(0, PIECE, 0)
         copy_x(2, 0, scalar)
         first_stage(PIECE, PIECE, 0, "x_raw20")
-        quant_h(0, PIECE, 0, h_first)
+        quant_h(0, 0)
         copy_x(3, 0, vector)
-        h_pair = tile("h_pair", [PACK * WIDE], BF16, "x_raw30")[:]
-        weigh(PIECE, PIECE, 0, h_pair[:, 0 : PACK * PIECE])
+        weigh(PIECE, PIECE, 0)
         quant_late_x(0)
         copy_x(2, 1, scalar)
         copy_x(3, 1, scalar)
         first_stage(0, WIDE, 1, "x_raw21", cuts=(PIECE,))
+        quant_h(PIECE, 0)
         quant_late_x(1)
         first_stage(WIDE, WIDE, 0, cuts=(PIECE,))
         first_stage(WIDE, WIDE, 1, cuts=(PIECE, PIECE + P))
-        weigh(0, PIECE, 1, h_pair[:, PACK * PIECE : PACK * WIDE])
-        waiting = (PIECE, WIDE, 0, h_pair)
-        ranges = [(PIECE, PIECE, 1), (WIDE, PIECE, 0), (WIDE + PIECE, PIECE, 0), (WIDE, PIECE, 1)]
-        for m0, w, a in ranges + [(WIDE + PIECE, P, 1), (WIDE + PIECE + P, P, 1)]:
-            staged = tile("h_staged%d_%d" % (m0, a), [PACK * w], BF16)[:]
-            weigh(m0, w, a, staged)
-            quant_h(*waiting)
-            waiting = (m0, w, a, staged)
-        quant_h(*waiting)
+        ranges = [(0, 1), (PIECE, 1), (WIDE, 0), (WIDE + PIECE, 0), (WIDE, 1)]
+        for i, (m0, a) in enumerate(ranges):
+            weigh(m0, PIECE, a, tag="side%d" % (i % 2))
+            if i > 0:
+                quant_h(*ranges[i - 1])
+        weigh(WIDE + PIECE, P, 1, side=0)
+        quant_h(*ranges[-1])
+        weigh(WIDE + PIECE + P, P, 1, side=0)
+        for i in range(2):
+            quant_h(WIDE + PIECE + P * i, 1)
 
         first_sums = [next_bank()[:] for half in range(2)]
         for a in range(2):

@@ -1,6 +1,7 @@
 from contextlib import ExitStack
 
 import concourse.mybir as mybir
+from concourse.masks import make_identity
 
 K, M, N, J, T = 1024, 1024, 256, 1024, 2048
 FLOPS = 2 * K * J * M + 2 * 2 * J * N * M
@@ -25,6 +26,10 @@ PIECE = 256
 D_BANKS = 7
 SIDE = 64
 PLACED = {
+    "x_first01": 12288,
+    "picked_w768": 12288,
+    "cw_turned": 14080,
+    "x_first10": 14336,
     "x_first11": 0,
     "h_main0_0": 0,
     "h_side0_0": 1536,
@@ -59,16 +64,13 @@ def tile_list_kernl_sigm_res_bias_kernel(
         cw_t = keep.tile([P, 2, PACK], F32, name="cw_t")
         nc.scalar.dma_start(cw_t[:], cw.rearrange("(a p t) -> p a t", a=2, t=PACK))
 
+        warm_in = keep.tile([P, 1], F32, name="warm_in")
+        nc.vector.memset(warm_in[:], 0.0)
+        warm_out = keep.tile([P, 1], F32, name="warm_out")
+        nc.scalar.activation(warm_out[:], warm_in[:], ACT.Sigmoid)
+
         identity = tile("identity", [P], F32)
-        ones = tile("ones", [P], F32)
-        nc.vector.memset(ones[:], 1.0)
-        count = tile("count", [P], F32)
-        nc.vector.tensor_tensor_scan(count[:], ones[:], ones[:], 0.0, ALU.mult, ALU.add)
-        count_turned = tile("count_turned", [P], F32)
-        nc.vector.transpose(count_turned[:], count[:])
-        for q in range(4):
-            rows = slice(32 * q, 32 * (q + 1))
-            nc.vector.tensor_scalar(identity[rows, :], count[rows, :], count_turned[rows, 32 * q : 32 * q + 1], None, ALU.is_equal)
+        make_identity(nc, identity[:])
 
         tab_sc = tile("tab_sc", [T // 4], I32)
         nc.sync.dma_start(tab_sc[0:32, :], tab_scales.bitcast(I32).rearrange("g r n -> r g n"))
@@ -80,11 +82,6 @@ def tile_list_kernl_sigm_res_bias_kernel(
         al_planes = [tile("al_planes%d" % tier, [2, N // 4], I32) for tier in range(2)]
         for plane in planes + al_planes:
             nc.gpsimd.memset(plane[:], 0)
-
-        warm_in = keep.tile([P, 1], F32, name="warm_in")
-        nc.vector.memset(warm_in[:], 0.0)
-        warm_out = keep.tile([P, 1], F32, name="warm_out")
-        nc.scalar.activation(warm_out[:], warm_in[:], ACT.Sigmoid)
 
         sorted_sc = tile("sorted_sc", [J], U8)
 
@@ -313,7 +310,7 @@ def tile_list_kernl_sigm_res_bias_kernel(
         warm_up(picked_w[0][:].bitcast(U16)[:, 0:P].bitcast(FP4X4), WARM_LATE)
         copy_x(0, 1, scalar)
         quant_x(0, 1)
-        pick_words(PASS + PASS // 2, PASS // 2, "x_first01")
+        pick_words(PASS + PASS // 2, PASS // 2)
         copy_x(1, 0, scalar)
         part_words(PASS, PASS // 2)
         quant_x(1, 0)

@@ -23,8 +23,11 @@ PASS = P * PACK
 RUN = 4
 WIDE = 512
 PIECE = 256
-D_BANKS = 7
+RING = 7
 SIDE = 64
+PORT_ORDER = (0, 2, 1, 3)
+WARM_EARLY, WARM_LATE = 5, 4
+
 PLACED = {
     "x_first01": 12288,
     "picked_w768": 12288,
@@ -36,12 +39,11 @@ PLACED = {
     "x_raw30": 2048,
     "h_main256_0": 2048,
     "h_side256_0": 3584,
-    "x_staged11": 6144,
+    "x_late1": 6144,
     "h_side0_1": 6144,
     "h_side512_0": 6144,
     "h_side512_1": 6144,
 }
-WARM_EARLY, WARM_LATE = 5, 4
 
 
 def tile_list_kernl_sigm_res_bias_kernel(
@@ -78,21 +80,21 @@ def tile_list_kernl_sigm_res_bias_kernel(
         nc.vector.memset(tab_sc[64:128, :], 0)
 
         cw_runs = tile("cw_runs", [P], F32)
-        planes = [tile("planes%d" % a, [2, PASS // 4], I32) for a in range(2)]
-        al_planes = [tile("al_planes%d" % tier, [2, N // 4], I32) for tier in range(2)]
-        for plane in planes + al_planes:
-            nc.gpsimd.memset(plane[:], 0)
+        all_planes = tile("planes", [2, (J + 2 * N) // 4], I32)
+        nc.gpsimd.memset(all_planes[:], 0)
+        planes = [all_planes[:, :, PASS // 4 * a : PASS // 4 * (a + 1)] for a in range(2)]
+        al_planes = [all_planes[:, :, (J + N * tier) // 4 : (J + N * (tier + 1)) // 4] for tier in range(2)]
 
         sorted_sc = tile("sorted_sc", [J], U8)
-
         cb_t = keep.tile([P, 2, PACK], F32, name="cb_t")
 
-        banks = [psum.tile([P, 512], F32, name="bank%d" % i) for i in range(8)]
-        turns = {"d": 0}
+        banks = [psum.tile([P, WIDE], F32, name="bank%d" % i) for i in range(RING + 1)]
+        cw_bank = banks[RING]
+        taken = []
 
         def next_bank():
-            turns["d"] = turns["d"] + 1
-            return banks[(turns["d"] - 1) % D_BANKS]
+            taken.append(banks[len(taken) % RING])
+            return taken[-1]
 
         tab_w = tile("tab_w", [T], I32)
         x_raw = {}
@@ -107,8 +109,8 @@ def tile_list_kernl_sigm_res_bias_kernel(
         picked_w = {}
         v_w = [tile("v_w%d" % a, [2, PASS], U16) for a in range(2)]
 
-        def pick_words(first, count, tag=None):
-            picked_w[first] = tile("picked_w%d" % first, [count], U32, tag)
+        def pick_words(first, count):
+            picked_w[first] = tile("picked_w%d" % first, [count], U32)
             entries = offsets[:, first // 16 : (first + count) // 16]
             nc.vector.tensor_copy(picked_w[first][:], tab_w[:].bitcast(U32).indirect(entries))
 
@@ -120,17 +122,15 @@ def tile_list_kernl_sigm_res_bias_kernel(
                 picked_w[first][:].bitcast(U16).rearrange("p (b i t g) -> p g b t i", t=PACK, g=2, i=4),
             )
 
-        x_staged = {(c, g): tile("x_staged%d%d" % (c, g), [2, PACK * PIECE], BF16) for c, g in ((1, 0), (1, 1))}
+        x_late = [tile("x_late%d" % g, [2, PACK * PIECE], BF16) for g in range(2)]
         x_first = {}
-
-        def staging(s, g):
-            return x_first[s, g][:] if s < 2 else x_staged[1, g][:, s - 2, :]
 
         def copy_x(s, g, copy):
             if s < 2:
                 x_first[s, g] = tile("x_first%d%d" % (s, g), [PACK * PIECE], BF16)
+            staged = x_first[s, g][:] if s < 2 else x_late[g][:, s - 2, :]
             copy(
-                staging(s, g).rearrange("p (c i t) -> p c t i", i=RUN, t=PACK),
+                staged.rearrange("p (c i t) -> p c t i", i=RUN, t=PACK),
                 x_raw[s, g][:].rearrange("p t (c i) -> p c t i", i=RUN),
             )
 
@@ -144,7 +144,7 @@ def tile_list_kernl_sigm_res_bias_kernel(
             )
 
         def quant_late_x(g):
-            staged = x_staged[1, g][:].rearrange("p s c -> p (s c)")
+            staged = x_late[g][:].rearrange("p s c -> p (s c)")
             nc.vector.quantize_mx(out=x_codes[1, g][:].bitcast(FP8X4), scales=x_scales[1, g][:], in_=staged)
 
         def sigmoid(m0, a, t, sums):
@@ -153,7 +153,8 @@ def tile_list_kernl_sigm_res_bias_kernel(
         def first_stage(m0, w, a, tag=None, cuts=()):
             parts = list(zip((0,) + cuts, cuts + (w,)))
             for first, last in parts:
-                sigs[m0 + first, a] = tile("sig%d_%d" % (m0 + first, a), [PACK, last - first], F32, tag if first == 0 else None)
+                name = "sig%d_%d" % (m0 + first, a)
+                sigs[m0 + first, a] = tile(name, [PACK, last - first], F32, tag if first == 0 else None)
             c, n0 = divmod(m0, WIDE)
             step = w if w == WIDE else P
             sums = [next_bank() for t in range(PACK)]
@@ -182,16 +183,16 @@ def tile_list_kernl_sigm_res_bias_kernel(
             values = cw_t[:].rearrange("p a (t r i) -> p r (a t) i", r=1, i=1)
             nc.scalar.copy(runs, values.to_broadcast([P, P // (2 * PACK * RUN), 2 * PACK, RUN]))
             turned = tile("cw_turned", [P], F32)
-            nc.tensor.transpose(banks[D_BANKS][:, P : 2 * P], cw_runs[:], identity[:])
-            nc.scalar.copy(turned[:], banks[D_BANKS][:, P : 2 * P])
-            nc.tensor.transpose(banks[D_BANKS][:, 0:P], turned[:], identity[:])
+            nc.tensor.transpose(cw_bank[:, P : 2 * P], cw_runs[:], identity[:])
+            nc.scalar.copy(turned[:], cw_bank[:, P : 2 * P])
+            nc.tensor.transpose(cw_bank[:, 0:P], turned[:], identity[:])
 
         h_parts = {}
 
         def weigh(m0, w, a, side=SIDE, tag=None):
             cut = w - side
             main = tile("h_main%d_%d" % (m0, a), [PACK * cut], BF16)
-            shares = [(nc.vector, banks[D_BANKS], main, 0, cut)]
+            shares = [(nc.vector, cw_bank, main, 0, cut)]
             if side:
                 shares.append((nc.gpsimd, cw_runs, tile("h_side%d_%d" % (m0, a), [PACK * side], BF16, tag), cut, w))
             h_parts[m0, a] = [(staged, first, last) for engine, factors, staged, first, last in shares]
@@ -220,7 +221,7 @@ def tile_list_kernl_sigm_res_bias_kernel(
             codes, scales = x_codes[0, 0][:, 0:PIECE], x_scales[0, 0][:, 0:PIECE]
             for i in range(passes):
                 nc.tensor.matmul_mx(
-                    out=banks[D_BANKS][:, PIECE : 2 * PIECE],
+                    out=cw_bank[:, PIECE : 2 * PIECE],
                     lhsT=lhsT,
                     lhsT_scale=scales[:, 0:P],
                     rhs=codes.bitcast(FP8X4),
@@ -233,8 +234,9 @@ def tile_list_kernl_sigm_res_bias_kernel(
         al4_w = tile("al4_w", [2, N // 2], I32)
         al8_w = tile("al8_w", [2, N], I32)
 
-        def second_passes(c, at, w, a, half, dst, opens, closes):
-            codes, scales = h_codes[c][:, WIDE * a : WIDE * (a + 1)], h_scales[c][:, WIDE * a : WIDE * (a + 1)]
+        def second_passes(m0, w, a, half, dst, opens, closes):
+            c, n0 = divmod(m0, WIDE)
+            at = WIDE * a + n0
             al4 = al4_w[:, a, P // 2 * half : P // 2 * (half + 1)].bitcast(FP4X4)
             al8 = al8_w[:, a, P * half : P * (half + 1)].bitcast(FP8X4)
             step = w if w == WIDE else P
@@ -244,25 +246,30 @@ def tile_list_kernl_sigm_res_bias_kernel(
                     out=dst[:, k : k + n],
                     lhsT=lhsT,
                     lhsT_scale=al_planes[tier][:, a, :].bitcast(U8)[:, P * half : P * (half + 1)],
-                    rhs=codes[:, at + k : at + k + n].bitcast(FP8X4),
-                    rhs_scale=scales[:, at + k : at + k + n],
+                    rhs=h_codes[c][:, at + k : at + k + n].bitcast(FP8X4),
+                    rhs_scale=h_scales[c][:, at + k : at + k + n],
                     start=(opens and i == 0),
                     stop=(closes and i == len(passes) - 1),
                 )
 
+        def bias_on_scalar(dst, sums, half):
+            nc.scalar.activation(dst, sums, ACT.Identity, bias=b_t[:, half : half + 1])
+
+        def bias_on_vector(dst, sums, half):
+            nc.vector.tensor_scalar(dst, sums, b_t[:, half : half + 1], None, ALU.add)
+
         out_v = out.rearrange("(h p) m -> p h m", p=P)
 
-        def add_bias(dst, sums, half, engine):
-            if engine == "scalar":
-                nc.scalar.activation(dst, sums, ACT.Identity, bias=b_t[:, half : half + 1])
-            else:
-                nc.vector.tensor_scalar(dst, sums, b_t[:, half : half + 1], None, ALU.add)
-
-        def store(m0, w, sums, engines, tag=None):
-            res = tile("res%d" % m0, [2, w], F32, tag)
+        def store(m0, w, sums, adders):
+            res = tile("res%d" % m0, [2, w], F32)
             for half in range(2):
-                add_bias(res[:, half, :], sums[half], half, engines[half])
+                adders[half](res[:, half, :], sums[half], half)
             nc.sync.dma_start(out_v[:, :, m0 : m0 + w], res[:])
+
+        def move_scales(a):
+            for q in PORT_ORDER:
+                rows = sorted_sc[8 * q : 8 * (q + 1), PASS * a : PASS * (a + 1)].bitcast(I32)
+                nc.sync.dma_start(planes[a][32 * q : 32 * q + 4, :, :], rows)
 
         load_x(0, 0)
         nc.sync.dma_start(tab_w[:], tab_words[0].rearrange("p t b -> p (t b)").bitcast(I32))
@@ -281,40 +288,37 @@ def tile_list_kernl_sigm_res_bias_kernel(
         quant_x(0, 0)
         warm_up(x_codes[0, 0][:, 0:P].bitcast(FP8X4), WARM_EARLY)
 
-        def move_scales(plane, first, last):
-            for q in (0, 2, 1, 3):
-                rows = sorted_sc[8 * q : 8 * (q + 1), first:last].bitcast(I32)
-                nc.sync.dma_start(plane[32 * q : 32 * q + 4, :, :], rows)
-
         load_x(1, 0)
-        move_scales(planes[0], 0, PASS)
+        move_scales(0)
         nc.sync.dma_start(cb_t[:], cb.rearrange("(a p t) -> p a t", a=2, t=PACK))
         load_x(1, 1)
         load_x(2, 0)
-        move_scales(planes[1], PASS, J)
+        move_scales(1)
         load_x(3, 0)
         load_x(2, 1)
         load_x(3, 1)
         nc.sync.dma_start(al8_w[:], al8_words.rearrange("a p n i -> a p (n i)").bitcast(I32).rearrange("a p n -> p a n"))
         nc.sync.dma_start(al4_w[:], al4_words.bitcast(I32).rearrange("a p n -> p a n"))
         for tier, src in enumerate((al4_scales, al8_scales)):
-            for q in (0, 2, 1, 3):
+            for q in PORT_ORDER:
                 rows = src.bitcast(I32)[:, 4 * q : 4 * (q + 1), :].rearrange("a r n -> r a n")
                 nc.sync.dma_start(al_planes[tier][32 * q : 32 * q + 4, :, :], rows)
         with nc.allow_non_contiguous_dma(reason="one bias value a partition"):
             nc.sync.dma_start(b_t[:], b.rearrange("(h p) -> p h", p=P))
 
+        quarter = PASS // 2
         pick_words(0, PASS)
         part_words(0, PASS)
-        pick_words(PASS, PASS // 2)
+        pick_words(PASS, quarter)
         warm_up(picked_w[0][:].bitcast(U16)[:, 0:P].bitcast(FP4X4), WARM_LATE)
         copy_x(0, 1, scalar)
         quant_x(0, 1)
-        pick_words(PASS + PASS // 2, PASS // 2)
+        pick_words(PASS + quarter, quarter)
         copy_x(1, 0, scalar)
-        part_words(PASS, PASS // 2)
+        part_words(PASS, quarter)
         quant_x(1, 0)
-        part_words(PASS + PASS // 2, PASS // 2)
+        part_words(PASS + quarter, quarter)
+
         first_stage(0, PIECE, 0, "x_raw10")
         copy_x(1, 1, vector)
         quant_x(1, 1)
@@ -327,43 +331,48 @@ def tile_list_kernl_sigm_res_bias_kernel(
         quant_late_x(0)
         copy_x(2, 1, scalar)
         copy_x(3, 1, scalar)
+
         first_stage(0, WIDE, 1, "x_raw21", cuts=(PIECE,))
         quant_h(PIECE, 0)
         quant_late_x(1)
         first_stage(WIDE, WIDE, 0, cuts=(PIECE,))
         first_stage(WIDE, WIDE, 1, cuts=(PIECE, PIECE + P))
-        ranges = [(0, 1), (PIECE, 1), (WIDE, 0), (WIDE + PIECE, 0), (WIDE, 1)]
-        for i, (m0, a) in enumerate(ranges):
-            weigh(m0, PIECE, a, tag="side%d" % (i % 2))
+        steps = [(0, 1), (PIECE, 1), (WIDE, 0), (WIDE + PIECE, 0), (WIDE, 1)]
+        for i, (m0, a) in enumerate(steps):
+            weigh(m0, PIECE, a, tag="odd_side")
             if i > 0:
-                quant_h(*ranges[i - 1])
-        weigh(WIDE + PIECE, P, 1, side=0)
-        quant_h(*ranges[-1])
-        weigh(WIDE + PIECE + P, P, 1, side=0)
-        for i in range(2):
-            quant_h(WIDE + PIECE + P * i, 1)
+                quant_h(*steps[i - 1])
 
-        first_sums = [next_bank()[:] for half in range(2)]
-        for a in range(2):
-            for half in range(2):
-                second_passes(0, 0, WIDE, a, half, first_sums[half], a == 0, a == 1)
-        bank = next_bank()
-        third_sums = [bank[:, 0:PIECE], bank[:, PIECE : 2 * PIECE]]
+        for half in range(2):
+            sums = next_bank()[:]
+            for a in range(2):
+                second_passes(0, WIDE, a, half, sums, a == 0, a == 1)
+            res = tile("res_first%d" % half, [WIDE], F32)
+            bias_on_scalar(res[:], sums, half)
+            nc.sync.dma_start(out[P * half : P * (half + 1), 0:WIDE], res[:])
+
+        ends = [WIDE + PIECE, WIDE + PIECE + P]
+        weigh(ends[0], P, 1, side=0)
+        quant_h(*steps[-1])
+        weigh(ends[1], P, 1, side=0)
+        for m0 in ends:
+            quant_h(m0, 1)
+
+        third_sums = [next_bank()[:, 0:PIECE] for half in range(2)]
         bank = next_bank()
         end_sums = [[bank[:, 0:P], bank[:, P : 2 * P]], [next_bank()[:, 0:P] for half in range(2)]]
         for half in range(2):
-            second_passes(1, 0, PIECE, 0, half, third_sums[half], half == 0, False)
+            second_passes(WIDE, PIECE, 0, half, third_sums[half], True, False)
         for half in range(2):
-            second_passes(1, PIECE, P, 0, half, end_sums[0][half], half == 0, False)
+            second_passes(ends[0], P, 0, half, end_sums[0][half], half == 0, False)
         for half in range(2):
-            second_passes(1, PIECE + P, P, 0, half, end_sums[1][half], True, False)
-        store(0, WIDE, first_sums, ("scalar", "scalar"), "sig768_0")
+            second_passes(ends[1], P, 0, half, end_sums[1][half], True, False)
         for half in range(2):
-            second_passes(1, 0, PIECE, 1, half, third_sums[half], False, half == 1)
-        store(WIDE, PIECE, third_sums, ("scalar", "scalar"))
+            second_passes(WIDE, PIECE, 1, half, third_sums[half], False, True)
+        store(WIDE, PIECE, third_sums, (bias_on_scalar, bias_on_vector))
         for half in range(2):
-            second_passes(1, PIECE, P, 1, half, end_sums[0][half], False, half == 1)
-        store(WIDE + PIECE, P, end_sums[0], ("vector", "vector"))
+            second_passes(ends[0], P, 1, half, end_sums[0][half], False, half == 1)
+        store(ends[0], P, end_sums[0], (bias_on_scalar, bias_on_scalar))
         for half in range(2):
-            second_passes(1, PIECE + P, P, 1, half, end_sums[1][half], False, True)
-        store(WIDE + PIECE + P, P, end_sums[1], ("vector", "scalar"))
+            second_passes(ends[1], P, 1, half, end_sums[1][half], False, True)
+        store(ends[1], P, end_sums[1], (bias_on_vector, bias_on_scalar))

@@ -85,7 +85,6 @@ def tile_list_kernl_sigm_res_bias_kernel(
         planes = [all_planes[:, :, PASS // 4 * a : PASS // 4 * (a + 1)] for a in range(2)]
         al_planes = [all_planes[:, :, (J + N * tier) // 4 : (J + N * (tier + 1)) // 4] for tier in range(2)]
 
-        sorted_sc = tile("sorted_sc", [J], U8)
         cb_t = keep.tile([P, 2, PACK], F32, name="cb_t")
 
         banks = [psum.tile([P, WIDE], F32, name="bank%d" % i) for i in range(RING + 1)]
@@ -156,7 +155,7 @@ def tile_list_kernl_sigm_res_bias_kernel(
                 name = "sig%d_%d" % (m0 + first, a)
                 sigs[m0 + first, a] = tile(name, [PACK, last - first], F32, tag if first == 0 else None)
             c, n0 = divmod(m0, WIDE)
-            step = w if w == WIDE else P
+            step = w
             sums = [next_bank() for t in range(PACK)]
             for t, bank in enumerate(sums):
                 for k in range(0, w, step):
@@ -239,7 +238,7 @@ def tile_list_kernl_sigm_res_bias_kernel(
             at = WIDE * a + n0
             al4 = al4_w[:, a, P // 2 * half : P // 2 * (half + 1)].bitcast(FP4X4)
             al8 = al8_w[:, a, P * half : P * (half + 1)].bitcast(FP8X4)
-            step = w if w == WIDE else P
+            step = w
             passes = [(1, al8, 0, w)] + [(0, al4, k, step) for k in range(0, w, step)]
             for i, (tier, lhsT, k, n) in enumerate(passes):
                 nc.tensor.matmul_mx(
@@ -268,7 +267,7 @@ def tile_list_kernl_sigm_res_bias_kernel(
 
         def move_scales(a):
             for q in PORT_ORDER:
-                rows = sorted_sc[8 * q : 8 * (q + 1), PASS * a : PASS * (a + 1)].bitcast(I32)
+                rows = picked_sc[8 * q : 8 * (q + 1), PASS * a : PASS * (a + 1)].bitcast(I32)
                 nc.sync.dma_start(planes[a][32 * q : 32 * q + 4, :, :], rows)
 
         load_x(0, 0)
@@ -280,10 +279,9 @@ def tile_list_kernl_sigm_res_bias_kernel(
         copy_x(0, 0, scalar)
         for a in range(2):
             cols = slice(PASS * a, PASS * (a + 1))
-            nc.vector.tensor_copy(picked_sc[:, cols], tab_sc[:].bitcast(U8).indirect(offsets[:, 32 * a : 32 * (a + 1)]))
             nc.vector.tensor_copy(
-                sorted_sc[:, cols].rearrange("p (t b i) -> p b t i", t=PACK, i=16),
-                picked_sc[:, cols].rearrange("p (b i t) -> p b t i", t=PACK, i=16),
+                picked_sc[:, cols].rearrange("p (t r) -> p r t", t=PACK),
+                tab_sc[:].bitcast(U8).indirect(offsets[:, 32 * a : 32 * (a + 1)]),
             )
         quant_x(0, 0)
         warm_up(x_codes[0, 0][:, 0:P].bitcast(FP8X4), WARM_EARLY)

@@ -25,6 +25,7 @@ WIDE = 512
 PIECE = 256
 RING = 7
 SIDE = 64
+ROOM = PACK * PIECE // 2 - 32
 PORT_ORDER = (0, 2, 1, 3)
 WARM_EARLY, WARM_LATE = 5, 4
 
@@ -34,15 +35,11 @@ PLACED = {
     "cw_turned": 14080,
     "x_first10": 14336,
     "x_first11": 0,
-    "h_main0_0": 0,
-    "h_side0_0": 1536,
+    "h0_0": 0,
     "x_raw30": 2048,
-    "h_main256_0": 2048,
-    "h_side256_0": 3584,
+    "h256_0": 2048,
     "x_late1": 6144,
-    "h_side0_1": 6144,
-    "h_side512_0": 6144,
-    "h_side512_1": 6144,
+    "h0_1": 6144,
 }
 
 
@@ -98,6 +95,7 @@ def tile_list_kernl_sigm_res_bias_kernel(
         tab_w = tile("tab_w", [T], I32)
         x_raw = {}
         sigs = {}
+        ahead = {}
 
         def load_x(s, g):
             x_raw[s, g] = tile("x_raw%d%d" % (s, g), [PACK, PIECE], F32)
@@ -153,7 +151,9 @@ def tile_list_kernl_sigm_res_bias_kernel(
             parts = list(zip((0,) + cuts, cuts + (w,)))
             for first, last in parts:
                 name = "sig%d_%d" % (m0 + first, a)
-                sigs[m0 + first, a] = tile(name, [PACK, last - first], F32, tag if first == 0 else None)
+                both = tile(name, [ROOM + PACK * (last - first)], F32, tag if first == 0 else None)
+                sigs[m0 + first, a] = both[:, ROOM:].rearrange("p (t m) -> p t m", t=PACK)
+                ahead[m0 + first, a] = both[:, 0 : PACK * PIECE // 2].bitcast(BF16)
             c, n0 = divmod(m0, WIDE)
             step = w
             sums = [next_bank() for t in range(PACK)]
@@ -190,15 +190,15 @@ def tile_list_kernl_sigm_res_bias_kernel(
 
         def weigh(m0, w, a, side=SIDE, tag=None):
             cut = w - side
-            main = tile("h_main%d_%d" % (m0, a), [PACK * cut], BF16)
-            shares = [(nc.vector, cw_bank, main, 0, cut)]
+            h_parts[m0, a] = ahead[tag] if tag else tile("h%d_%d" % (m0, a), [PACK * w], BF16)[:]
+            shares = [(nc.vector, cw_bank, 0, cut)]
             if side:
-                shares.append((nc.gpsimd, cw_runs, tile("h_side%d_%d" % (m0, a), [PACK * side], BF16, tag), cut, w))
-            h_parts[m0, a] = [(staged, first, last) for engine, factors, staged, first, last in shares]
-            for engine, factors, staged, first, last in shares:
+                shares.append((nc.gpsimd, cw_runs, cut, w))
+            for engine, factors, first, last in shares:
+                staged = h_parts[m0, a][:, PACK * first : PACK * last]
                 runs = factors[:, PACK * RUN * a : PACK * RUN * (a + 1)].rearrange("p (c t i) -> p c t i", c=1, t=PACK)
                 engine.tensor_tensor(
-                    staged[:].rearrange("p (c i t) -> p c t i", i=RUN, t=PACK),
+                    staged.rearrange("p (c i t) -> p c t i", i=RUN, t=PACK),
                     sigs[m0, a][:, :, first:last].rearrange("p t (c i) -> p c t i", i=RUN),
                     runs.to_broadcast([P, (last - first) // RUN, PACK, RUN]),
                     ALU.mult,
@@ -206,15 +206,9 @@ def tile_list_kernl_sigm_res_bias_kernel(
 
         def quant_h(m0, a):
             c, n0 = divmod(m0, WIDE)
-            for staged, first, last in reversed(h_parts[m0, a]):
-                for k in range(first, last, P):
-                    end = min(k + P, last)
-                    cols = slice(WIDE * a + n0 + k, WIDE * a + n0 + end)
-                    nc.vector.quantize_mx(
-                        out=h_codes[c][:, cols].bitcast(FP8X4),
-                        scales=h_scales[c][:, cols],
-                        in_=staged[:, PACK * (k - first) : PACK * (end - first)],
-                    )
+            staged = h_parts[m0, a]
+            cols = slice(WIDE * a + n0, WIDE * a + n0 + staged.shape[1] // PACK)
+            nc.vector.quantize_mx(out=h_codes[c][:, cols].bitcast(FP8X4), scales=h_scales[c][:, cols], in_=staged)
 
         def warm_up(lhsT, passes):
             codes, scales = x_codes[0, 0][:, 0:PIECE], x_scales[0, 0][:, 0:PIECE]
@@ -337,7 +331,7 @@ def tile_list_kernl_sigm_res_bias_kernel(
         first_stage(WIDE, WIDE, 1, cuts=(PIECE, PIECE + P))
         steps = [(0, 1), (PIECE, 1), (WIDE, 0), (WIDE + PIECE, 0), (WIDE, 1)]
         for i, (m0, a) in enumerate(steps):
-            weigh(m0, PIECE, a, tag="odd_side")
+            weigh(m0, PIECE, a, tag=steps[i - 1] if i else None)
             if i > 0:
                 quant_h(*steps[i - 1])
 

@@ -32,7 +32,7 @@ WARM_EARLY, WARM_LATE = 5, 4
 PLACED = {
     "x_first01": 12288,
     "picked_w768": 12288,
-    "cw_turned": 14080,
+    "rows": 13312,
     "x_first10": 14336,
     "x_first11": 0,
     "h0_0": 0,
@@ -60,8 +60,10 @@ def tile_list_kernl_sigm_res_bias_kernel(
         offsets = keep.tile([P, J // 16], U16, name="offsets")
         nc.sync.dma_start(offsets[:], offs)
 
-        cw_t = keep.tile([P, 2, PACK], F32, name="cw_t")
-        nc.scalar.dma_start(cw_t[:], cw.rearrange("(a p t) -> p a t", a=2, t=PACK))
+        rows = tile("rows", [PASS], F32)
+        nc.scalar.dma_start(rows[P - 4 : P - 2, :], cw.rearrange("(a j) -> a j", a=2))
+        nc.scalar.dma_start(rows[P - 2 : P, :], cb.rearrange("(a j) -> a j", a=2))
+        nc.vector.memset(rows[0 : P - 4, :], 0.0)
 
         warm_in = keep.tile([P, 1], F32, name="warm_in")
         nc.vector.memset(warm_in[:], 0.0)
@@ -76,16 +78,16 @@ def tile_list_kernl_sigm_res_bias_kernel(
         nc.vector.memset(tab_sc[32:64, :], 0)
         nc.vector.memset(tab_sc[64:128, :], 0)
 
-        cw_runs = tile("cw_runs", [P], F32)
+        factors_sb = tile("factors_sb", [4 * PACK], F32)
         all_planes = tile("planes", [2, (J + 2 * N) // 4], I32)
         nc.gpsimd.memset(all_planes[:], 0)
         planes = [all_planes[:, :, PASS // 4 * a : PASS // 4 * (a + 1)] for a in range(2)]
         al_planes = [all_planes[:, :, (J + N * tier) // 4 : (J + N * (tier + 1)) // 4] for tier in range(2)]
 
-        cb_t = keep.tile([P, 2, PACK], F32, name="cb_t")
 
         banks = [psum.tile([P, WIDE], F32, name="bank%d" % i) for i in range(RING + 1)]
         cw_bank = banks[RING]
+        factors_ps = cw_bank[:, P - 4 : P - 4 + 4 * PACK]
         taken = []
 
         def next_bank():
@@ -145,7 +147,7 @@ def tile_list_kernl_sigm_res_bias_kernel(
             nc.vector.quantize_mx(out=x_codes[1, g][:].bitcast(FP8X4), scales=x_scales[1, g][:], in_=staged)
 
         def sigmoid(m0, a, t, sums):
-            nc.scalar.activation(sigs[m0, a][:, t, :], sums, ACT.Sigmoid, bias=cb_t[:, a, t : t + 1])
+            nc.scalar.activation(sigs[m0, a][:, t, :], sums, ACT.Sigmoid, bias=factors_sb[:, 4 * t + 2 + a : 4 * t + 3 + a])
 
         def first_stage(m0, w, a, tag=None, cuts=()):
             parts = list(zip((0,) + cuts, cuts + (w,)))
@@ -178,25 +180,21 @@ def tile_list_kernl_sigm_res_bias_kernel(
         h_scales = [tile("h_scales%d" % c, [2 * WIDE], U8) for c in range(2)]
 
         def spread_cw():
-            runs = cw_runs[:].rearrange("p (r k i) -> p r k i", k=2 * PACK, i=RUN)
-            values = cw_t[:].rearrange("p a (t r i) -> p r (a t) i", r=1, i=1)
-            nc.scalar.copy(runs, values.to_broadcast([P, P // (2 * PACK * RUN), 2 * PACK, RUN]))
-            turned = tile("cw_turned", [P], F32)
-            nc.tensor.transpose(cw_bank[:, P : 2 * P], cw_runs[:], identity[:])
-            nc.scalar.copy(turned[:], cw_bank[:, P : 2 * P])
-            nc.tensor.transpose(cw_bank[:, 0:P], turned[:], identity[:])
+            for t in reversed(range(PACK)):
+                nc.tensor.transpose(cw_bank[:, 4 * t : 4 * t + P], rows[:, t:PASS:PACK], identity[:])
+            nc.scalar.copy(factors_sb[:], factors_ps)
 
         h_parts = {}
 
         def weigh(m0, w, a, side=SIDE, tag=None):
             cut = w - side
             h_parts[m0, a] = ahead[tag] if tag else tile("h%d_%d" % (m0, a), [PACK * w], BF16)[:]
-            shares = [(nc.vector, cw_bank, 0, cut)]
+            shares = [(nc.vector, factors_ps, 0, cut)]
             if side:
-                shares.append((nc.gpsimd, cw_runs, cut, w))
+                shares.append((nc.gpsimd, factors_sb[:], cut, w))
             for engine, factors, first, last in shares:
                 staged = h_parts[m0, a][:, PACK * first : PACK * last]
-                runs = factors[:, PACK * RUN * a : PACK * RUN * (a + 1)].rearrange("p (c t i) -> p c t i", c=1, t=PACK)
+                runs = factors.rearrange("p (c t k) -> p c t k", c=1, t=PACK)[:, :, :, a : a + 1]
                 engine.tensor_tensor(
                     staged.rearrange("p (c i t) -> p c t i", i=RUN, t=PACK),
                     sigs[m0, a][:, :, first:last].rearrange("p t (c i) -> p c t i", i=RUN),
@@ -282,7 +280,6 @@ def tile_list_kernl_sigm_res_bias_kernel(
 
         load_x(1, 0)
         move_scales(0)
-        nc.sync.dma_start(cb_t[:], cb.rearrange("(a p t) -> p a t", a=2, t=PACK))
         load_x(1, 1)
         load_x(2, 0)
         move_scales(1)

@@ -24,7 +24,7 @@ RUN = 4
 WIDE = 512
 PIECE = 256
 RING = 7
-SIDE = 64
+SIDE = 72
 ROOM = PACK * PIECE // 2 - 32
 PORT_ORDER = (0, 2, 1, 3)
 WARM_EARLY, WARM_LATE = 5, 4
@@ -36,7 +36,7 @@ PLACED = {
     "x_first10": 14336,
     "x_first11": 0,
     "h0_0": 0,
-    "x_raw30": 2048,
+    "x_raw21": 2048,
     "h256_0": 2048,
     "x_late1": 6144,
     "h0_1": 6144,
@@ -127,7 +127,7 @@ def tile_list_kernl_sigm_res_bias_kernel(
         def copy_x(s, g, copy):
             if s < 2:
                 x_first[s, g] = tile("x_first%d%d" % (s, g), [PACK * PIECE], BF16)
-            staged = x_first[s, g][:] if s < 2 else x_late[g][:, s - 2, :]
+            staged = x_first[s, g][:] if s < 2 else x_late[s - 2][:, g, :]
             copy(
                 staged.rearrange("p (c i t) -> p c t i", i=RUN, t=PACK),
                 x_raw[s, g][:].rearrange("p t (c i) -> p c t i", i=RUN),
@@ -158,7 +158,15 @@ def tile_list_kernl_sigm_res_bias_kernel(
                 ahead[m0 + first, a] = both[:, 0 : PACK * PIECE // 2].bitcast(BF16)
             c, n0 = divmod(m0, WIDE)
             step = w
-            sums = [next_bank() for t in range(PACK)]
+            if c:
+                pairs = [next_bank() for pair in range(2)]
+                sums = [pairs[t // 2][:, PIECE * (t % 2) : PIECE * (t % 2 + 1)] for t in range(PACK)]
+                codes = [x_codes[1, n0 // PIECE][:, PIECE * g : PIECE * (g + 1)] for g in range(2)]
+                scales = [x_scales[1, n0 // PIECE][:, PIECE * g : PIECE * (g + 1)] for g in range(2)]
+            else:
+                sums = [next_bank() for t in range(PACK)]
+                codes = [x_codes[0, g][:, n0 : n0 + w] for g in range(2)]
+                scales = [x_scales[0, g][:, n0 : n0 + w] for g in range(2)]
             for t, bank in enumerate(sums):
                 for k in range(0, w, step):
                     for g in range(2):
@@ -166,12 +174,16 @@ def tile_list_kernl_sigm_res_bias_kernel(
                             out=bank[:, k : k + step],
                             lhsT=v_w[a][:, g, P * t : P * (t + 1)].bitcast(FP4X4),
                             lhsT_scale=planes[a][:, g, :].bitcast(U8)[:, P * t : P * (t + 1)],
-                            rhs=x_codes[c, g][:, n0 + k : n0 + k + step].bitcast(FP8X4),
-                            rhs_scale=x_scales[c, g][:, n0 + k : n0 + k + step],
+                            rhs=codes[g].bitcast(FP8X4),
+                            rhs_scale=scales[g],
                             start=(g == 0),
                             stop=(g == 1),
                         )
-                sigmoid(m0, a, t, bank[:, 0 : parts[0][1]])
+                if not c:
+                    sigmoid(m0, a, t, bank[:, 0 : parts[0][1]])
+                elif t % 2:
+                    for u in (t - 1, t):
+                        sigmoid(m0, a, u, sums[u][:, 0 : parts[0][1]])
             for first, last in parts[1:]:
                 for t, bank in enumerate(sums):
                     sigmoid(m0 + first, a, t, bank[:, first:last])
@@ -188,7 +200,7 @@ def tile_list_kernl_sigm_res_bias_kernel(
 
         def weigh(m0, w, a, side=SIDE, tag=None):
             cut = w - side
-            h_parts[m0, a] = ahead[tag] if tag else tile("h%d_%d" % (m0, a), [PACK * w], BF16)[:]
+            h_parts[m0, a] = ahead[tag][:, PACK * (PIECE - w) :] if tag else tile("h%d_%d" % (m0, a), [PACK * w], BF16)[:]
             shares = [(nc.vector, factors_ps, 0, cut)]
             if side:
                 shares.append((nc.gpsimd, factors_sb[:], cut, w))
@@ -283,8 +295,8 @@ def tile_list_kernl_sigm_res_bias_kernel(
         load_x(1, 1)
         load_x(2, 0)
         move_scales(1)
-        load_x(3, 0)
         load_x(2, 1)
+        load_x(3, 0)
         load_x(3, 1)
         nc.sync.dma_start(al8_w[:], al8_words.rearrange("a p n i -> a p (n i)").bitcast(I32).rearrange("a p n -> p a n"))
         nc.sync.dma_start(al4_w[:], al4_words.bitcast(I32).rearrange("a p n -> p a n"))
@@ -315,18 +327,19 @@ def tile_list_kernl_sigm_res_bias_kernel(
         copy_x(2, 0, scalar)
         first_stage(PIECE, PIECE, 0, "x_raw20")
         quant_h(0, 0)
-        copy_x(3, 0, vector)
+        copy_x(2, 1, vector)
         weigh(PIECE, PIECE, 0)
         quant_late_x(0)
-        copy_x(2, 1, scalar)
+        copy_x(3, 0, scalar)
         copy_x(3, 1, scalar)
 
-        first_stage(0, WIDE, 1, "x_raw21", cuts=(PIECE,))
+        first_stage(0, WIDE, 1, "x_raw30", cuts=(PIECE,))
         quant_h(PIECE, 0)
         quant_late_x(1)
-        first_stage(WIDE, WIDE, 0, cuts=(PIECE,))
-        first_stage(WIDE, WIDE, 1, cuts=(PIECE, PIECE + P))
-        steps = [(0, 1), (PIECE, 1), (WIDE, 0), (WIDE + PIECE, 0), (WIDE, 1)]
+        steps = [(0, 1), (PIECE, 1), (WIDE, 0), (WIDE, 1), (WIDE + PIECE, 0)]
+        for m0, a in steps[2:]:
+            first_stage(m0, PIECE, a)
+        first_stage(WIDE + PIECE, PIECE, 1, cuts=(P,))
         for i, (m0, a) in enumerate(steps):
             weigh(m0, PIECE, a, tag=steps[i - 1] if i else None)
             if i > 0:
@@ -341,27 +354,35 @@ def tile_list_kernl_sigm_res_bias_kernel(
             nc.sync.dma_start(out[P * half : P * (half + 1), 0:WIDE], res[:])
 
         ends = [WIDE + PIECE, WIDE + PIECE + P]
-        weigh(ends[0], P, 1, side=0)
+        weigh(ends[0], P, 1, side=SIDE // 2, tag=steps[-1])
         quant_h(*steps[-1])
-        weigh(ends[1], P, 1, side=0)
-        for m0 in ends:
-            quant_h(m0, 1)
+        quant_h(ends[0], 1)
+        planes_h = tile("planes_h", [PACK, P], BF16)
+        for t in range(PACK):
+            nc.scalar.activation(
+                planes_h[:, t, :], sigs[ends[1], 1][:, t, :], ACT.Copy, scale=factors_sb[:, 4 * t + 1 : 4 * t + 2]
+            )
+        h_parts[ends[1], 1] = tile("h_last", [PACK * P], BF16)[:]
+        nc.vector.tensor_copy(
+            h_parts[ends[1], 1].rearrange("p (c i t) -> p c t i", i=RUN, t=PACK),
+            planes_h[:].rearrange("p t (c i) -> p c t i", i=RUN),
+        )
+        quant_h(ends[1], 1)
 
-        third_sums = [next_bank()[:, 0:PIECE] for half in range(2)]
         bank = next_bank()
-        end_sums = [[bank[:, 0:P], bank[:, P : 2 * P]], [next_bank()[:, 0:P] for half in range(2)]]
+        third_sums = [bank[:, PIECE * half : PIECE * (half + 1)] for half in range(2)]
+        end_sums = [[next_bank()[:, 0:P] for half in range(2)] for end in ends]
         for half in range(2):
-            second_passes(WIDE, PIECE, 0, half, third_sums[half], True, False)
+            for a in range(2):
+                second_passes(WIDE, PIECE, a, half, third_sums[half], a == 0, a == 1)
+        store(WIDE, PIECE, third_sums, (bias_on_scalar, bias_on_scalar))
         for half in range(2):
-            second_passes(ends[0], P, 0, half, end_sums[0][half], half == 0, False)
+            second_passes(ends[0], P, 0, half, end_sums[0][half], True, False)
         for half in range(2):
             second_passes(ends[1], P, 0, half, end_sums[1][half], True, False)
         for half in range(2):
-            second_passes(WIDE, PIECE, 1, half, third_sums[half], False, True)
-        store(WIDE, PIECE, third_sums, (bias_on_scalar, bias_on_vector))
-        for half in range(2):
-            second_passes(ends[0], P, 1, half, end_sums[0][half], False, half == 1)
-        store(ends[0], P, end_sums[0], (bias_on_scalar, bias_on_scalar))
+            second_passes(ends[0], P, 1, half, end_sums[0][half], False, True)
+        store(ends[0], P, end_sums[0], (bias_on_vector, bias_on_vector))
         for half in range(2):
             second_passes(ends[1], P, 1, half, end_sums[1][half], False, True)
-        store(ends[1], P, end_sums[1], (bias_on_vector, bias_on_scalar))
+        store(ends[1], P, end_sums[1], (bias_on_scalar, bias_on_vector))

@@ -24,7 +24,7 @@ RUN = 4
 WIDE = 512
 PIECE = 256
 RING = 7
-SIDE = 72
+SIDE = 64
 ROOM = PACK * PIECE // 2 - 32
 PORT_ORDER = (0, 2, 1, 3)
 WARM_EARLY, WARM_LATE = 5, 4
@@ -58,7 +58,6 @@ def tile_list_kernl_sigm_res_bias_kernel(
             return keep.tile([P] + shape, dtype, name=name, tag=tag or name, align_bytes=64)
 
         offsets = keep.tile([P, J // 16], U16, name="offsets")
-        nc.sync.dma_start(offsets[:], offs)
 
         rows = tile("rows", [PASS], F32)
         nc.scalar.dma_start(rows[P - 4 : P - 2, :], cw.rearrange("(a j) -> a j", a=2))
@@ -75,6 +74,7 @@ def tile_list_kernl_sigm_res_bias_kernel(
 
         tab_sc = tile("tab_sc", [T // 4], I32)
         nc.sync.dma_start(tab_sc[0:32, :], tab_scales.bitcast(I32).rearrange("g r n -> r g n"))
+        nc.sync.dma_start(offsets[:], offs)
         nc.vector.memset(tab_sc[32:64, :], 0)
         nc.vector.memset(tab_sc[64:128, :], 0)
 
@@ -317,11 +317,11 @@ def tile_list_kernl_sigm_res_bias_kernel(
         pick_words(PASS + quarter, quarter)
         copy_x(1, 0, scalar)
         part_words(PASS, quarter)
-        quant_x(1, 0)
         part_words(PASS + quarter, quarter)
 
         first_stage(0, PIECE, 0, "x_raw10")
         copy_x(1, 1, vector)
+        quant_x(1, 0)
         quant_x(1, 1)
         weigh(0, PIECE, 0)
         copy_x(2, 0, scalar)

@@ -34,12 +34,11 @@ PLACED = {
     "picked_w768": 12288,
     "rows": 13312,
     "x_first10": 14336,
-    "x_first11": 0,
-    "h0_0": 0,
+    "x_raw11": 20480,
+    "h0_0": 20480,
     "x_raw21": 2048,
     "h256_0": 2048,
-    "x_late1": 6144,
-    "h0_1": 6144,
+    "h0_1": 2048,
 }
 
 
@@ -326,8 +325,8 @@ def tile_list_kernl_sigm_res_bias_kernel(
         weigh(0, PIECE, 0)
         copy_x(2, 0, scalar)
         first_stage(PIECE, PIECE, 0, "x_raw20")
-        quant_h(0, 0)
         copy_x(2, 1, vector)
+        quant_h(0, 0)
         weigh(PIECE, PIECE, 0)
         quant_late_x(0)
         copy_x(3, 0, scalar)
@@ -341,7 +340,7 @@ def tile_list_kernl_sigm_res_bias_kernel(
             first_stage(m0, PIECE, a)
         first_stage(WIDE + PIECE, PIECE, 1, cuts=(P,))
         for i, (m0, a) in enumerate(steps):
-            weigh(m0, PIECE, a, tag=steps[i - 1] if i else None)
+            weigh(m0, PIECE, a, side=SIDE if i else SIDE // 2, tag=steps[i - 1] if i else None)
             if i > 0:
                 quant_h(*steps[i - 1])
 

@@ -34,7 +34,7 @@ PLACED = {
     "picked_w768": 12288,
     "rows": 13312,
     "x_first10": 14336,
-    "x_raw11": 20480,
+    "x_half0": 20480,
     "h0_0": 20480,
     "x_raw21": 2048,
     "h256_0": 2048,
@@ -213,11 +213,17 @@ def tile_list_kernl_sigm_res_bias_kernel(
                     ALU.mult,
                 )
 
-        def quant_h(m0, a):
+        def quant_h(m0, a, calls=1):
             c, n0 = divmod(m0, WIDE)
             staged = h_parts[m0, a]
-            cols = slice(WIDE * a + n0, WIDE * a + n0 + staged.shape[1] // PACK)
-            nc.vector.quantize_mx(out=h_codes[c][:, cols].bitcast(FP8X4), scales=h_scales[c][:, cols], in_=staged)
+            each = staged.shape[1] // PACK // calls
+            for first in range(0, each * calls, each):
+                cols = slice(WIDE * a + n0 + first, WIDE * a + n0 + first + each)
+                nc.vector.quantize_mx(
+                    out=h_codes[c][:, cols].bitcast(FP8X4),
+                    scales=h_scales[c][:, cols],
+                    in_=staged[:, PACK * first : PACK * (first + each)],
+                )
 
         def warm_up(lhsT, passes):
             codes, scales = x_codes[0, 0][:, 0:PIECE], x_scales[0, 0][:, 0:PIECE]
@@ -308,8 +314,8 @@ def tile_list_kernl_sigm_res_bias_kernel(
 
         quarter = PASS // 2
         pick_words(0, PASS)
-        part_words(0, PASS)
         pick_words(PASS, quarter)
+        part_words(0, PASS)
         warm_up(picked_w[0][:].bitcast(U16)[:, 0:P].bitcast(FP4X4), WARM_LATE)
         copy_x(0, 1, scalar)
         quant_x(0, 1)
@@ -319,9 +325,16 @@ def tile_list_kernl_sigm_res_bias_kernel(
         part_words(PASS + quarter, quarter)
 
         first_stage(0, PIECE, 0, "x_raw10")
-        copy_x(1, 1, vector)
+        halves = [tile("x_half%d" % i, [PACK * P], BF16) for i in range(2)]
+        for i, staged in enumerate(halves):
+            vector(
+                staged[:].rearrange("p (c i t) -> p c t i", i=RUN, t=PACK),
+                x_raw[1, 1][:, :, P * i : P * (i + 1)].rearrange("p t (c i) -> p c t i", i=RUN),
+            )
         quant_x(1, 0)
-        quant_x(1, 1)
+        for i, staged in enumerate(halves):
+            cols = slice(PIECE + P * i, PIECE + P * (i + 1))
+            nc.vector.quantize_mx(out=x_codes[0, 1][:, cols].bitcast(FP8X4), scales=x_scales[0, 1][:, cols], in_=staged[:])
         weigh(0, PIECE, 0)
         copy_x(2, 0, scalar)
         first_stage(PIECE, PIECE, 0, "x_raw20")
@@ -362,11 +375,12 @@ def tile_list_kernl_sigm_res_bias_kernel(
                 planes_h[:, t, :], sigs[ends[1], 1][:, t, :], ACT.Copy, scale=factors_sb[:, 4 * t + 1 : 4 * t + 2]
             )
         h_parts[ends[1], 1] = tile("h_last", [PACK * P], BF16)[:]
-        nc.vector.tensor_copy(
-            h_parts[ends[1], 1].rearrange("p (c i t) -> p c t i", i=RUN, t=PACK),
-            planes_h[:].rearrange("p t (c i) -> p c t i", i=RUN),
-        )
-        quant_h(ends[1], 1)
+        for first in (0, P // 2):
+            nc.vector.tensor_copy(
+                h_parts[ends[1], 1][:, PACK * first : PACK * (first + P // 2)].rearrange("p (c i t) -> p c t i", i=RUN, t=PACK),
+                planes_h[:, :, first : first + P // 2].rearrange("p t (c i) -> p c t i", i=RUN),
+            )
+        quant_h(ends[1], 1, calls=2)
 
         bank = next_bank()
         third_sums = [bank[:, PIECE * half : PIECE * (half + 1)] for half in range(2)]

@@ -157,13 +157,15 @@ def tile_list_kernl_sigm_res_bias_kernel(
                 ahead[m0 + first, a] = both[:, 0 : PACK * PIECE // 2].bitcast(BF16)
             c, n0 = divmod(m0, WIDE)
             step = w
-            if c:
+            if c or a:
                 pairs = [next_bank() for pair in range(2)]
                 sums = [pairs[t // 2][:, PIECE * (t % 2) : PIECE * (t % 2 + 1)] for t in range(PACK)]
+            else:
+                sums = [next_bank() for t in range(PACK)]
+            if c:
                 codes = [x_codes[1, n0 // PIECE][:, PIECE * g : PIECE * (g + 1)] for g in range(2)]
                 scales = [x_scales[1, n0 // PIECE][:, PIECE * g : PIECE * (g + 1)] for g in range(2)]
             else:
-                sums = [next_bank() for t in range(PACK)]
                 codes = [x_codes[0, g][:, n0 : n0 + w] for g in range(2)]
                 scales = [x_scales[0, g][:, n0 : n0 + w] for g in range(2)]
             for t, bank in enumerate(sums):
@@ -178,7 +180,7 @@ def tile_list_kernl_sigm_res_bias_kernel(
                             start=(g == 0),
                             stop=(g == 1),
                         )
-                if not c:
+                if not (c or a):
                     sigmoid(m0, a, t, bank[:, 0 : parts[0][1]])
                 elif t % 2:
                     for u in (t - 1, t):
@@ -342,20 +344,21 @@ def tile_list_kernl_sigm_res_bias_kernel(
         quant_h(0, 0)
         weigh(PIECE, PIECE, 0)
         quant_late_x(0)
-        copy_x(3, 0, scalar)
-        copy_x(3, 1, scalar)
 
-        first_stage(0, WIDE, 1, "x_raw30", cuts=(PIECE,))
+        first_stage(0, PIECE, 1)
         quant_h(PIECE, 0)
-        quant_late_x(1)
+        copy_x(3, 1, scalar)
+        first_stage(PIECE, PIECE, 1, "x_raw31")
         steps = [(0, 1), (PIECE, 1), (WIDE, 0), (WIDE, 1), (WIDE + PIECE, 0)]
+        weigh(0, PIECE, 1)
+        copy_x(3, 0, vector)
+        quant_late_x(1)
         for m0, a in steps[2:]:
             first_stage(m0, PIECE, a)
         first_stage(WIDE + PIECE, PIECE, 1, cuts=(P,))
-        for i, (m0, a) in enumerate(steps):
-            weigh(m0, PIECE, a, side=SIDE if i else SIDE // 2, tag=steps[i - 1] if i else None)
-            if i > 0:
-                quant_h(*steps[i - 1])
+        for before, (m0, a) in zip(steps, steps[1:]):
+            weigh(m0, PIECE, a, tag=before)
+            quant_h(*before)
 
         for half in range(2):
             sums = next_bank()[:]

@@ -27,18 +27,17 @@ RING = 7
 SIDE = 64
 ROOM = PACK * PIECE // 2 - 32
 PORT_ORDER = (0, 2, 1, 3)
-WARM_EARLY, WARM_LATE = 5, 4
+WARM = 9
 
 PLACED = {
-    "x_first01": 12288,
-    "picked_w768": 12288,
-    "rows": 13312,
-    "x_first10": 14336,
     "x_half0": 20480,
     "h0_0": 20480,
     "x_raw21": 2048,
     "h256_0": 2048,
     "h0_1": 2048,
+    "x_raw20": 61440,
+    "sig256_0": 61440 - 5120,
+    "sig0_1": 61440 + 3072,
 }
 
 
@@ -58,28 +57,31 @@ def tile_list_kernl_sigm_res_bias_kernel(
 
         offsets = keep.tile([P, J // 16], U16, name="offsets")
 
+        tab_sc = tile("tab_sc", [T // 4], I32)
+        nc.sync.dma_start(tab_sc[96:128, :], tab_scales.bitcast(I32).rearrange("g r n -> r g n"))
+        nc.sync.dma_start(offsets[:], offs)
+        nc.vector.memset(tab_sc[0:96, :], 0)
+
         rows = tile("rows", [PASS], F32)
         nc.scalar.dma_start(rows[P - 4 : P - 2, :], cw.rearrange("(a j) -> a j", a=2))
         nc.scalar.dma_start(rows[P - 2 : P, :], cb.rearrange("(a j) -> a j", a=2))
         nc.vector.memset(rows[0 : P - 4, :], 0.0)
 
-        warm_in = keep.tile([P, 1], F32, name="warm_in")
-        nc.vector.memset(warm_in[:], 0.0)
         warm_out = keep.tile([P, 1], F32, name="warm_out")
-        nc.scalar.activation(warm_out[:], warm_in[:], ACT.Sigmoid)
+        nc.scalar.activation(warm_out[0:64, :], rows[0:64, 0:1], ACT.Sigmoid)
+
+        zeros = tile("zeros", [PASS], BF16)
+        nc.vector.memset(zeros[:], 0.0)
+        zero_codes = tile("zero_codes", [P], U32)
+        zero_scales = tile("zero_scales", [P], U8)
+        nc.vector.quantize_mx(out=zero_codes[:].bitcast(FP8X4), scales=zero_scales[:], in_=zeros[:])
 
         identity = tile("identity", [P], F32)
-        make_identity(nc, identity[:])
-
-        tab_sc = tile("tab_sc", [T // 4], I32)
-        nc.sync.dma_start(tab_sc[0:32, :], tab_scales.bitcast(I32).rearrange("g r n -> r g n"))
-        nc.sync.dma_start(offsets[:], offs)
-        nc.vector.memset(tab_sc[32:64, :], 0)
-        nc.vector.memset(tab_sc[64:128, :], 0)
 
         factors_sb = tile("factors_sb", [4 * PACK], F32)
         all_planes = tile("planes", [2, (J + 2 * N) // 4], I32)
         nc.gpsimd.memset(all_planes[:], 0)
+        make_identity(nc, identity[:])
         planes = [all_planes[:, :, PASS // 4 * a : PASS // 4 * (a + 1)] for a in range(2)]
         al_planes = [all_planes[:, :, (J + N * tier) // 4 : (J + N * (tier + 1)) // 4] for tier in range(2)]
 
@@ -157,7 +159,7 @@ def tile_list_kernl_sigm_res_bias_kernel(
                 ahead[m0 + first, a] = both[:, 0 : PACK * PIECE // 2].bitcast(BF16)
             c, n0 = divmod(m0, WIDE)
             step = w
-            if c or a:
+            if m0 or a:
                 pairs = [next_bank() for pair in range(2)]
                 sums = [pairs[t // 2][:, PIECE * (t % 2) : PIECE * (t % 2 + 1)] for t in range(PACK)]
             else:
@@ -180,7 +182,7 @@ def tile_list_kernl_sigm_res_bias_kernel(
                             start=(g == 0),
                             stop=(g == 1),
                         )
-                if not (c or a):
+                if not (m0 or a):
                     sigmoid(m0, a, t, bank[:, 0 : parts[0][1]])
                 elif t % 2:
                     for u in (t - 1, t):
@@ -195,7 +197,6 @@ def tile_list_kernl_sigm_res_bias_kernel(
         def spread_cw():
             for t in reversed(range(PACK)):
                 nc.tensor.transpose(cw_bank[:, 4 * t : 4 * t + P], rows[:, t:PASS:PACK], identity[:])
-            nc.scalar.copy(factors_sb[:], factors_ps)
 
         h_parts = {}
 
@@ -225,19 +226,6 @@ def tile_list_kernl_sigm_res_bias_kernel(
                     out=h_codes[c][:, cols].bitcast(FP8X4),
                     scales=h_scales[c][:, cols],
                     in_=staged[:, PACK * first : PACK * (first + each)],
-                )
-
-        def warm_up(lhsT, passes):
-            codes, scales = x_codes[0, 0][:, 0:PIECE], x_scales[0, 0][:, 0:PIECE]
-            for i in range(passes):
-                nc.tensor.matmul_mx(
-                    out=cw_bank[:, PIECE : 2 * PIECE],
-                    lhsT=lhsT,
-                    lhsT_scale=scales[:, 0:P],
-                    rhs=codes.bitcast(FP8X4),
-                    rhs_scale=scales,
-                    start=True,
-                    stop=True,
                 )
 
         b_t = keep.tile([P, 2], F32, name="b_t")
@@ -278,27 +266,24 @@ def tile_list_kernl_sigm_res_bias_kernel(
 
         def move_scales(a):
             for q in PORT_ORDER:
-                rows = picked_sc[8 * q : 8 * (q + 1), PASS * a : PASS * (a + 1)].bitcast(I32)
+                rows = picked_sc[96 + 8 * q : 96 + 8 * (q + 1), PASS * a : PASS * (a + 1)].bitcast(I32)
                 nc.sync.dma_start(planes[a][32 * q : 32 * q + 4, :, :], rows)
 
-        load_x(0, 0)
         nc.sync.dma_start(tab_w[:], tab_words[0].rearrange("p t b -> p (t b)").bitcast(I32))
+        load_x(0, 0)
         load_x(0, 1)
 
         scalar, vector = nc.scalar.copy, nc.vector.tensor_copy
         spread_cw()
-        copy_x(0, 0, scalar)
         for a in range(2):
             cols = slice(PASS * a, PASS * (a + 1))
             nc.vector.tensor_copy(
                 picked_sc[:, cols].rearrange("p (t r) -> p r t", t=PACK),
                 tab_sc[:].bitcast(U8).indirect(offsets[:, 32 * a : 32 * (a + 1)]),
             )
-        quant_x(0, 0)
-        warm_up(x_codes[0, 0][:, 0:P].bitcast(FP8X4), WARM_EARLY)
 
-        load_x(1, 0)
         move_scales(0)
+        load_x(1, 0)
         load_x(1, 1)
         load_x(2, 0)
         move_scales(1)
@@ -314,17 +299,25 @@ def tile_list_kernl_sigm_res_bias_kernel(
         with nc.allow_non_contiguous_dma(reason="one bias value a partition"):
             nc.sync.dma_start(b_t[:], b.rearrange("(h p) -> p h", p=P))
 
-        quarter = PASS // 2
         pick_words(0, PASS)
-        pick_words(PASS, quarter)
+        pick_words(PASS, PASS)
+        for i in range(WARM):
+            nc.tensor.matmul_mx(
+                out=cw_bank[:, PIECE : 2 * PIECE],
+                lhsT=zero_codes[:].bitcast(FP8X4),
+                lhsT_scale=zero_scales[:],
+                rhs=picked_w[0][:].bitcast(U16)[:, 0:PIECE].bitcast(FP4X4),
+                rhs_scale=picked_sc[:, 0:PIECE],
+                start=True,
+                stop=True,
+            )
         part_words(0, PASS)
-        warm_up(picked_w[0][:].bitcast(U16)[:, 0:P].bitcast(FP4X4), WARM_LATE)
-        copy_x(0, 1, scalar)
-        quant_x(0, 1)
-        pick_words(PASS + quarter, quarter)
+        part_words(PASS, PASS)
+        for g in range(2):
+            copy_x(0, g, scalar)
+            quant_x(0, g)
         copy_x(1, 0, scalar)
-        part_words(PASS, quarter)
-        part_words(PASS + quarter, quarter)
+        nc.scalar.copy(factors_sb[:], factors_ps)
 
         first_stage(0, PIECE, 0, "x_raw10")
         halves = [tile("x_half%d" % i, [PACK * P], BF16) for i in range(2)]
@@ -339,7 +332,7 @@ def tile_list_kernl_sigm_res_bias_kernel(
             nc.vector.quantize_mx(out=x_codes[0, 1][:, cols].bitcast(FP8X4), scales=x_scales[0, 1][:, cols], in_=staged[:])
         weigh(0, PIECE, 0)
         copy_x(2, 0, scalar)
-        first_stage(PIECE, PIECE, 0, "x_raw20")
+        first_stage(PIECE, PIECE, 0)
         copy_x(2, 1, vector)
         quant_h(0, 0)
         weigh(PIECE, PIECE, 0)
@@ -350,8 +343,8 @@ def tile_list_kernl_sigm_res_bias_kernel(
         copy_x(3, 1, scalar)
         first_stage(PIECE, PIECE, 1, "x_raw31")
         steps = [(0, 1), (PIECE, 1), (WIDE, 0), (WIDE, 1), (WIDE + PIECE, 0)]
-        weigh(0, PIECE, 1)
         copy_x(3, 0, vector)
+        weigh(0, PIECE, 1)
         quant_late_x(1)
         for m0, a in steps[2:]:
             first_stage(m0, PIECE, a)

@@ -35,6 +35,8 @@ PLACED = {
     "x_raw21": 2048,
     "h256_0": 2048,
     "h0_1": 2048,
+    "x_raw01": 73728,
+    "v_w1": 73728,
     "x_raw20": 61440,
     "sig256_0": 61440 - 5120,
     "sig0_1": 61440 + 3072,
@@ -312,10 +314,10 @@ def tile_list_kernl_sigm_res_bias_kernel(
                 stop=True,
             )
         part_words(0, PASS)
-        part_words(PASS, PASS)
         for g in range(2):
             copy_x(0, g, scalar)
             quant_x(0, g)
+        part_words(PASS, PASS)
         copy_x(1, 0, scalar)
         nc.scalar.copy(factors_sb[:], factors_ps)
 

@@ -284,8 +284,8 @@ def tile_list_kernl_sigm_res_bias_kernel(
                 tab_sc[:].bitcast(U8).indirect(offsets[:, 32 * a : 32 * (a + 1)]),
             )
 
-        move_scales(0)
         load_x(1, 0)
+        move_scales(0)
         load_x(1, 1)
         load_x(2, 0)
         move_scales(1)

@@ -34,7 +34,10 @@ PLACED = {
     "h0_0": 20480,
     "x_raw21": 2048,
     "h256_0": 2048,
-    "h0_1": 2048,
+    "h256_1": 2048,
+    "x_raw31": 40960,
+    "sig256_1": 40960 - 5120,
+    "h_codes1": 40960 + 2048,
     "x_raw01": 73728,
     "v_w1": 73728,
     "x_raw20": 61440,
@@ -193,8 +196,8 @@ def tile_list_kernl_sigm_res_bias_kernel(
                 for t, bank in enumerate(sums):
                     sigmoid(m0 + first, a, t, bank[:, first:last])
 
-        h_codes = [tile("h_codes%d" % c, [2 * WIDE], U32) for c in range(2)]
-        h_scales = [tile("h_scales%d" % c, [2 * WIDE], U8) for c in range(2)]
+        h_codes = [tile("h_codes%d" % c, [2 * PIECE], U32) for c in range(4)]
+        h_scales = [tile("h_scales%d" % c, [2 * PIECE], U8) for c in range(4)]
 
         def spread_cw():
             for t in reversed(range(PACK)):
@@ -219,11 +222,11 @@ def tile_list_kernl_sigm_res_bias_kernel(
                 )
 
         def quant_h(m0, a, calls=1):
-            c, n0 = divmod(m0, WIDE)
+            c, n0 = divmod(m0, PIECE)
             staged = h_parts[m0, a]
             each = staged.shape[1] // PACK // calls
             for first in range(0, each * calls, each):
-                cols = slice(WIDE * a + n0 + first, WIDE * a + n0 + first + each)
+                cols = slice(PIECE * a + n0 + first, PIECE * a + n0 + first + each)
                 nc.vector.quantize_mx(
                     out=h_codes[c][:, cols].bitcast(FP8X4),
                     scales=h_scales[c][:, cols],
@@ -235,8 +238,8 @@ def tile_list_kernl_sigm_res_bias_kernel(
         al8_w = tile("al8_w", [2, N], I32)
 
         def second_passes(m0, w, a, half, dst, opens, closes):
-            c, n0 = divmod(m0, WIDE)
-            at = WIDE * a + n0
+            c, n0 = divmod(m0, PIECE)
+            at = PIECE * a + n0
             al4 = al4_w[:, a, P // 2 * half : P // 2 * (half + 1)].bitcast(FP4X4)
             al8 = al8_w[:, a, P * half : P * (half + 1)].bitcast(FP8X4)
             step = w
@@ -341,24 +344,25 @@ def tile_list_kernl_sigm_res_bias_kernel(
         quant_late_x(0)
 
         first_stage(0, PIECE, 1)
-        quant_h(PIECE, 0)
         copy_x(3, 1, scalar)
-        first_stage(PIECE, PIECE, 1, "x_raw31")
+        first_stage(PIECE, PIECE, 1)
         steps = [(0, 1), (PIECE, 1), (WIDE, 0), (WIDE, 1), (WIDE + PIECE, 0)]
+        weigh(0, PIECE, 1, tag=(PIECE, 0))
         copy_x(3, 0, vector)
-        weigh(0, PIECE, 1)
+        quant_h(PIECE, 0)
         quant_late_x(1)
         for m0, a in steps[2:]:
             first_stage(m0, PIECE, a)
         first_stage(WIDE + PIECE, PIECE, 1, cuts=(P,))
         for before, (m0, a) in zip(steps, steps[1:]):
-            weigh(m0, PIECE, a, tag=before)
+            weigh(m0, PIECE, a, tag=before if m0 >= WIDE else None)
             quant_h(*before)
 
         for half in range(2):
             sums = next_bank()[:]
-            for a in range(2):
-                second_passes(0, WIDE, a, half, sums, a == 0, a == 1)
+            for m0 in (0, PIECE):
+                for a in range(2):
+                    second_passes(m0, PIECE, a, half, sums[:, m0 : m0 + PIECE], a == 0, a == 1)
             res = tile("res_first%d" % half, [WIDE], F32)
             bias_on_scalar(res[:], sums, half)
             nc.sync.dma_start(out[P * half : P * (half + 1), 0:WIDE], res[:])

@@ -30,14 +30,14 @@ PORT_ORDER = (0, 2, 1, 3)
 WARM = 9
 
 PLACED = {
-    "x_half0": 20480,
+    "x_half11_0": 20480,
     "h0_0": 20480,
     "x_raw21": 2048,
     "h256_0": 2048,
-    "h256_1": 2048,
+    "x_half30_0": 8192,
+    "h256_1": 8192,
     "x_raw31": 40960,
     "sig256_1": 40960 - 5120,
-    "h_codes1": 40960 + 2048,
     "x_raw01": 73728,
     "v_w1": 73728,
     "x_raw20": 61440,
@@ -147,6 +147,20 @@ def tile_list_kernl_sigm_res_bias_kernel(
             nc.vector.quantize_mx(
                 out=x_codes[0, g][:, cols].bitcast(FP8X4), scales=x_scales[0, g][:, cols], in_=x_first[s, g][:]
             )
+
+        def copy_halves(s, g):
+            halves = [tile("x_half%d%d_%d" % (s, g, i), [PACK * P], BF16) for i in range(2)]
+            for i, staged in enumerate(halves):
+                nc.vector.tensor_copy(
+                    staged[:].rearrange("p (c i t) -> p c t i", i=RUN, t=PACK),
+                    x_raw[s, g][:, :, P * i : P * (i + 1)].rearrange("p t (c i) -> p c t i", i=RUN),
+                )
+            return halves
+
+        def quant_halves(halves, c, g, first):
+            for i, staged in enumerate(halves):
+                cols = slice(first + P * i, first + P * (i + 1))
+                nc.vector.quantize_mx(out=x_codes[c, g][:, cols].bitcast(FP8X4), scales=x_scales[c, g][:, cols], in_=staged[:])
 
         def quant_late_x(g):
             staged = x_late[g][:].rearrange("p s c -> p (s c)")
@@ -293,8 +307,8 @@ def tile_list_kernl_sigm_res_bias_kernel(
         load_x(2, 0)
         move_scales(1)
         load_x(2, 1)
-        load_x(3, 0)
         load_x(3, 1)
+        load_x(3, 0)
         nc.sync.dma_start(al8_w[:], al8_words.rearrange("a p n i -> a p (n i)").bitcast(I32).rearrange("a p n -> p a n"))
         nc.sync.dma_start(al4_w[:], al4_words.bitcast(I32).rearrange("a p n -> p a n"))
         for tier, src in enumerate((al4_scales, al8_scales)):
@@ -325,16 +339,9 @@ def tile_list_kernl_sigm_res_bias_kernel(
         nc.scalar.copy(factors_sb[:], factors_ps)
 
         first_stage(0, PIECE, 0, "x_raw10")
-        halves = [tile("x_half%d" % i, [PACK * P], BF16) for i in range(2)]
-        for i, staged in enumerate(halves):
-            vector(
-                staged[:].rearrange("p (c i t) -> p c t i", i=RUN, t=PACK),
-                x_raw[1, 1][:, :, P * i : P * (i + 1)].rearrange("p t (c i) -> p c t i", i=RUN),
-            )
+        halves = copy_halves(1, 1)
         quant_x(1, 0)
-        for i, staged in enumerate(halves):
-            cols = slice(PIECE + P * i, PIECE + P * (i + 1))
-            nc.vector.quantize_mx(out=x_codes[0, 1][:, cols].bitcast(FP8X4), scales=x_scales[0, 1][:, cols], in_=staged[:])
+        quant_halves(halves, 0, 1, PIECE)
         weigh(0, PIECE, 0)
         copy_x(2, 0, scalar)
         first_stage(PIECE, PIECE, 0)
@@ -348,9 +355,11 @@ def tile_list_kernl_sigm_res_bias_kernel(
         first_stage(PIECE, PIECE, 1)
         steps = [(0, 1), (PIECE, 1), (WIDE, 0), (WIDE, 1), (WIDE + PIECE, 0)]
         weigh(0, PIECE, 1, tag=(PIECE, 0))
-        copy_x(3, 0, vector)
         quant_h(PIECE, 0)
-        quant_late_x(1)
+        nc.vector.quantize_mx(
+            out=x_codes[1, 1][:, PIECE:WIDE].bitcast(FP8X4), scales=x_scales[1, 1][:, PIECE:WIDE], in_=x_late[1][:, 1, :]
+        )
+        quant_halves(copy_halves(3, 0), 1, 1, 0)
         for m0, a in steps[2:]:
             first_stage(m0, PIECE, a)
         first_stage(WIDE + PIECE, PIECE, 1, cuts=(P,))

@@ -26,6 +26,7 @@ PIECE = 256
 RING = 7
 SIDE = 64
 ROOM = PACK * PIECE // 2 - 32
+ORDER = (0, 1, 2, 3, 4, 5, 6, 0, 1, 2, 6, 0, 3, 4, 5, 1, 2, 6, 0, 3, 4, 5, 1, 2, 6)
 PORT_ORDER = (0, 2, 1, 3)
 WARM = 9
 
@@ -38,6 +39,9 @@ PLACED = {
     "h256_1": 8192,
     "x_raw31": 40960,
     "sig256_1": 40960 - 5120,
+    "sig512_0": 40960 + 3072,
+    "x_raw30": 90112,
+    "sig512_1": 90112,
     "x_raw01": 73728,
     "v_w1": 73728,
     "x_raw20": 61440,
@@ -97,7 +101,7 @@ def tile_list_kernl_sigm_res_bias_kernel(
         taken = []
 
         def next_bank():
-            taken.append(banks[len(taken) % RING])
+            taken.append(banks[ORDER[len(taken)]])
             return taken[-1]
 
         tab_w = tile("tab_w", [T], I32)
@@ -169,7 +173,7 @@ def tile_list_kernl_sigm_res_bias_kernel(
         def sigmoid(m0, a, t, sums):
             nc.scalar.activation(sigs[m0, a][:, t, :], sums, ACT.Sigmoid, bias=factors_sb[:, 4 * t + 2 + a : 4 * t + 3 + a])
 
-        def first_stage(m0, w, a, tag=None, cuts=()):
+        def first_stage(m0, w, a, tag=None, cuts=(), split=False):
             parts = list(zip((0,) + cuts, cuts + (w,)))
             for first, last in parts:
                 name = "sig%d_%d" % (m0 + first, a)
@@ -177,7 +181,6 @@ def tile_list_kernl_sigm_res_bias_kernel(
                 sigs[m0 + first, a] = both[:, ROOM:].rearrange("p (t m) -> p t m", t=PACK)
                 ahead[m0 + first, a] = both[:, 0 : PACK * PIECE // 2].bitcast(BF16)
             c, n0 = divmod(m0, WIDE)
-            step = w
             if m0 or a:
                 pairs = [next_bank() for pair in range(2)]
                 sums = [pairs[t // 2][:, PIECE * (t % 2) : PIECE * (t % 2 + 1)] for t in range(PACK)]
@@ -189,18 +192,27 @@ def tile_list_kernl_sigm_res_bias_kernel(
             else:
                 codes = [x_codes[0, g][:, n0 : n0 + w] for g in range(2)]
                 scales = [x_scales[0, g][:, n0 : n0 + w] for g in range(2)]
+
+            def product(t, g, start, stop):
+                nc.tensor.matmul_mx(
+                    out=sums[t][:, 0:w],
+                    lhsT=v_w[a][:, g, P * t : P * (t + 1)].bitcast(FP4X4),
+                    lhsT_scale=planes[a][:, g, :].bitcast(U8)[:, P * t : P * (t + 1)],
+                    rhs=codes[g].bitcast(FP8X4),
+                    rhs_scale=scales[g],
+                    start=start,
+                    stop=stop,
+                )
+
+            if split:
+                for t in range(PACK):
+                    product(t, 1, t % 2 == 0, False)
             for t, bank in enumerate(sums):
-                for k in range(0, w, step):
-                    for g in range(2):
-                        nc.tensor.matmul_mx(
-                            out=bank[:, k : k + step],
-                            lhsT=v_w[a][:, g, P * t : P * (t + 1)].bitcast(FP4X4),
-                            lhsT_scale=planes[a][:, g, :].bitcast(U8)[:, P * t : P * (t + 1)],
-                            rhs=codes[g].bitcast(FP8X4),
-                            rhs_scale=scales[g],
-                            start=(g == 0),
-                            stop=(g == 1),
-                        )
+                if split:
+                    product(t, 0, False, t % 2 == 1)
+                else:
+                    product(t, 0, True, False)
+                    product(t, 1, False, True)
                 if not (m0 or a):
                     sigmoid(m0, a, t, bank[:, 0 : parts[0][1]])
                 elif t % 2:
@@ -305,8 +317,8 @@ def tile_list_kernl_sigm_res_bias_kernel(
         move_scales(0)
         load_x(1, 1)
         load_x(2, 0)
-        move_scales(1)
         load_x(2, 1)
+        move_scales(1)
         load_x(3, 1)
         load_x(3, 0)
         nc.sync.dma_start(al8_w[:], al8_words.rearrange("a p n i -> a p (n i)").bitcast(I32).rearrange("a p n -> p a n"))
@@ -361,7 +373,7 @@ def tile_list_kernl_sigm_res_bias_kernel(
         )
         quant_halves(copy_halves(3, 0), 1, 1, 0)
         for m0, a in steps[2:]:
-            first_stage(m0, PIECE, a)
+            first_stage(m0, PIECE, a, split=(m0 == WIDE + PIECE))
         first_stage(WIDE + PIECE, PIECE, 1, cuts=(P,))
         for before, (m0, a) in zip(steps, steps[1:]):
             weigh(m0, PIECE, a, tag=before if m0 >= WIDE else None)

from contextlib import ExitStack

import concourse.mybir as mybir
from concourse.masks import make_identity

K, M, N, J, T = 1024, 1024, 256, 1024, 2048
FLOPS = 2 * K * J * M + 2 * 2 * J * N * M

F32 = mybir.dt.float32
BF16 = mybir.dt.bfloat16
I32 = mybir.dt.int32
U32 = mybir.dt.uint32
U16 = mybir.dt.uint16
U8 = mybir.dt.uint8
FP8X4 = mybir.dt.float8_e4m3fn_x4
FP4X4 = mybir.dt.float4_e2m1fn_x4
ACT = mybir.ActivationFunctionType
ALU = mybir.AluOpType

P = 128
PACK = 4
PASS = P * PACK
RUN = 4
WIDE = 512
PIECE = 256
RING = 7
SIDE = 64
ROOM = PACK * PIECE // 2 - 32
ORDER = (0, 1, 2, 3, 4, 5, 6, 0, 1, 2, 6, 0, 3, 4, 5, 1, 2, 6, 0, 3, 4, 5, 1, 2, 6)
PORT_ORDER = (0, 2, 1, 3)
WARM = 9

PLACED = {
    "x_half11_0": 20480,
    "h0_0": 20480,
    "x_raw21": 2048,
    "h256_0": 2048,
    "x_half30_0": 8192,
    "h256_1": 8192,
    "x_raw31": 40960,
    "sig256_1": 40960 - 5120,
    "sig512_0": 40960 + 3072,
    "x_raw30": 90112,
    "sig512_1": 90112,
    "x_raw01": 73728,
    "v_w1": 73728,
    "x_raw20": 61440,
    "sig256_0": 61440 - 5120,
    "sig0_1": 61440 + 3072,
}


def tile_list_kernl_sigm_res_bias_kernel(
    tc, x, tab_words, tab_scales, cw, cb, al4_words, al4_scales, al8_words, al8_scales, b, offs, out
):
    nc = tc.nc
    with ExitStack() as ctx:
        keep = ctx.enter_context(tc.tile_pool(name="keep", bufs=1))
        shared = ctx.enter_context(tc.tile_pool(name="shared", bufs=1))
        psum = ctx.enter_context(tc.psum_pool(name="psum", bufs=1))

        def tile(name, shape, dtype, tag=None):
            if name in PLACED:
                return shared.tile([P] + shape, dtype, name=name, align_bytes=64, offset=PLACED[name])
            return keep.tile([P] + shape, dtype, name=name, tag=tag or name, align_bytes=64)

        offsets = keep.tile([P, J // 16], U16, name="offsets")

        tab_sc = tile("tab_sc", [T // 4], I32)
        nc.sync.dma_start(tab_sc[96:128, :], tab_scales.bitcast(I32).rearrange("g r n -> r g n"))
        nc.sync.dma_start(offsets[:], offs)
        nc.vector.memset(tab_sc[0:96, :], 0)

        rows = tile("rows", [PASS], F32)
        nc.scalar.dma_start(rows[P - 4 : P - 2, :], cw.rearrange("(a j) -> a j", a=2))
        nc.scalar.dma_start(rows[P - 2 : P, :], cb.rearrange("(a j) -> a j", a=2))
        nc.vector.memset(rows[0 : P - 4, :], 0.0)

        warm_out = keep.tile([P, 1], F32, name="warm_out")
        nc.scalar.activation(warm_out[0:64, :], rows[0:64, 0:1], ACT.Sigmoid)

        zeros = tile("zeros", [PASS], BF16)
        nc.vector.memset(zeros[:], 0.0)
        zero_codes = tile("zero_codes", [P], U32)
        zero_scales = tile("zero_scales", [P], U8)
        nc.vector.quantize_mx(out=zero_codes[:].bitcast(FP8X4), scales=zero_scales[:], in_=zeros[:])

        identity = tile("identity", [P], F32)

        factors_sb = tile("factors_sb", [4 * PACK], F32)
        all_planes = tile("planes", [2, (J + 2 * N) // 4], I32)
        nc.gpsimd.memset(all_planes[:], 0)
        make_identity(nc, identity[:])
        planes = [all_planes[:, :, PASS // 4 * a : PASS // 4 * (a + 1)] for a in range(2)]
        al_planes = [all_planes[:, :, (J + N * tier) // 4 : (J + N * (tier + 1)) // 4] for tier in range(2)]


        banks = [psum.tile([P, WIDE], F32, name="bank%d" % i) for i in range(RING + 1)]
        cw_bank = banks[RING]
        factors_ps = cw_bank[:, P - 4 : P - 4 + 4 * PACK]
        taken = []

        def next_bank():
            taken.append(banks[ORDER[len(taken)]])
            return taken[-1]

        tab_w = tile("tab_w", [T], I32)
        x_raw = {}
        sigs = {}
        ahead = {}

        def load_x(s, g):
            x_raw[s, g] = tile("x_raw%d%d" % (s, g), [PACK, PIECE], F32)
            rows = x[PASS * g : PASS * (g + 1), PIECE * s : PIECE * (s + 1)]
            nc.sync.dma_start(x_raw[s, g][:], rows.rearrange("(p t) m -> p t m", t=PACK))

        picked_sc = tile("picked_sc", [J], U8)
        picked_w = {}
        v_w = [tile("v_w%d" % a, [2, PASS], U16) for a in range(2)]

        def pick_words(first, count):
            picked_w[first] = tile("picked_w%d" % first, [count], U32)
            entries = offsets[:, first // 16 : (first + count) // 16]
            nc.vector.tensor_copy(picked_w[first][:], tab_w[:].bitcast(U32).indirect(entries))

        def part_words(first, count):
            a, at = divmod(first, PASS)
            by_slot = v_w[a][:].rearrange("p g (t r) -> p g t r", t=PACK)[:, :, :, at // PACK : (at + count) // PACK]
            nc.vector.tensor_copy(
                by_slot.rearrange("p g t (b i) -> p g b t i", i=4),
                picked_w[first][:].bitcast(U16).rearrange("p (b i t g) -> p g b t i", t=PACK, g=2, i=4),
            )

        x_late = [tile("x_late%d" % g, [2, PACK * PIECE], BF16) for g in range(2)]
        x_first = {}

        def copy_x(s, g, copy):
            if s < 2:
                x_first[s, g] = tile("x_first%d%d" % (s, g), [PACK * PIECE], BF16)
            staged = x_first[s, g][:] if s < 2 else x_late[s - 2][:, g, :]
            copy(
                staged.rearrange("p (c i t) -> p c t i", i=RUN, t=PACK),
                x_raw[s, g][:].rearrange("p t (c i) -> p c t i", i=RUN),
            )

        x_codes = {(c, g): tile("x_codes%d%d" % (c, g), [WIDE], U32) for c in range(2) for g in range(2)}
        x_scales = {(c, g): tile("x_scales%d%d" % (c, g), [WIDE], U8) for c in range(2) for g in range(2)}

        def quant_x(s, g):
            cols = slice(PIECE * s, PIECE * (s + 1))
            nc.vector.quantize_mx(
                out=x_codes[0, g][:, cols].bitcast(FP8X4), scales=x_scales[0, g][:, cols], in_=x_first[s, g][:]
            )

        def copy_halves(s, g):
            halves = [tile("x_half%d%d_%d" % (s, g, i), [PACK * P], BF16) for i in range(2)]
            for i, staged in enumerate(halves):
                nc.vector.tensor_copy(
                    staged[:].rearrange("p (c i t) -> p c t i", i=RUN, t=PACK),
                    x_raw[s, g][:, :, P * i : P * (i + 1)].rearrange("p t (c i) -> p c t i", i=RUN),
                )
            return halves

        def quant_halves(halves, c, g, first):
            for i, staged in enumerate(halves):
                cols = slice(first + P * i, first + P * (i + 1))
                nc.vector.quantize_mx(out=x_codes[c, g][:, cols].bitcast(FP8X4), scales=x_scales[c, g][:, cols], in_=staged[:])

        def quant_late_x(g):
            staged = x_late[g][:].rearrange("p s c -> p (s c)")
            nc.vector.quantize_mx(out=x_codes[1, g][:].bitcast(FP8X4), scales=x_scales[1, g][:], in_=staged)

        def sigmoid(m0, a, t, sums):
            nc.scalar.activation(sigs[m0, a][:, t, :], sums, ACT.Sigmoid, bias=factors_sb[:, 4 * t + 2 + a : 4 * t + 3 + a])

        def first_stage(m0, w, a, tag=None, cuts=(), split=False):
            parts = list(zip((0,) + cuts, cuts + (w,)))
            for first, last in parts:
                name = "sig%d_%d" % (m0 + first, a)
                both = tile(name, [ROOM + PACK * (last - first)], F32, tag if first == 0 else None)
                sigs[m0 + first, a] = both[:, ROOM:].rearrange("p (t m) -> p t m", t=PACK)
                ahead[m0 + first, a] = both[:, 0 : PACK * PIECE // 2].bitcast(BF16)
            c, n0 = divmod(m0, WIDE)
            if m0 or a:
                pairs = [next_bank() for pair in range(2)]
                sums = [pairs[t // 2][:, PIECE * (t % 2) : PIECE * (t % 2 + 1)] for t in range(PACK)]
            else:
                sums = [next_bank() for t in range(PACK)]
            if c:
                codes = [x_codes[1, n0 // PIECE][:, PIECE * g : PIECE * (g + 1)] for g in range(2)]
                scales = [x_scales[1, n0 // PIECE][:, PIECE * g : PIECE * (g + 1)] for g in range(2)]
            else:
                codes = [x_codes[0, g][:, n0 : n0 + w] for g in range(2)]
                scales = [x_scales[0, g][:, n0 : n0 + w] for g in range(2)]

            def product(t, g, start, stop):
                nc.tensor.matmul_mx(
                    out=sums[t][:, 0:w],
                    lhsT=v_w[a][:, g, P * t : P * (t + 1)].bitcast(FP4X4),
                    lhsT_scale=planes[a][:, g, :].bitcast(U8)[:, P * t : P * (t + 1)],
                    rhs=codes[g].bitcast(FP8X4),
                    rhs_scale=scales[g],
                    start=start,
                    stop=stop,
                )

            if split:
                for t in range(PACK):
                    product(t, 1, t % 2 == 0, False)
            for t, bank in enumerate(sums):
                if split:
                    product(t, 0, False, t % 2 == 1)
                else:
                    product(t, 0, True, False)
                    product(t, 1, False, True)
                if not (m0 or a):
                    sigmoid(m0, a, t, bank[:, 0 : parts[0][1]])
                elif t % 2:
                    for u in (t - 1, t):
                        sigmoid(m0, a, u, sums[u][:, 0 : parts[0][1]])
            for first, last in parts[1:]:
                for t, bank in enumerate(sums):
                    sigmoid(m0 + first, a, t, bank[:, first:last])

        h_codes = [tile("h_codes%d" % c, [2 * PIECE], U32) for c in range(4)]
        h_scales = [tile("h_scales%d" % c, [2 * PIECE], U8) for c in range(4)]

        def spread_cw():
            for t in reversed(range(PACK)):
                nc.tensor.transpose(cw_bank[:, 4 * t : 4 * t + P], rows[:, t:PASS:PACK], identity[:])

        h_parts = {}

        def weigh(m0, w, a, side=SIDE, tag=None):
            cut = w - side
            h_parts[m0, a] = ahead[tag][:, PACK * (PIECE - w) :] if tag else tile("h%d_%d" % (m0, a), [PACK * w], BF16)[:]
            shares = [(nc.vector, factors_ps, 0, cut)]
            if side:
                shares.append((nc.gpsimd, factors_sb[:], cut, w))
            for engine, factors, first, last in shares:
                staged = h_parts[m0, a][:, PACK * first : PACK * last]
                runs = factors.rearrange("p (c t k) -> p c t k", c=1, t=PACK)[:, :, :, a : a + 1]
                engine.tensor_tensor(
                    staged.rearrange("p (c i t) -> p c t i", i=RUN, t=PACK),
                    sigs[m0, a][:, :, first:last].rearrange("p t (c i) -> p c t i", i=RUN),
                    runs.to_broadcast([P, (last - first) // RUN, PACK, RUN]),
                    ALU.mult,
                )

        def quant_h(m0, a, calls=1):
            c, n0 = divmod(m0, PIECE)
            staged = h_parts[m0, a]
            each = staged.shape[1] // PACK // calls
            for first in range(0, each * calls, each):
                cols = slice(PIECE * a + n0 + first, PIECE * a + n0 + first + each)
                nc.vector.quantize_mx(
                    out=h_codes[c][:, cols].bitcast(FP8X4),
                    scales=h_scales[c][:, cols],
                    in_=staged[:, PACK * first : PACK * (first + each)],
                )

        b_t = keep.tile([P, 2], F32, name="b_t")
        al4_w = tile("al4_w", [2, N // 2], I32)
        al8_w = tile("al8_w", [2, N], I32)

        def second_passes(m0, w, a, half, dst, opens, closes):
            c, n0 = divmod(m0, PIECE)
            at = PIECE * a + n0
            al4 = al4_w[:, a, P // 2 * half : P // 2 * (half + 1)].bitcast(FP4X4)
            al8 = al8_w[:, a, P * half : P * (half + 1)].bitcast(FP8X4)
            step = w
            passes = [(1, al8, 0, w)] + [(0, al4, k, step) for k in range(0, w, step)]
            for i, (tier, lhsT, k, n) in enumerate(passes):
                nc.tensor.matmul_mx(
                    out=dst[:, k : k + n],
                    lhsT=lhsT,
                    lhsT_scale=al_planes[tier][:, a, :].bitcast(U8)[:, P * half : P * (half + 1)],
                    rhs=h_codes[c][:, at + k : at + k + n].bitcast(FP8X4),
                    rhs_scale=h_scales[c][:, at + k : at + k + n],
                    start=(opens and i == 0),
                    stop=(closes and i == len(passes) - 1),
                )

        def bias_on_scalar(dst, sums, half):
            nc.scalar.activation(dst, sums, ACT.Identity, bias=b_t[:, half : half + 1])

        def bias_on_vector(dst, sums, half):
            nc.vector.tensor_scalar(dst, sums, b_t[:, half : half + 1], None, ALU.add)

        out_v = out.rearrange("(h p) m -> p h m", p=P)

        def store(m0, w, sums, adders):
            res = tile("res%d" % m0, [2, w], F32)
            for half in range(2):
                adders[half](res[:, half, :], sums[half], half)
            nc.sync.dma_start(out_v[:, :, m0 : m0 + w], res[:])

        def move_scales(a):
            for q in PORT_ORDER:
                rows = picked_sc[96 + 8 * q : 96 + 8 * (q + 1), PASS * a : PASS * (a + 1)].bitcast(I32)
                nc.sync.dma_start(planes[a][32 * q : 32 * q + 4, :, :], rows)

        nc.sync.dma_start(tab_w[:], tab_words[0].rearrange("p t b -> p (t b)").bitcast(I32))
        load_x(0, 0)
        load_x(0, 1)

        scalar, vector = nc.scalar.copy, nc.vector.tensor_copy
        spread_cw()
        for a in range(2):
            cols = slice(PASS * a, PASS * (a + 1))
            nc.vector.tensor_copy(
                picked_sc[:, cols].rearrange("p (t r) -> p r t", t=PACK),
                tab_sc[:].bitcast(U8).indirect(offsets[:, 32 * a : 32 * (a + 1)]),
            )

        load_x(1, 0)
        move_scales(0)
        load_x(1, 1)
        load_x(2, 0)
        load_x(2, 1)
        move_scales(1)
        load_x(3, 1)
        load_x(3, 0)
        nc.sync.dma_start(al8_w[:], al8_words.rearrange("a p n i -> a p (n i)").bitcast(I32).rearrange("a p n -> p a n"))
        nc.sync.dma_start(al4_w[:], al4_words.bitcast(I32).rearrange("a p n -> p a n"))
        for tier, src in enumerate((al4_scales, al8_scales)):
            for q in PORT_ORDER:
                rows = src.bitcast(I32)[:, 4 * q : 4 * (q + 1), :].rearrange("a r n -> r a n")
                nc.sync.dma_start(al_planes[tier][32 * q : 32 * q + 4, :, :], rows)
        with nc.allow_non_contiguous_dma(reason="one bias value a partition"):
            nc.sync.dma_start(b_t[:], b.rearrange("(h p) -> p h", p=P))

        pick_words(0, PASS)
        pick_words(PASS, PASS)
        for i in range(WARM):
            nc.tensor.matmul_mx(
                out=cw_bank[:, PIECE : 2 * PIECE],
                lhsT=zero_codes[:].bitcast(FP8X4),
                lhsT_scale=zero_scales[:],
                rhs=picked_w[0][:].bitcast(U16)[:, 0:PIECE].bitcast(FP4X4),
                rhs_scale=picked_sc[:, 0:PIECE],
                start=True,
                stop=True,
            )
        part_words(0, PASS)
        for g in range(2):
            copy_x(0, g, scalar)
            quant_x(0, g)
        part_words(PASS, PASS)
        copy_x(1, 0, scalar)
        nc.scalar.copy(factors_sb[:], factors_ps)

        first_stage(0, PIECE, 0, "x_raw10")
        halves = copy_halves(1, 1)
        quant_x(1, 0)
        quant_halves(halves, 0, 1, PIECE)
        weigh(0, PIECE, 0)
        copy_x(2, 0, scalar)
        first_stage(PIECE, PIECE, 0)
        copy_x(2, 1, vector)
        quant_h(0, 0)
        weigh(PIECE, PIECE, 0)
        quant_late_x(0)

        first_stage(0, PIECE, 1)
        copy_x(3, 1, scalar)
        first_stage(PIECE, PIECE, 1)
        steps = [(0, 1), (PIECE, 1), (WIDE, 0), (WIDE, 1), (WIDE + PIECE, 0)]
        weigh(0, PIECE, 1, tag=(PIECE, 0))
        quant_h(PIECE, 0)
        nc.vector.quantize_mx(
            out=x_codes[1, 1][:, PIECE:WIDE].bitcast(FP8X4), scales=x_scales[1, 1][:, PIECE:WIDE], in_=x_late[1][:, 1, :]
        )
        quant_halves(copy_halves(3, 0), 1, 1, 0)
        for m0, a in steps[2:]:
            first_stage(m0, PIECE, a, split=(m0 == WIDE + PIECE))
        first_stage(WIDE + PIECE, PIECE, 1, cuts=(P,))
        for before, (m0, a) in zip(steps, steps[1:]):
            weigh(m0, PIECE, a, tag=before if m0 >= WIDE else None)
            quant_h(*before)

        for half in range(2):
            sums = next_bank()[:]
            for m0 in (0, PIECE):
                for a in range(2):
                    second_passes(m0, PIECE, a, half, sums[:, m0 : m0 + PIECE], a == 0, a == 1)
            res = tile("res_first%d" % half, [WIDE], F32)
            bias_on_scalar(res[:], sums, half)
            nc.sync.dma_start(out[P * half : P * (half + 1), 0:WIDE], res[:])

        ends = [WIDE + PIECE, WIDE + PIECE + P]
        weigh(ends[0], P, 1, side=SIDE // 2, tag=steps[-1])
        quant_h(*steps[-1])
        quant_h(ends[0], 1)
        planes_h = tile("planes_h", [PACK, P], BF16)
        for t in range(PACK):
            nc.scalar.activation(
                planes_h[:, t, :], sigs[ends[1], 1][:, t, :], ACT.Copy, scale=factors_sb[:, 4 * t + 1 : 4 * t + 2]
            )
        h_parts[ends[1], 1] = tile("h_last", [PACK * P], BF16)[:]
        for first in (0, P // 2):
            nc.vector.tensor_copy(
                h_parts[ends[1], 1][:, PACK * first : PACK * (first + P // 2)].rearrange("p (c i t) -> p c t i", i=RUN, t=PACK),
                planes_h[:, :, first : first + P // 2].rearrange("p t (c i) -> p c t i", i=RUN),
            )
        quant_h(ends[1], 1, calls=2)

        bank = next_bank()
        third_sums = [bank[:, PIECE * half : PIECE * (half + 1)] for half in range(2)]
        end_sums = [[next_bank()[:, 0:P] for half in range(2)] for end in ends]
        for half in range(2):
            for a in range(2):
                second_passes(WIDE, PIECE, a, half, third_sums[half], a == 0, a == 1)
        store(WIDE, PIECE, third_sums, (bias_on_scalar, bias_on_scalar))
        for half in range(2):
            second_passes(ends[0], P, 0, half, end_sums[0][half], True, False)
        for half in range(2):
            second_passes(ends[1], P, 0, half, end_sums[1][half], True, False)
        for half in range(2):
            second_passes(ends[0], P, 1, half, end_sums[0][half], False, True)
        store(ends[0], P, end_sums[0], (bias_on_vector, bias_on_vector))
        for half in range(2):
            second_passes(ends[1], P, 1, half, end_sums[1][half], False, True)
        store(ends[1], P, end_sums[1], (bias_on_scalar, bias_on_vector))
